import numpy as np
import ml_dtypes


def mxq(x, axis, fmt="e4m3"):
    dtype, down = {"e4m3": (ml_dtypes.float8_e4m3fn, 7), "e5m2": (ml_dtypes.float8_e5m2, 14)}[fmt]
    v = np.moveaxis(np.asarray(x, np.float32).astype(ml_dtypes.bfloat16).astype(np.float64), axis, -1)
    blocks = v.reshape(v.shape[:-1] + (-1, 32))
    amax = np.abs(blocks).max(-1, keepdims=True)
    byte = np.maximum(np.where(amax > 0, np.frexp(amax)[1] - 1 + 127, 0) - down, 1)
    scale = np.exp2(byte - 127.0)
    codes = (blocks / scale).astype(np.float32).astype(dtype).astype(np.float64)
    return np.moveaxis((codes * scale).reshape(v.shape), -1, axis)


WIDE = False


def mx_kscale(k):
    if not WIDE:
        return np.ones(k)
    levels = np.array([10, -10, 5, -5, 0])
    if k % 512:
        return np.exp2(np.random.permutation(np.resize(levels, k // 32))).repeat(32)
    a = np.empty((k // 512, 16))
    for p in range(k // 512):
        a[p, :8] = np.random.permutation(np.resize(levels, 8))
        for g in range(8):
            far = levels[np.abs(levels - a[p, g]) >= 10]
            a[p, g + 8] = far[np.random.randint(len(far))]
    return np.exp2(a.ravel()).repeat(32)


def f64(x):
    return np.asarray(x).astype(np.float64)


def striped(idx):
    return np.tile(idx.reshape(-1, 16).T, (8, 1)).astype(np.uint16)


def unstriped(offs):
    return offs[:16].T.reshape(-1).astype(np.int64)


E2M1 = np.array([0.0, 0.5, 1.0, 1.5, 2.0, 3.0, 4.0, 6.0, -0.0, -0.5, -1.0, -1.5, -2.0, -3.0, -4.0, -6.0])


def pack_weight(w, fmt):
    k, n = w.shape
    w = f64(np.asarray(w, np.float32).astype(ml_dtypes.bfloat16)).reshape(k // 32, 32, n)
    amax = np.abs(w).max(1)
    if fmt == "e4m3":
        byte = np.frexp(amax)[1] - 1 + 127 - 7
    else:
        mant, ex = np.frexp(amax / 6.0)
        byte = np.where(mant > 0.5, ex, ex - 1) + 127
    byte = np.clip(np.where(amax > 0, byte, 1), 1, 254)
    scaled = (w * np.exp2(127.0 - byte)[:, None, :]).reshape(k, n).astype(np.float32)
    by_word = np.ascontiguousarray(scaled.reshape(k // 512, 128, 4, n).transpose(0, 1, 3, 2))
    if fmt == "e4m3":
        words = by_word.astype(ml_dtypes.float8_e4m3fn).view(np.uint8)
    else:
        c = by_word.astype(ml_dtypes.float4_e2m1fn).view(np.uint8) & 0xF
        words = (c[..., 0::2] | (c[..., 1::2] << 4)).reshape(k // 512, 128, 2 * n)
    return np.ascontiguousarray(words), np.ascontiguousarray(byte.astype(np.uint8).reshape(k // 512, 16, n))


def unpack_weight(words, scales, fmt):
    g, _, n = scales.shape
    words = np.ascontiguousarray(words).reshape(g, 128, n, -1)
    if fmt == "e4m3":
        vals = words.view(ml_dtypes.float8_e4m3fn).astype(np.float64)
    else:
        nib = np.empty((g, 128, n, 4), np.uint8)
        nib[..., 0::2] = words & 0xF
        nib[..., 1::2] = words >> 4
        vals = E2M1[nib]
    vals = vals * np.repeat(np.exp2(scales.astype(np.float64) - 127.0), 8, axis=1)[..., None]
    return vals.transpose(0, 1, 3, 2).reshape(g * 512, n)


def gelu(v):
    return 0.5 * v * (1.0 + np.tanh(np.sqrt(2.0 / np.pi) * (v + 0.044715 * v**3)))


def often(T, S):
    return np.random.permutation(T)[(T * np.random.uniform(0, 1, S) ** 4).astype(np.int64)]


K, T, S, K2, T2, P, H, N = 1024, 4096, 1024, 1536, 2048, 512, 1024, 512

def setup_inputs():
    n = np.random.standard_normal
    s = mx_kscale(K)[:, None]
    s2 = mx_kscale(K2)[:, None]
    u = mx_kscale(H)[:, None]
    tab_words, tab_scales = pack_weight(n((K, T)) * s, "e4m3")
    tab2_words, tab2_scales = pack_weight(n((K2, T2)) * s2, "e4m3")
    w2_words, w2_scales = pack_weight(n((K2, H)) / np.sqrt(K2) / s2, "e2m1")
    w3_words, w3_scales = pack_weight(n((H, N)) / np.sqrt(H) / u, "e4m3")
    return {
        "tab_words": tab_words, "tab_scales": tab_scales,
        "tab2_words": tab2_words, "tab2_scales": tab2_scales,
        "w1": (n((K, H)) / np.sqrt(K) / s).astype(np.float32),
        "w2_words": w2_words, "w2_scales": w2_scales,
        "w3_words": w3_words, "w3_scales": w3_scales,
        "gain": (np.exp(0.4 * n(H)) * u[:, 0]).astype(np.float32),
        "offs": striped(np.random.permutation(T)[:S]),
        "pos1": striped(often(S, P)),
        "offs2": striped(np.random.permutation(T2)[:P]),
    }

def reference(tab_words, tab_scales, tab2_words, tab2_scales, w1, w2_words, w2_scales,
              w3_words, w3_scales, gain, offs, pos1, offs2):
    v = unpack_weight(tab_words, tab_scales, "e4m3")[:, unstriped(offs)]
    v2 = unpack_weight(tab2_words, tab2_scales, "e4m3")[:, unstriped(offs2)]
    h = mxq(f64(w1), 0, "e4m3").T @ v
    a = h[:, unstriped(pos1)]
    b = unpack_weight(w2_words, w2_scales, "e2m1").T @ v2
    z = np.log((0.5 + np.square(b)) / (0.5 + np.square(a))) * f64(gain)[:, None]
    y = unpack_weight(w3_words, w3_scales, "e4m3").T @ mxq(z, 0, "e4m3")
    return 1.0 / (1.0 + np.exp(-y))

@@ -1,0 +1,274 @@
+import itertools
+from contextlib import ExitStack
+
+import concourse.mybir as mybir
+from concourse.masks import make_identity
+
+K, T, S, K2, T2, M, H, N = 1024, 4096, 1024, 1536, 2048, 512, 1024, 512
+FLOPS = 2 * (K * H * S + K2 * H * M + H * N * M)
+
+F32 = mybir.dt.float32
+BF16 = mybir.dt.bfloat16
+I32 = mybir.dt.int32
+U32 = mybir.dt.uint32
+U16 = mybir.dt.uint16
+U8 = mybir.dt.uint8
+FP8X4 = mybir.dt.float8_e4m3fn_x4
+FP4X4 = mybir.dt.float4_e2m1fn_x4
+ACT = mybir.ActivationFunctionType
+ALU = mybir.AluOpType
+
+P = 128
+PACK = 4
+PASS = P * PACK
+BANK = 512
+QUADS = 4
+A1, A2, B = K // PASS, K2 // PASS, H // PASS
+LIST = 16
+
+
+def words_of(packed):
+    return packed.rearrange("p n i -> p (n i)").bitcast(I32)
+
+
+def tile_list_ransomware_alarm_levels_kernel(
+    tc, tab_words, tab_scales, tab2_words, tab2_scales, w1, w2_words, w2_scales,
+    w3_words, w3_scales, gain, offs, pos1, offs2, out,
+):
+    nc = tc.nc
+    with ExitStack() as ctx:
+        keep = ctx.enter_context(tc.tile_pool(name="keep", bufs=1))
+        ring = ctx.enter_context(tc.tile_pool(name="ring", bufs=2))
+        psum = ctx.enter_context(tc.psum_pool(name="psum", bufs=1))
+
+        def kept(shape, dtype, name, pool=keep):
+            return pool.tile(shape, dtype, name=name, tag=name, align_bytes=64)
+
+        offs_sb = keep.tile([P, S // LIST], U16, name="offs_sb")
+        pos_sb = keep.tile([P, M // LIST], U16, name="pos_sb")
+        offs2_sb = keep.tile([P, M // LIST], U16, name="offs2_sb")
+
+        with tc.tile_pool(name="head", bufs=1) as head:
+            tab_sc = kept([P, T], U8, "tab_sc", head)
+            tab2_sc = kept([P, T2], U8, "tab2_sc", head)
+            v_planes = kept([P, A1 * S], U8, "v_planes")
+            v2_planes = kept([P, A2 * M], U8, "v2_planes")
+            nc.vector.memset(tab_sc[:].bitcast(I32)[:, :T // 8], 0)
+            nc.gpsimd.memset(tab_sc[:].bitcast(I32)[:, T // 8:], 0)
+            for zeroed in (tab2_sc, v_planes, v2_planes):
+                nc.vector.memset(zeroed[:].bitcast(I32), 0)
+            half = keep.tile([P, 1], F32, name="half", tag="half")
+            nc.vector.memset(half[:], 0.5)
+            warm = kept([P, 1], F32, "warm")
+            nc.scalar.activation(out=warm[:], in_=half[:], func=ACT.Ln)
+
+            def load_w1(b, a, pool):
+                raw = kept([P, PACK, PASS], F32, "w1_raw%d" % a, pool)
+                rows = w1[a * PASS:(a + 1) * PASS, b * PASS:(b + 1) * PASS]
+                nc.sync.dma_start(out=raw[:], in_=rows.rearrange("(p j) c -> p j c", j=PACK))
+                return raw
+
+            def load_words(src, width, name):
+                dst = kept([P, width], I32, name, late)
+                nc.sync.dma_start(out=dst[:], in_=src)
+                return dst
+
+            def load_planes(planes, scales, passes):
+                view = planes[:].bitcast(I32).rearrange("p (a c) -> p a c", a=passes)
+                for q in range(QUADS):
+                    nc.sync.dma_start(
+                        out=view[32 * q:32 * q + 4],
+                        in_=scales[:, 4 * q:4 * q + 4, :].bitcast(I32).rearrange("a r c -> r a c"),
+                    )
+
+            w1_raw = {}
+            w1_raw[0, 0] = load_w1(0, 0, head)
+            nc.sync.dma_start(offs_sb[:], offs)
+            nc.sync.dma_start(
+                out=tab_sc[:].bitcast(I32)[0:P:4],
+                in_=tab_scales.bitcast(I32).rearrange("a q c -> q a c"),
+            )
+            w1_raw[0, 1] = load_w1(0, 1, head)
+            nc.sync.dma_start(offs2_sb[:], offs2)
+            nc.sync.dma_start(
+                out=tab2_sc[:].bitcast(I32)[0:96:2],
+                in_=tab2_scales.bitcast(I32).rearrange("a q c -> q a c"),
+            )
+            nc.sync.dma_start(pos_sb[:], pos1)
+            gain_sb = kept([P, B, PACK], F32, "gain_sb")
+            nc.sync.dma_start(out=gain_sb[:], in_=gain.rearrange("(b p t) -> p b t", b=B, t=PACK))
+            tab_sb = [kept([P, T], I32, "tab%d" % a) for a in range(A1)]
+            for a in range(A1):
+                for c0 in range(0, T, T // 2):
+                    nc.sync.dma_start(out=tab_sb[a][:, c0:c0 + T // 2], in_=words_of(tab_words[a])[:, c0:c0 + T // 2])
+
+            ident = kept([P, P], F32, "ident")
+            make_identity(nc, ident[:])
+
+            v_sc = kept([P, S], U8, "v_sc")
+            nc.vector.tensor_copy(v_sc[:], tab_sc[:].indirect(offs_sb[:]))
+            v2_sc = kept([P, M], U8, "v2_sc")
+            nc.vector.tensor_copy(v2_sc[:], tab2_sc[:].indirect(offs2_sb[:]))
+            for q in range(QUADS):
+                nc.gpsimd.dma_start(
+                    out=v2_planes[:].bitcast(I32).rearrange("p (a c) -> p a c", a=A2)[32 * q:32 * q + 4],
+                    in_=v2_sc[:].bitcast(I32)[24 * q:24 * q + 24:2],
+                )
+
+            w1_codes, w1_planes = {}, {}
+
+            def round_w1(b, a, copy):
+                grouped = ring.tile([P, PACK * PASS], BF16, name="w1_bf", tag="w1_bf", align_bytes=64)
+                copy(
+                    grouped[:].rearrange("p (t m j) -> p m j t", t=PACK, j=PACK),
+                    w1_raw[b, a][:].rearrange("p j (m t) -> p m j t", t=PACK),
+                )
+                return grouped
+
+            def quantise_w1(b, a, grouped):
+                w1_codes[b, a] = kept([P, PASS], U32, "w1c%d%d" % (b, a))
+                w1_planes[b, a] = kept([P, PASS], U8, "w1s%d%d" % (b, a))
+                nc.vector.quantize_mx(out=w1_codes[b, a][:].bitcast(FP8X4), scales=w1_planes[b, a][:], in_=grouped[:])
+
+            for a in range(A1):
+                quantise_w1(0, a, round_w1(0, a, nc.scalar.copy))
+            for q in range(QUADS):
+                nc.sync.dma_start(
+                    out=v_planes[:].bitcast(I32).rearrange("p (a c) -> p a c", a=A1)[32 * q:32 * q + 4],
+                    in_=v_sc[:].bitcast(I32)[32 * q:32 * q + 32:4],
+                )
+
+        late = ctx.enter_context(tc.tile_pool(name="late", bufs=1))
+
+        halves = S // BANK
+        v_codes = {}
+        for a in range(A1):
+            for u in range(halves):
+                v_codes[a, u] = kept([P, BANK], U32, "v%d%d" % (a, u))
+                cols = slice(u * BANK // LIST, (u + 1) * BANK // LIST)
+                nc.vector.tensor_copy(v_codes[a, u][:], tab_sb[a][:].bitcast(U32).indirect(offs_sb[:, cols]))
+
+        for a in range(A1):
+            w1_raw[1, a] = load_w1(1, a, late)
+        w2_planes = kept([P, A2 * H], U8, "w2_planes", late)
+        w3_planes = kept([P, B * N], U8, "w3_planes", late)
+        for zeroed in (w2_planes, w3_planes):
+            nc.vector.memset(zeroed[:].bitcast(I32), 0)
+        tab2_sb, w2_sb = [], []
+        load_planes(w2_planes, w2_scales, A2)
+        for a in range(A2):
+            w2_sb.append(load_words(w2_words[a].bitcast(I32), H // 2, "w2_%d" % a))
+            tab2_sb.append(load_words(words_of(tab2_words[a]), T2, "tab2_%d" % a))
+        load_planes(w3_planes, w3_scales, B)
+        w3_sb = [load_words(words_of(w3_words[b]), N, "w3_%d" % b) for b in range(B)]
+
+        log_a = {}
+
+        def first_stage(b, copies):
+            h = [ring.tile([P, S], F32, name="h", tag="h", bufs=6) for t in range(PACK)]
+            for t0 in range(0, PACK, 2):
+                for u, t in itertools.product(range(halves), (t0, t0 + 1)):
+                    acc = psum.tile([P, BANK], F32, name="acc", tag="acc", bufs=4)
+                    for a in range(A1):
+                        nc.tensor.matmul_mx(
+                            out=acc[:],
+                            lhsT=w1_codes[b, a][:, t * P:(t + 1) * P].bitcast(FP8X4),
+                            lhsT_scale=w1_planes[b, a][:, t * P:(t + 1) * P],
+                            rhs=v_codes[a, u][:].bitcast(FP8X4),
+                            rhs_scale=v_planes[:, a * S + u * BANK:a * S + (u + 1) * BANK],
+                            start=(a == 0), stop=(a == A1 - 1),
+                        )
+                    copies[t % 2](h[t][:, u * BANK:(u + 1) * BANK], acc[:])
+            return h
+
+        def pick(b, h, tag, square_tag):
+            log_a[b] = kept([P, PACK, M], F32, "log_a%d" % b)
+            picked = late.tile([P, PACK, M], F32, name="picked", tag=tag, align_bytes=64)
+            square_a = kept([P, PACK, M], F32, square_tag)
+            for t in range(PACK):
+                nc.vector.tensor_copy(picked[:, t, :], h[t][:].indirect(pos_sb[:]))
+                nc.scalar.activation(out=square_a[:, t, :], in_=picked[:, t, :], func=ACT.Square)
+                nc.scalar.activation(out=log_a[b][:, t, :], in_=square_a[:, t, :], func=ACT.Ln, bias=half[:])
+
+        z_codes, z_planes = {}, {}
+
+        def project_files(b):
+            log_b = kept([P, PACK, M], F32, "log_b%d" % b)
+            square_bt = kept([P, M // P, PACK, P], F32, "square_bt%d" % b)
+            for i in range(M // P):
+                files = slice(i * P, (i + 1) * P)
+                bt = psum.tile([P, BANK], F32, name="bt", tag="bt", bufs=2)
+                for a in range(A2):
+                    nc.tensor.matmul_mx(
+                        out=bt[:],
+                        lhsT=v2_codes[a][:, files].bitcast(FP8X4),
+                        lhsT_scale=v2_planes[:, a * M + i * P:a * M + (i + 1) * P],
+                        rhs=w2_sb[a][:].bitcast(U8)[:, 2 * b * PASS:2 * (b + 1) * PASS].bitcast(FP4X4),
+                        rhs_scale=w2_planes[:, a * H + b * PASS:a * H + (b + 1) * PASS],
+                        start=(a == 0), stop=(a == A2 - 1),
+                    )
+                nc.scalar.activation(
+                    out=square_bt[:, i], in_=bt[:].rearrange("m (p t) -> m t p", t=PACK), func=ACT.Square
+                )
+                square_b = psum.tile([P, PACK, P], F32, name="square_b", tag="square_b", bufs=2)
+                for t in range(PACK):
+                    nc.tensor.transpose(square_b[:, t, :], square_bt[:, i, t, :], ident[:])
+                nc.scalar.activation(out=log_b[:, :, files], in_=square_b[:], func=ACT.Ln, bias=half[:])
+            return log_b
+
+        def make_z(b, log_b, width):
+            chunks = M // width
+            z = {}
+            for step in range(chunks + 2):
+                if step < chunks:
+                    files = slice(step * width, (step + 1) * width)
+                    diff = log_b[:, :, files]
+                    nc.vector.tensor_tensor(diff, diff, log_a[b][:, :, files], ALU.subtract)
+                if 1 <= step <= chunks:
+                    c = step - 1
+                    z[c] = ring.tile([P, PACK * width], BF16, name="z", tag="z", align_bytes=64, bufs=3)
+                    nc.vector.tensor_tensor(
+                        z[c][:].rearrange("p (c e t) -> p c t e", e=4, t=PACK),
+                        log_b[:, :, c * width:(c + 1) * width].rearrange("p t (c e) -> p c t e", e=4),
+                        gain_sb[:, b, :].unsqueeze(1).unsqueeze(3).to_broadcast([P, width // 4, PACK, 4]),
+                        ALU.mult,
+                    )
+                if step >= 2:
+                    c = step - 2
+                    codes = kept([P, width], U32, "zc%d_%d" % (b, c))
+                    planes = kept([P, width], U8, "zs%d_%d" % (b, c))
+                    nc.vector.quantize_mx(out=codes[:].bitcast(FP8X4), scales=planes[:], in_=z[c][:])
+                    for c0 in range(0, width, P):
+                        z_codes[b, (c * width + c0) // P] = codes[:, c0:c0 + P]
+                        z_planes[b, (c * width + c0) // P] = planes[:, c0:c0 + P]
+
+        h0 = first_stage(0, (nc.scalar.copy, nc.scalar.copy))
+        for a in range(A1):
+            quantise_w1(1, a, round_w1(1, a, nc.vector.tensor_copy))
+        pick(0, h0, "picked0", "square_bt1")
+        v2_codes = []
+        for a in range(A2):
+            v2_codes.append(kept([P, M], U32, "v2_%d" % a))
+            nc.vector.tensor_copy(v2_codes[a][:], tab2_sb[a][:].bitcast(U32).indirect(offs2_sb[:]))
+        h1 = first_stage(1, (nc.scalar.copy, nc.scalar.copy))
+        log_b0 = project_files(0)
+        pick(1, h1, "tab2_%d" % (A2 - 1), "square_bt0")
+        make_z(0, log_b0, 2 * P)
+        make_z(1, project_files(1), P)
+
+        out_view = out.rearrange("(g p) m -> p g m", p=P)
+        levels = keep.tile([P, M // P, N // P, P], F32, name="levels", tag="half")
+        for i in range(M // P):
+            y = psum.tile([P, N // P, P], F32, name="acc", tag="acc", bufs=4)
+            for g in range(N // P):
+                for b in range(B):
+                    nc.tensor.matmul_mx(
+                        out=y[:, g, :],
+                        lhsT=w3_sb[b][:, g * P:(g + 1) * P].bitcast(FP8X4),
+                        lhsT_scale=w3_planes[:, b * N + g * P:b * N + (g + 1) * P],
+                        rhs=z_codes[b, i].bitcast(FP8X4),
+                        rhs_scale=z_planes[b, i],
+                        start=(b == 0), stop=(b == B - 1),
+                    )
+            nc.scalar.activation(out=levels[:, i], in_=y[:], func=ACT.Sigmoid)
+            nc.sync.dma_start(out=out_view[:, :, i * P:(i + 1) * P], in_=levels[:, i])

@@ -25,6 +25,8 @@ BANK = 512
 QUADS = 4
 A1, A2, B = K // PASS, K2 // PASS, H // PASS
 LIST = 16
+NV = 3
+NACC, NBT, NSQ, W0, TAG1, SQT = 4, 4, 4, 256, "tab2_2", "acc"
 
 
 def words_of(packed):
@@ -53,12 +55,13 @@ def tile_list_ransomware_alarm_levels_kernel(
             tab2_sc = kept([P, T2], U8, "tab2_sc", head)
             v_planes = kept([P, A1 * S], U8, "v_planes")
             v2_planes = kept([P, A2 * M], U8, "v2_planes")
-            nc.vector.memset(tab_sc[:].bitcast(I32)[:, :T // 8], 0)
-            nc.gpsimd.memset(tab_sc[:].bitcast(I32)[:, T // 8:], 0)
-            for zeroed in (tab2_sc, v_planes, v2_planes):
-                nc.vector.memset(zeroed[:].bitcast(I32), 0)
             half = keep.tile([P, 1], F32, name="half", tag="half")
             nc.vector.memset(half[:], 0.5)
+            row0, row0_2 = P - 16 * A1, P - 16 * A2
+            nc.vector.memset(tab_sc[:].bitcast(I32)[:row0], 0)
+            nc.vector.memset(tab2_sc[:].bitcast(I32)[:row0_2], 0)
+            for zeroed in (v_planes, v2_planes):
+                nc.vector.memset(zeroed[:].bitcast(I32), 0)
             warm = kept([P, 1], F32, "warm")
             nc.scalar.activation(out=warm[:], in_=half[:], func=ACT.Ln)
 
@@ -82,18 +85,18 @@ def tile_list_ransomware_alarm_levels_kernel(
                     )
 
             w1_raw = {}
-            w1_raw[0, 0] = load_w1(0, 0, head)
-            nc.sync.dma_start(offs_sb[:], offs)
             nc.sync.dma_start(
-                out=tab_sc[:].bitcast(I32)[0:P:4],
+                out=tab_sc[:].bitcast(I32)[row0:],
                 in_=tab_scales.bitcast(I32).rearrange("a q c -> q a c"),
             )
-            w1_raw[0, 1] = load_w1(0, 1, head)
-            nc.sync.dma_start(offs2_sb[:], offs2)
-            nc.sync.dma_start(
-                out=tab2_sc[:].bitcast(I32)[0:96:2],
+            nc.sync.dma_start(offs_sb[:], offs)
+            w1_raw[0, 0] = load_w1(0, 0, head)
+            nc.scalar.dma_start(
+                out=tab2_sc[:].bitcast(I32)[row0_2:],
                 in_=tab2_scales.bitcast(I32).rearrange("a q c -> q a c"),
             )
+            nc.sync.dma_start(offs2_sb[:], offs2)
+            w1_raw[0, 1] = load_w1(0, 1, head)
             nc.sync.dma_start(pos_sb[:], pos1)
             gain_sb = kept([P, B, PACK], F32, "gain_sb")
             nc.sync.dma_start(out=gain_sb[:], in_=gain.rearrange("(b p t) -> p b t", b=B, t=PACK))
@@ -112,16 +115,16 @@ def tile_list_ransomware_alarm_levels_kernel(
             for q in range(QUADS):
                 nc.gpsimd.dma_start(
                     out=v2_planes[:].bitcast(I32).rearrange("p (a c) -> p a c", a=A2)[32 * q:32 * q + 4],
-                    in_=v2_sc[:].bitcast(I32)[24 * q:24 * q + 24:2],
+                    in_=v2_sc[:].bitcast(I32)[row0_2 + 4 * A2 * q:row0_2 + 4 * A2 * (q + 1)],
                 )
 
             w1_codes, w1_planes = {}, {}
 
-            def round_w1(b, a, copy):
-                grouped = ring.tile([P, PACK * PASS], BF16, name="w1_bf", tag="w1_bf", align_bytes=64)
+            def round_w1(b, a, copy, pool):
+                grouped = kept([P, PACK * PASS], BF16, "w1_bf%d" % a, pool)
                 copy(
-                    grouped[:].rearrange("p (t m j) -> p m j t", t=PACK, j=PACK),
-                    w1_raw[b, a][:].rearrange("p j (m t) -> p m j t", t=PACK),
+                    grouped[:].rearrange("p (u v m j) -> p u m j v", u=2, v=2, j=PACK),
+                    w1_raw[b, a][:].rearrange("p j (m u v) -> p u m j v", u=2, v=2),
                 )
                 return grouped
 
@@ -131,11 +134,11 @@ def tile_list_ransomware_alarm_levels_kernel(
                 nc.vector.quantize_mx(out=w1_codes[b, a][:].bitcast(FP8X4), scales=w1_planes[b, a][:], in_=grouped[:])
 
             for a in range(A1):
-                quantise_w1(0, a, round_w1(0, a, nc.scalar.copy))
+                quantise_w1(0, a, round_w1(0, a, (nc.scalar.copy, nc.vector.tensor_copy)[a], head))
             for q in range(QUADS):
-                nc.sync.dma_start(
+                nc.scalar.dma_start(
                     out=v_planes[:].bitcast(I32).rearrange("p (a c) -> p a c", a=A1)[32 * q:32 * q + 4],
-                    in_=v_sc[:].bitcast(I32)[32 * q:32 * q + 32:4],
+                    in_=v_sc[:].bitcast(I32)[row0 + 4 * A1 * q:row0 + 4 * A1 * (q + 1)],
                 )
 
         late = ctx.enter_context(tc.tile_pool(name="late", bufs=1))
@@ -165,10 +168,10 @@ def tile_list_ransomware_alarm_levels_kernel(
         log_a = {}
 
         def first_stage(b, copies):
-            h = [ring.tile([P, S], F32, name="h", tag="h", bufs=6) for t in range(PACK)]
+            h = [ring.tile([P, S], F32, name="h", tag="h", bufs=8) for t in range(PACK)]
             for t0 in range(0, PACK, 2):
                 for u, t in itertools.product(range(halves), (t0, t0 + 1)):
-                    acc = psum.tile([P, BANK], F32, name="acc", tag="acc", bufs=4)
+                    acc = psum.tile([P, BANK], F32, name="acc", tag="low%d" % (2 * u + t % 2))
                     for a in range(A1):
                         nc.tensor.matmul_mx(
                             out=acc[:],
@@ -181,23 +184,25 @@ def tile_list_ransomware_alarm_levels_kernel(
                     copies[t % 2](h[t][:, u * BANK:(u + 1) * BANK], acc[:])
             return h
 
-        def pick(b, h, tag, square_tag):
-            log_a[b] = kept([P, PACK, M], F32, "log_a%d" % b)
+        def pick(h, tag):
             picked = late.tile([P, PACK, M], F32, name="picked", tag=tag, align_bytes=64)
-            square_a = kept([P, PACK, M], F32, square_tag)
             for t in range(PACK):
                 nc.vector.tensor_copy(picked[:, t, :], h[t][:].indirect(pos_sb[:]))
-                nc.scalar.activation(out=square_a[:, t, :], in_=picked[:, t, :], func=ACT.Square)
-                nc.scalar.activation(out=log_a[b][:, t, :], in_=square_a[:, t, :], func=ACT.Ln, bias=half[:])
+            return picked
+
+        def logs(b, picked):
+            log_a[b] = kept([P, PACK, M], F32, "log_a%d" % b)
+            for t in range(PACK):
+                nc.scalar.activation(out=picked[:, t, :], in_=picked[:, t, :], func=ACT.Square)
+                nc.scalar.activation(out=log_a[b][:, t, :], in_=picked[:, t, :], func=ACT.Ln, bias=half[:])
 
         z_codes, z_planes = {}, {}
 
         def project_files(b):
-            log_b = kept([P, PACK, M], F32, "log_b%d" % b)
             square_bt = kept([P, M // P, PACK, P], F32, "square_bt%d" % b)
             for i in range(M // P):
                 files = slice(i * P, (i + 1) * P)
-                bt = psum.tile([P, BANK], F32, name="bt", tag="bt", bufs=2)
+                bt = psum.tile([P, BANK], F32, name="bt", tag="low%d" % i)
                 for a in range(A2):
                     nc.tensor.matmul_mx(
                         out=bt[:],
@@ -208,67 +213,83 @@ def tile_list_ransomware_alarm_levels_kernel(
                         start=(a == 0), stop=(a == A2 - 1),
                     )
                 nc.scalar.activation(
-                    out=square_bt[:, i], in_=bt[:].rearrange("m (p t) -> m t p", t=PACK), func=ACT.Square
+                    out=square_bt[:, i].rearrange("m (u v) p -> m u p v", u=2),
+                    in_=bt[:].rearrange("m (p u v) -> m u p v", u=2, v=2),
+                    func=ACT.Square,
                 )
-                square_b = psum.tile([P, PACK, P], F32, name="square_b", tag="square_b", bufs=2)
+            return square_bt
+
+        def turn_and_log(b, square_bt, picked=None):
+            log_b = kept([P, PACK, M], F32, "log_b%d" % b)
+            for i in range(M // P):
+                if picked is not None:
+                    part = picked[:, :, i * P:(i + 1) * P]
+                    nc.scalar.activation(
+                        out=log_a[b][:, :, i * P:(i + 1) * P], in_=part, func=ACT.Ln, bias=half[:]
+                    )
+                square_b = psum.tile([P, PACK, P], F32, name="square_b", tag="high%d" % i)
                 for t in range(PACK):
                     nc.tensor.transpose(square_b[:, t, :], square_bt[:, i, t, :], ident[:])
-                nc.scalar.activation(out=log_b[:, :, files], in_=square_b[:], func=ACT.Ln, bias=half[:])
+                nc.scalar.activation(
+                    out=log_b[:, :, i * P:(i + 1) * P], in_=square_b[:], func=ACT.Ln, bias=half[:]
+                )
             return log_b
 
         def make_z(b, log_b, width):
-            chunks = M // width
-            z = {}
-            for step in range(chunks + 2):
-                if step < chunks:
-                    files = slice(step * width, (step + 1) * width)
-                    diff = log_b[:, :, files]
-                    nc.vector.tensor_tensor(diff, diff, log_a[b][:, :, files], ALU.subtract)
-                if 1 <= step <= chunks:
-                    c = step - 1
-                    z[c] = ring.tile([P, PACK * width], BF16, name="z", tag="z", align_bytes=64, bufs=3)
-                    nc.vector.tensor_tensor(
-                        z[c][:].rearrange("p (c e t) -> p c t e", e=4, t=PACK),
-                        log_b[:, :, c * width:(c + 1) * width].rearrange("p t (c e) -> p c t e", e=4),
-                        gain_sb[:, b, :].unsqueeze(1).unsqueeze(3).to_broadcast([P, width // 4, PACK, 4]),
-                        ALU.mult,
-                    )
-                if step >= 2:
-                    c = step - 2
-                    codes = kept([P, width], U32, "zc%d_%d" % (b, c))
-                    planes = kept([P, width], U8, "zs%d_%d" % (b, c))
-                    nc.vector.quantize_mx(out=codes[:].bitcast(FP8X4), scales=planes[:], in_=z[c][:])
-                    for c0 in range(0, width, P):
-                        z_codes[b, (c * width + c0) // P] = codes[:, c0:c0 + P]
-                        z_planes[b, (c * width + c0) // P] = planes[:, c0:c0 + P]
+            for m0 in range(0, M, width):
+                files = slice(m0, m0 + width)
+                diff = log_b[:, :, files]
+                nc.vector.tensor_tensor(diff, diff, log_a[b][:, :, files], ALU.subtract)
+                z = ring.tile([P, PACK * width], BF16, name="z", tag="z", align_bytes=64, bufs=3)
+                nc.vector.tensor_tensor(
+                    z[:].rearrange("p (c e t) -> p c t e", e=4, t=PACK),
+                    diff.rearrange("p t (c e) -> p c t e", e=4),
+                    gain_sb[:, b, :].unsqueeze(1).unsqueeze(3).to_broadcast([P, width // 4, PACK, 4]),
+                    ALU.mult,
+                )
+                codes = kept([P, width], U32, "zc%d_%d" % (b, m0))
+                planes = kept([P, width], U8, "zs%d_%d" % (b, m0))
+                nc.vector.quantize_mx(out=codes[:].bitcast(FP8X4), scales=planes[:], in_=z[:])
+                for c0 in range(0, width, P):
+                    z_codes[b, (m0 + c0) // P] = codes[:, c0:c0 + P]
+                    z_planes[b, (m0 + c0) // P] = planes[:, c0:c0 + P]
 
         h0 = first_stage(0, (nc.scalar.copy, nc.scalar.copy))
         for a in range(A1):
-            quantise_w1(1, a, round_w1(1, a, nc.vector.tensor_copy))
-        pick(0, h0, "picked0", "square_bt1")
+            quantise_w1(1, a, round_w1(1, a, nc.vector.tensor_copy, late))
+        picked0 = pick(h0, "w1_bf1")
+        h1 = first_stage(1, (nc.scalar.copy, nc.scalar.copy))
         v2_codes = []
         for a in range(A2):
             v2_codes.append(kept([P, M], U32, "v2_%d" % a))
             nc.vector.tensor_copy(v2_codes[a][:], tab2_sb[a][:].bitcast(U32).indirect(offs2_sb[:]))
-        h1 = first_stage(1, (nc.scalar.copy, nc.scalar.copy))
-        log_b0 = project_files(0)
-        pick(1, h1, "tab2_%d" % (A2 - 1), "square_bt0")
-        make_z(0, log_b0, 2 * P)
-        make_z(1, project_files(1), P)
+        logs(0, picked0)
+        picked1 = pick(h1, TAG1)
+        log_b0 = turn_and_log(0, project_files(0))
+        square_bt1 = project_files(1)
+        log_a[1] = kept([P, PACK, M], F32, "log_a1")
+        if NV:
+            part = picked1[:, :, :NV * P]
+            nc.vector.tensor_tensor(part, part, part, ALU.mult)
+        if NV < 4:
+            part = picked1[:, :, NV * P:]
+            nc.scalar.activation(out=part, in_=part, func=ACT.Square)
+        make_z(0, log_b0, W0)
+        make_z(1, turn_and_log(1, square_bt1, picked1), P)
 
         out_view = out.rearrange("(g p) m -> p g m", p=P)
         levels = keep.tile([P, M // P, N // P, P], F32, name="levels", tag="half")
         for i in range(M // P):
-            y = psum.tile([P, N // P, P], F32, name="acc", tag="acc", bufs=4)
-            for g in range(N // P):
-                for b in range(B):
+            y = psum.tile([P, N // P, P], F32, name="y", tag="low%d" % i)
+            for b in range(B):
+                for g in range(N // P):
                     nc.tensor.matmul_mx(
                         out=y[:, g, :],
                         lhsT=w3_sb[b][:, g * P:(g + 1) * P].bitcast(FP8X4),
                         lhsT_scale=w3_planes[:, b * N + g * P:b * N + (g + 1) * P],
                         rhs=z_codes[b, i].bitcast(FP8X4),
                         rhs_scale=z_planes[b, i],
-                        start=(b == 0), stop=(b == B - 1),
+                        start=(b == 0 and g == 0), stop=(b == B - 1 and g == N // P - 1),
                     )
             nc.scalar.activation(out=levels[:, i], in_=y[:], func=ACT.Sigmoid)
             nc.sync.dma_start(out=out_view[:, :, i * P:(i + 1) * P], in_=levels[:, i])

@@ -78,10 +78,10 @@ def tile_list_ransomware_alarm_levels_kernel(
 
             def load_planes(planes, scales, passes):
                 view = planes[:].bitcast(I32).rearrange("p (a c) -> p a c", a=passes)
-                for q in range(QUADS):
+                for r in range(4):
                     nc.sync.dma_start(
-                        out=view[32 * q:32 * q + 4],
-                        in_=scales[:, 4 * q:4 * q + 4, :].bitcast(I32).rearrange("a r c -> r a c"),
+                        out=view[r:P:32],
+                        in_=scales[:, r:16:4, :].bitcast(I32).rearrange("a q c -> q a c"),
                     )
 
             w1_raw = {}
@@ -123,8 +123,8 @@ def tile_list_ransomware_alarm_levels_kernel(
             def round_w1(b, a, copy, pool):
                 grouped = kept([P, PACK * PASS], BF16, "w1_bf%d" % a, pool)
                 copy(
-                    grouped[:].rearrange("p (u v m j) -> p u m j v", u=2, v=2, j=PACK),
-                    w1_raw[b, a][:].rearrange("p j (m u v) -> p u m j v", u=2, v=2),
+                    grouped[:].rearrange("p (t m j) -> p m t j", t=PACK, j=PACK),
+                    w1_raw[b, a][:].rearrange("p j (m t) -> p m t j", t=PACK),
                 )
                 return grouped
 
@@ -190,11 +190,20 @@ def tile_list_ransomware_alarm_levels_kernel(
                 nc.vector.tensor_copy(picked[:, t, :], h[t][:].indirect(pos_sb[:]))
             return picked
 
+        def log_of_picks(b, picked, m0, width):
+            nc.scalar.activation(
+                out=log_a[b][:, m0:m0 + width, :].rearrange("p (c e) t -> p c t e", e=4),
+                in_=picked[:, :, m0:m0 + width].rearrange("p t (c e) -> p c t e", e=4),
+                func=ACT.Ln, bias=half[:],
+            )
+
         def logs(b, picked):
-            log_a[b] = kept([P, PACK, M], F32, "log_a%d" % b)
-            for t in range(PACK):
-                nc.scalar.activation(out=picked[:, t, :], in_=picked[:, t, :], func=ACT.Square)
-                nc.scalar.activation(out=log_a[b][:, t, :], in_=picked[:, t, :], func=ACT.Ln, bias=half[:])
+            log_a[b] = kept([P, M, PACK], F32, "log_a%d" % b)
+            for m0 in range(0, M, W0):
+                part = picked[:, :, m0:m0 + W0]
+                nc.scalar.activation(out=part, in_=part, func=ACT.Square)
+            for m0 in range(0, M, W0):
+                log_of_picks(b, picked, m0, W0)
 
         z_codes, z_planes = {}, {}
 
@@ -220,31 +229,29 @@ def tile_list_ransomware_alarm_levels_kernel(
             return square_bt
 
         def turn_and_log(b, square_bt, picked=None):
-            log_b = kept([P, PACK, M], F32, "log_b%d" % b)
+            log_b = kept([P, M, PACK], F32, "log_b%d" % b)
             for i in range(M // P):
                 if picked is not None:
-                    part = picked[:, :, i * P:(i + 1) * P]
-                    nc.scalar.activation(
-                        out=log_a[b][:, :, i * P:(i + 1) * P], in_=part, func=ACT.Ln, bias=half[:]
-                    )
+                    log_of_picks(b, picked, i * P, P)
                 square_b = psum.tile([P, PACK, P], F32, name="square_b", tag="high%d" % i)
                 for t in range(PACK):
                     nc.tensor.transpose(square_b[:, t, :], square_bt[:, i, t, :], ident[:])
                 nc.scalar.activation(
-                    out=log_b[:, :, i * P:(i + 1) * P], in_=square_b[:], func=ACT.Ln, bias=half[:]
+                    out=log_b[:, i * P:(i + 1) * P, :], in_=square_b[:].rearrange("p t m -> p m t"),
+                    func=ACT.Ln, bias=half[:],
                 )
             return log_b
 
         def make_z(b, log_b, width):
             for m0 in range(0, M, width):
                 files = slice(m0, m0 + width)
-                diff = log_b[:, :, files]
-                nc.vector.tensor_tensor(diff, diff, log_a[b][:, :, files], ALU.subtract)
+                diff = log_b[:, files, :]
+                nc.vector.tensor_tensor(diff, diff, log_a[b][:, files, :], ALU.subtract)
                 z = ring.tile([P, PACK * width], BF16, name="z", tag="z", align_bytes=64, bufs=3)
                 nc.vector.tensor_tensor(
-                    z[:].rearrange("p (c e t) -> p c t e", e=4, t=PACK),
-                    diff.rearrange("p t (c e) -> p c t e", e=4),
-                    gain_sb[:, b, :].unsqueeze(1).unsqueeze(3).to_broadcast([P, width // 4, PACK, 4]),
+                    z[:].rearrange("p (m t) -> p m t", t=PACK),
+                    diff,
+                    gain_sb[:, b, :].unsqueeze(1).to_broadcast([P, width, PACK]),
                     ALU.mult,
                 )
                 codes = kept([P, width], U32, "zc%d_%d" % (b, m0))
@@ -267,7 +274,7 @@ def tile_list_ransomware_alarm_levels_kernel(
         picked1 = pick(h1, TAG1)
         log_b0 = turn_and_log(0, project_files(0))
         square_bt1 = project_files(1)
-        log_a[1] = kept([P, PACK, M], F32, "log_a1")
+        log_a[1] = kept([P, M, PACK], F32, "log_a1")
         if NV:
             part = picked1[:, :, :NV * P]
             nc.vector.tensor_tensor(part, part, part, ALU.mult)

@@ -4,7 +4,9 @@ from contextlib import ExitStack
 import concourse.mybir as mybir
 from concourse.masks import make_identity
 
-K, T, S, K2, T2, M, H, N = 1024, 4096, 1024, 1536, 2048, 512, 1024, 512
+K, T, S = 1024, 4096, 1024
+K2, T2, M = 1536, 2048, 512
+H, N = 1024, 512
 FLOPS = 2 * (K * H * S + K2 * H * M + H * N * M)
 
 F32 = mybir.dt.float32
@@ -22,15 +24,21 @@ P = 128
 PACK = 4
 PASS = P * PACK
 BANK = 512
-QUADS = 4
-A1, A2, B = K // PASS, K2 // PASS, H // PASS
-LIST = 16
-NV = 3
-NACC, NBT, NSQ, W0, TAG1, SQT = 4, 4, 4, 256, "tab2_2", "acc"
+QUADS, QUAD = 4, 32
+ROWS = 4
+SCALE_ROWS = QUADS * ROWS
+GROUP = 16
+PASSES, PASSES2, BLOCKS = K // PASS, K2 // PASS, H // PASS
+HALVES = S // BANK
+CHUNKS = M // P
+LINE = 4
+
+VECTOR_SQUARES = 3
+WIDE = 2 * P
 
 
 def words_of(packed):
-    return packed.rearrange("p n i -> p (n i)").bitcast(I32)
+    return packed.rearrange("p c i -> p (c i)").bitcast(I32)
 
 
 def tile_list_ransomware_alarm_levels_kernel(
@@ -39,264 +47,252 @@ def tile_list_ransomware_alarm_levels_kernel(
 ):
     nc = tc.nc
     with ExitStack() as ctx:
-        keep = ctx.enter_context(tc.tile_pool(name="keep", bufs=1))
-        ring = ctx.enter_context(tc.tile_pool(name="ring", bufs=2))
+        sbuf = ctx.enter_context(tc.tile_pool(name="sbuf", bufs=1))
         psum = ctx.enter_context(tc.psum_pool(name="psum", bufs=1))
 
-        def kept(shape, dtype, name, pool=keep):
-            return pool.tile(shape, dtype, name=name, tag=name, align_bytes=64)
+        def new_tile(shape, dtype, name, after=None):
+            return sbuf.tile(shape, dtype, name=name, tag=after or name, align_bytes=64)
 
-        offs_sb = keep.tile([P, S // LIST], U16, name="offs_sb")
-        pos_sb = keep.tile([P, M // LIST], U16, name="pos_sb")
-        offs2_sb = keep.tile([P, M // LIST], U16, name="offs2_sb")
+        offs_sb = sbuf.tile([P, S // GROUP], U16, name="offs_sb")
+        pos_sb = sbuf.tile([P, M // GROUP], U16, name="pos_sb")
+        offs2_sb = sbuf.tile([P, M // GROUP], U16, name="offs2_sb")
 
-        with tc.tile_pool(name="head", bufs=1) as head:
-            tab_sc = kept([P, T], U8, "tab_sc", head)
-            tab2_sc = kept([P, T2], U8, "tab2_sc", head)
-            v_planes = kept([P, A1 * S], U8, "v_planes")
-            v2_planes = kept([P, A2 * M], U8, "v2_planes")
-            half = keep.tile([P, 1], F32, name="half", tag="half")
-            nc.vector.memset(half[:], 0.5)
-            row0, row0_2 = P - 16 * A1, P - 16 * A2
-            nc.vector.memset(tab_sc[:].bitcast(I32)[:row0], 0)
-            nc.vector.memset(tab2_sc[:].bitcast(I32)[:row0_2], 0)
-            for zeroed in (v_planes, v2_planes):
-                nc.vector.memset(zeroed[:].bitcast(I32), 0)
-            warm = kept([P, 1], F32, "warm")
-            nc.scalar.activation(out=warm[:], in_=half[:], func=ACT.Ln)
+        tab_sc = new_tile([P, T], U8, "tab_sc")
+        tab2_sc = new_tile([P, T2], U8, "tab2_sc")
+        v_planes = new_tile([P, PASSES * S], U8, "v_planes")
+        v2_planes = new_tile([P, PASSES2 * M], U8, "v2_planes")
+        top, top2 = P - SCALE_ROWS * PASSES, P - SCALE_ROWS * PASSES2
+        half = new_tile([P, 1], F32, "half")
+        nc.vector.memset(half[:], 0.5)
+        nc.vector.memset(tab_sc[:].bitcast(I32)[:top], 0)
+        nc.vector.memset(tab2_sc[:].bitcast(I32)[:top2], 0)
+        for planes in (v_planes, v2_planes):
+            nc.vector.memset(planes[:].bitcast(I32), 0)
 
-            def load_w1(b, a, pool):
-                raw = kept([P, PACK, PASS], F32, "w1_raw%d" % a, pool)
-                rows = w1[a * PASS:(a + 1) * PASS, b * PASS:(b + 1) * PASS]
-                nc.sync.dma_start(out=raw[:], in_=rows.rearrange("(p j) c -> p j c", j=PACK))
-                return raw
+        warm = new_tile([P, 1], F32, "warm")
+        nc.scalar.activation(out=warm[:], in_=half[:], func=ACT.Ln)
 
-            def load_words(src, width, name):
-                dst = kept([P, width], I32, name, late)
-                nc.sync.dma_start(out=dst[:], in_=src)
-                return dst
+        def load_w1(blk, a, after=None):
+            raw = new_tile([P, PACK, PASS], F32, "w1_raw%d%d" % (blk, a), after)
+            rows = w1[a * PASS:(a + 1) * PASS, blk * PASS:(blk + 1) * PASS]
+            nc.sync.dma_start(out=raw[:], in_=rows.rearrange("(p j) c -> p j c", j=PACK))
+            return raw
 
-            def load_planes(planes, scales, passes):
-                view = planes[:].bitcast(I32).rearrange("p (a c) -> p a c", a=passes)
-                for r in range(4):
-                    nc.sync.dma_start(
-                        out=view[r:P:32],
-                        in_=scales[:, r:16:4, :].bitcast(I32).rearrange("a q c -> q a c"),
-                    )
+        def load_tab2(a, after):
+            words = new_tile([P, T2], I32, "tab2_%d" % a, after)
+            nc.sync.dma_start(out=words[:], in_=words_of(tab2_words[a]))
+            return words
 
-            w1_raw = {}
-            nc.sync.dma_start(
-                out=tab_sc[:].bitcast(I32)[row0:],
-                in_=tab_scales.bitcast(I32).rearrange("a q c -> q a c"),
-            )
-            nc.sync.dma_start(offs_sb[:], offs)
-            w1_raw[0, 0] = load_w1(0, 0, head)
-            nc.scalar.dma_start(
-                out=tab2_sc[:].bitcast(I32)[row0_2:],
-                in_=tab2_scales.bitcast(I32).rearrange("a q c -> q a c"),
-            )
-            nc.sync.dma_start(offs2_sb[:], offs2)
-            w1_raw[0, 1] = load_w1(0, 1, head)
-            nc.sync.dma_start(pos_sb[:], pos1)
-            gain_sb = kept([P, B, PACK], F32, "gain_sb")
-            nc.sync.dma_start(out=gain_sb[:], in_=gain.rearrange("(b p t) -> p b t", b=B, t=PACK))
-            tab_sb = [kept([P, T], I32, "tab%d" % a) for a in range(A1)]
-            for a in range(A1):
-                for c0 in range(0, T, T // 2):
-                    nc.sync.dma_start(out=tab_sb[a][:, c0:c0 + T // 2], in_=words_of(tab_words[a])[:, c0:c0 + T // 2])
+        def load_planes(planes, scales, passes):
+            view = planes[:].bitcast(I32).rearrange("p (a c) -> p a c", a=passes)
+            for r in range(ROWS):
+                nc.sync.dma_start(
+                    out=view[r:P:QUAD],
+                    in_=scales[:, r:SCALE_ROWS:ROWS, :].bitcast(I32).rearrange("a q c -> q a c"),
+                )
 
-            ident = kept([P, P], F32, "ident")
-            make_identity(nc, ident[:])
-
-            v_sc = kept([P, S], U8, "v_sc")
-            nc.vector.tensor_copy(v_sc[:], tab_sc[:].indirect(offs_sb[:]))
-            v2_sc = kept([P, M], U8, "v2_sc")
-            nc.vector.tensor_copy(v2_sc[:], tab2_sc[:].indirect(offs2_sb[:]))
+        def carry_planes(planes, gathered, lowest, passes):
+            view = planes[:].bitcast(I32).rearrange("p (a c) -> p a c", a=passes)
             for q in range(QUADS):
-                nc.gpsimd.dma_start(
-                    out=v2_planes[:].bitcast(I32).rearrange("p (a c) -> p a c", a=A2)[32 * q:32 * q + 4],
-                    in_=v2_sc[:].bitcast(I32)[row0_2 + 4 * A2 * q:row0_2 + 4 * A2 * (q + 1)],
+                start = lowest + q * ROWS * passes
+                nc.sync.dma_start(
+                    out=view[q * QUAD:q * QUAD + ROWS], in_=gathered[:].bitcast(I32)[start:start + ROWS * passes]
                 )
 
-            w1_codes, w1_planes = {}, {}
+        w1_raw = {}
+        nc.sync.dma_start(out=tab_sc[:].bitcast(I32)[top:], in_=tab_scales.bitcast(I32).rearrange("a q c -> q a c"))
+        nc.sync.dma_start(offs_sb[:], offs)
+        w1_raw[0, 0] = load_w1(0, 0)
+        nc.scalar.dma_start(
+            out=tab2_sc[:].bitcast(I32)[top2:], in_=tab2_scales.bitcast(I32).rearrange("a q c -> q a c")
+        )
+        w1_raw[0, 1] = load_w1(0, 1)
+        nc.sync.dma_start(offs2_sb[:], offs2)
+        nc.sync.dma_start(pos_sb[:], pos1)
+        gain_sb = new_tile([P, BLOCKS, PACK], F32, "gain_sb")
+        nc.sync.dma_start(out=gain_sb[:], in_=gain.rearrange("(b p t) -> p b t", b=BLOCKS, t=PACK))
+        tab_sb = [new_tile([P, T], I32, "tab%d" % a) for a in range(PASSES)]
+        for a in range(PASSES):
+            for c0 in range(0, T, T // 2):
+                nc.sync.dma_start(out=tab_sb[a][:, c0:c0 + T // 2], in_=words_of(tab_words[a])[:, c0:c0 + T // 2])
 
-            def round_w1(b, a, copy, pool):
-                grouped = kept([P, PACK * PASS], BF16, "w1_bf%d" % a, pool)
-                copy(
-                    grouped[:].rearrange("p (t m j) -> p m t j", t=PACK, j=PACK),
-                    w1_raw[b, a][:].rearrange("p j (m t) -> p m t j", t=PACK),
-                )
-                return grouped
+        ident = new_tile([P, P], F32, "ident")
+        make_identity(nc, ident[:])
 
-            def quantise_w1(b, a, grouped):
-                w1_codes[b, a] = kept([P, PASS], U32, "w1c%d%d" % (b, a))
-                w1_planes[b, a] = kept([P, PASS], U8, "w1s%d%d" % (b, a))
-                nc.vector.quantize_mx(out=w1_codes[b, a][:].bitcast(FP8X4), scales=w1_planes[b, a][:], in_=grouped[:])
+        v_sc = new_tile([P, S], U8, "v_sc")
+        nc.vector.tensor_copy(v_sc[:], tab_sc[:].indirect(offs_sb[:]))
+        v2_sc = new_tile([P, M], U8, "v2_sc")
+        nc.vector.tensor_copy(v2_sc[:], tab2_sc[:].indirect(offs2_sb[:]))
 
-            for a in range(A1):
-                quantise_w1(0, a, round_w1(0, a, (nc.scalar.copy, nc.vector.tensor_copy)[a], head))
-            for q in range(QUADS):
-                nc.scalar.dma_start(
-                    out=v_planes[:].bitcast(I32).rearrange("p (a c) -> p a c", a=A1)[32 * q:32 * q + 4],
-                    in_=v_sc[:].bitcast(I32)[row0 + 4 * A1 * q:row0 + 4 * A1 * (q + 1)],
-                )
+        w1_codes, w1_planes = {}, {}
 
-        late = ctx.enter_context(tc.tile_pool(name="late", bufs=1))
+        def quantise_w1(blk, a, copy, after=None):
+            grouped = new_tile([P, PACK * PASS], BF16, "w1_bf%d%d" % (blk, a), after)
+            copy(
+                grouped[:].rearrange("p (u e m j) -> p u m j e", u=2, e=2, j=PACK),
+                w1_raw[blk, a][:].rearrange("p j (m u e) -> p u m j e", u=2, e=2),
+            )
+            w1_codes[blk, a] = new_tile([P, PASS], U32, "w1_codes%d%d" % (blk, a))
+            w1_planes[blk, a] = new_tile([P, PASS], U8, "w1_planes%d%d" % (blk, a))
+            nc.vector.quantize_mx(out=w1_codes[blk, a][:].bitcast(FP8X4), scales=w1_planes[blk, a][:], in_=grouped[:])
 
-        halves = S // BANK
+        quantise_w1(0, 0, nc.scalar.copy)
+        quantise_w1(0, 1, nc.vector.tensor_copy, "tab_sc")
+        carry_planes(v_planes, v_sc, top, PASSES)
+
         v_codes = {}
-        for a in range(A1):
-            for u in range(halves):
-                v_codes[a, u] = kept([P, BANK], U32, "v%d%d" % (a, u))
-                cols = slice(u * BANK // LIST, (u + 1) * BANK // LIST)
-                nc.vector.tensor_copy(v_codes[a, u][:], tab_sb[a][:].bitcast(U32).indirect(offs_sb[:, cols]))
+        for a, u in itertools.product(range(PASSES), range(HALVES)):
+            v_codes[a, u] = new_tile([P, BANK], U32, "v%d%d" % (a, u))
+            entries = offs_sb[:, u * BANK // GROUP:(u + 1) * BANK // GROUP]
+            nc.vector.tensor_copy(v_codes[a, u][:], tab_sb[a][:].bitcast(U32).indirect(entries))
 
-        for a in range(A1):
-            w1_raw[1, a] = load_w1(1, a, late)
-        w2_planes = kept([P, A2 * H], U8, "w2_planes", late)
-        w3_planes = kept([P, B * N], U8, "w3_planes", late)
-        for zeroed in (w2_planes, w3_planes):
-            nc.vector.memset(zeroed[:].bitcast(I32), 0)
-        tab2_sb, w2_sb = [], []
-        load_planes(w2_planes, w2_scales, A2)
-        for a in range(A2):
-            w2_sb.append(load_words(w2_words[a].bitcast(I32), H // 2, "w2_%d" % a))
-            tab2_sb.append(load_words(words_of(tab2_words[a]), T2, "tab2_%d" % a))
-        load_planes(w3_planes, w3_scales, B)
-        w3_sb = [load_words(words_of(w3_words[b]), N, "w3_%d" % b) for b in range(B)]
+        def zeroed_planes(width, name, after):
+            planes = new_tile([P, width], U8, name, after)
+            nc.gpsimd.memset(planes[:].bitcast(I32), 0)
+            return planes
 
-        log_a = {}
+        w1_raw[1, 0] = load_w1(1, 0, "w1_raw01")
+        w1_raw[1, 1] = load_w1(1, 1, "tab_sc")
+        tab2_sb = [load_tab2(0, "tab0")]
+        carry_planes(v2_planes, v2_sc, top2, PASSES2)
+        w2_planes = zeroed_planes(PASSES2 * H, "w2_planes", "v_sc")
+        load_planes(w2_planes, w2_scales, PASSES2)
+        tab2_sb.append(load_tab2(1, "tab1"))
+        w2_sb = new_tile([P, PASSES2 * 2 * H], U8, "w2_sb", "w1_raw01")
+        nc.sync.dma_start(
+            out=w2_sb[:].bitcast(I32).rearrange("p (a c) -> p a c", a=PASSES2),
+            in_=w2_words.bitcast(I32).rearrange("a p c -> p a c"),
+        )
+        tab2_sb.append(load_tab2(2, "tab_sc"))
 
-        def first_stage(b, copies):
-            h = [ring.tile([P, S], F32, name="h", tag="h", bufs=8) for t in range(PACK)]
+        def first_stage(blk):
+            h = [new_tile([P, S], F32, "h%d%d" % (blk, t)) for t in range(PACK)]
             for t0 in range(0, PACK, 2):
-                for u, t in itertools.product(range(halves), (t0, t0 + 1)):
-                    acc = psum.tile([P, BANK], F32, name="acc", tag="low%d" % (2 * u + t % 2))
-                    for a in range(A1):
+                for u, e in itertools.product(range(HALVES), range(2)):
+                    cols = slice((t0 + e) * P, (t0 + e + 1) * P)
+                    acc = psum.tile([P, BANK], F32, name="acc", tag="low%d" % (2 * u + e))
+                    for a in range(PASSES):
                         nc.tensor.matmul_mx(
                             out=acc[:],
-                            lhsT=w1_codes[b, a][:, t * P:(t + 1) * P].bitcast(FP8X4),
-                            lhsT_scale=w1_planes[b, a][:, t * P:(t + 1) * P],
+                            lhsT=w1_codes[blk, a][:, cols].bitcast(FP8X4),
+                            lhsT_scale=w1_planes[blk, a][:, cols],
                             rhs=v_codes[a, u][:].bitcast(FP8X4),
                             rhs_scale=v_planes[:, a * S + u * BANK:a * S + (u + 1) * BANK],
-                            start=(a == 0), stop=(a == A1 - 1),
+                            start=(a == 0), stop=(a == PASSES - 1),
                         )
-                    copies[t % 2](h[t][:, u * BANK:(u + 1) * BANK], acc[:])
+                    nc.scalar.copy(h[t0 + e][:, u * BANK:(u + 1) * BANK], acc[:])
             return h
 
-        def pick(h, tag):
-            picked = late.tile([P, PACK, M], F32, name="picked", tag=tag, align_bytes=64)
-            for t in range(PACK):
-                nc.vector.tensor_copy(picked[:, t, :], h[t][:].indirect(pos_sb[:]))
-            return picked
-
-        def log_of_picks(b, picked, m0, width):
-            nc.scalar.activation(
-                out=log_a[b][:, m0:m0 + width, :].rearrange("p (c e) t -> p c t e", e=4),
-                in_=picked[:, :, m0:m0 + width].rearrange("p t (c e) -> p c t e", e=4),
-                func=ACT.Ln, bias=half[:],
-            )
-
-        def logs(b, picked):
-            log_a[b] = kept([P, M, PACK], F32, "log_a%d" % b)
-            for m0 in range(0, M, W0):
-                part = picked[:, :, m0:m0 + W0]
-                nc.scalar.activation(out=part, in_=part, func=ACT.Square)
-            for m0 in range(0, M, W0):
-                log_of_picks(b, picked, m0, W0)
-
-        z_codes, z_planes = {}, {}
-
-        def project_files(b):
-            square_bt = kept([P, M // P, PACK, P], F32, "square_bt%d" % b)
-            for i in range(M // P):
-                files = slice(i * P, (i + 1) * P)
+        def project_files(blk):
+            square_bt = new_tile([P, CHUNKS, PACK, P], F32, "square_bt%d" % blk)
+            for i in range(CHUNKS):
                 bt = psum.tile([P, BANK], F32, name="bt", tag="low%d" % i)
-                for a in range(A2):
+                for a in range(PASSES2):
+                    c0 = a * H + blk * PASS
                     nc.tensor.matmul_mx(
                         out=bt[:],
-                        lhsT=v2_codes[a][:, files].bitcast(FP8X4),
+                        lhsT=v2_codes[a][:, i * P:(i + 1) * P].bitcast(FP8X4),
                         lhsT_scale=v2_planes[:, a * M + i * P:a * M + (i + 1) * P],
-                        rhs=w2_sb[a][:].bitcast(U8)[:, 2 * b * PASS:2 * (b + 1) * PASS].bitcast(FP4X4),
-                        rhs_scale=w2_planes[:, a * H + b * PASS:a * H + (b + 1) * PASS],
-                        start=(a == 0), stop=(a == A2 - 1),
+                        rhs=w2_sb[:, 2 * c0:2 * (c0 + PASS)].bitcast(FP4X4),
+                        rhs_scale=w2_planes[:, c0:c0 + PASS],
+                        start=(a == 0), stop=(a == PASSES2 - 1),
                     )
                 nc.scalar.activation(
-                    out=square_bt[:, i].rearrange("m (u v) p -> m u p v", u=2),
-                    in_=bt[:].rearrange("m (p u v) -> m u p v", u=2, v=2),
+                    out=square_bt[:, i].rearrange("m (u e) p -> m u p e", u=2),
+                    in_=bt[:].rearrange("m (p u e) -> m u p e", u=2, e=2),
                     func=ACT.Square,
                 )
             return square_bt
 
-        def turn_and_log(b, square_bt, picked=None):
-            log_b = kept([P, M, PACK], F32, "log_b%d" % b)
-            for i in range(M // P):
-                if picked is not None:
-                    log_of_picks(b, picked, i * P, P)
-                square_b = psum.tile([P, PACK, P], F32, name="square_b", tag="high%d" % i)
-                for t in range(PACK):
-                    nc.tensor.transpose(square_b[:, t, :], square_bt[:, i, t, :], ident[:])
-                nc.scalar.activation(
-                    out=log_b[:, i * P:(i + 1) * P, :], in_=square_b[:].rearrange("p t m -> p m t"),
-                    func=ACT.Ln, bias=half[:],
-                )
-            return log_b
+        def log_b_chunk(log_b, square_bt, i):
+            square_b = psum.tile([P, PACK, P], F32, name="square_b", tag="high%d" % i)
+            for t in range(PACK):
+                nc.tensor.transpose(square_b[:, t, :], square_bt[:, i, t, :], ident[:])
+            nc.scalar.activation(out=log_b[:, :, i * P:(i + 1) * P], in_=square_b[:], func=ACT.Ln, bias=half[:])
 
-        def make_z(b, log_b, width):
+        z_codes, z_planes = {}, {}
+
+        def make_z(blk, log_b, log_a, width):
             for m0 in range(0, M, width):
-                files = slice(m0, m0 + width)
-                diff = log_b[:, files, :]
-                nc.vector.tensor_tensor(diff, diff, log_a[b][:, files, :], ALU.subtract)
-                z = ring.tile([P, PACK * width], BF16, name="z", tag="z", align_bytes=64, bufs=3)
+                diff = log_b[:, :, m0:m0 + width]
+                nc.vector.tensor_tensor(diff, diff, log_a[:, :, m0:m0 + width], ALU.subtract)
+                z = sbuf.tile([P, PACK * width], BF16, name="z", tag="z", align_bytes=64, bufs=3)
                 nc.vector.tensor_tensor(
-                    z[:].rearrange("p (m t) -> p m t", t=PACK),
-                    diff,
-                    gain_sb[:, b, :].unsqueeze(1).to_broadcast([P, width, PACK]),
+                    z[:].rearrange("p (c e t) -> p c t e", e=LINE, t=PACK),
+                    diff.rearrange("p t (c e) -> p c t e", e=LINE),
+                    gain_sb[:, blk, :].unsqueeze(1).unsqueeze(3).to_broadcast([P, width // LINE, PACK, LINE]),
                     ALU.mult,
                 )
-                codes = kept([P, width], U32, "zc%d_%d" % (b, m0))
-                planes = kept([P, width], U8, "zs%d_%d" % (b, m0))
-                nc.vector.quantize_mx(out=codes[:].bitcast(FP8X4), scales=planes[:], in_=z[:])
+                codes = new_tile([P, width], U32, "z_codes%d_%d" % (blk, m0))
+                plane = new_tile([P, width], U8, "z_planes%d_%d" % (blk, m0))
+                nc.vector.quantize_mx(out=codes[:].bitcast(FP8X4), scales=plane[:], in_=z[:])
                 for c0 in range(0, width, P):
-                    z_codes[b, (m0 + c0) // P] = codes[:, c0:c0 + P]
-                    z_planes[b, (m0 + c0) // P] = planes[:, c0:c0 + P]
+                    z_codes[blk, (m0 + c0) // P] = codes[:, c0:c0 + P]
+                    z_planes[blk, (m0 + c0) // P] = plane[:, c0:c0 + P]
 
-        h0 = first_stage(0, (nc.scalar.copy, nc.scalar.copy))
-        for a in range(A1):
-            quantise_w1(1, a, round_w1(1, a, nc.vector.tensor_copy, late))
-        picked0 = pick(h0, "w1_bf1")
-        h1 = first_stage(1, (nc.scalar.copy, nc.scalar.copy))
-        v2_codes = []
-        for a in range(A2):
-            v2_codes.append(kept([P, M], U32, "v2_%d" % a))
+        h0 = first_stage(0)
+        for a in range(PASSES):
+            quantise_w1(1, a, nc.vector.tensor_copy)
+
+        first = new_tile([P, M], F32, "first", "w1_bf10")
+        others = new_tile([P, PACK - 1, M], F32, "others", "w1_bf11")
+        picked0 = [first[:]] + [others[:, t, :] for t in range(PACK - 1)]
+        for t in range(PACK):
+            nc.vector.tensor_copy(picked0[t], h0[t][:].indirect(pos_sb[:]))
+
+        w3_planes = zeroed_planes(BLOCKS * N, "w3_planes", "h00")
+        load_planes(w3_planes, w3_scales, BLOCKS)
+        w3_sb = new_tile([P, BLOCKS * N], I32, "w3_sb", "v_planes")
+        nc.sync.dma_start(
+            out=w3_sb[:].rearrange("p (b c) -> p b c", b=BLOCKS),
+            in_=w3_words.rearrange("b p c i -> p b (c i)").bitcast(I32),
+        )
+
+        h1 = first_stage(1)
+        v2_codes = [new_tile([P, M], U32, "v2_%d" % a) for a in range(PASSES2)]
+        for a in range(PASSES2):
             nc.vector.tensor_copy(v2_codes[a][:], tab2_sb[a][:].bitcast(U32).indirect(offs2_sb[:]))
-        logs(0, picked0)
-        picked1 = pick(h1, TAG1)
-        log_b0 = turn_and_log(0, project_files(0))
+
+        log_a0 = new_tile([P, PACK, M], F32, "log_a0")
+        for t in range(PACK):
+            nc.scalar.activation(out=picked0[t], in_=picked0[t], func=ACT.Square)
+            nc.scalar.activation(out=log_a0[:, t, :], in_=picked0[t], func=ACT.Ln, bias=half[:])
+
+        picked1 = new_tile([P, PACK, M], F32, "picked1", "tab_sc")
+        for t in range(PACK):
+            nc.vector.tensor_copy(picked1[:, t, :], h1[t][:].indirect(pos_sb[:]))
+
+        square_bt0 = project_files(0)
+        log_b0 = new_tile([P, PACK, M], F32, "log_b0")
+        for i in range(CHUNKS):
+            log_b_chunk(log_b0, square_bt0, i)
         square_bt1 = project_files(1)
-        log_a[1] = kept([P, M, PACK], F32, "log_a1")
-        if NV:
-            part = picked1[:, :, :NV * P]
-            nc.vector.tensor_tensor(part, part, part, ALU.mult)
-        if NV < 4:
-            part = picked1[:, :, NV * P:]
-            nc.scalar.activation(out=part, in_=part, func=ACT.Square)
-        make_z(0, log_b0, W0)
-        make_z(1, turn_and_log(1, square_bt1, picked1), P)
+        on_vector, on_scalar = picked1[:, :, :VECTOR_SQUARES * P], picked1[:, :, VECTOR_SQUARES * P:]
+        nc.vector.tensor_tensor(on_vector, on_vector, on_vector, ALU.mult)
+        nc.scalar.activation(out=on_scalar, in_=on_scalar, func=ACT.Square)
+        make_z(0, log_b0, log_a0, WIDE)
+
+        log_a1 = new_tile([P, PACK, M], F32, "log_a1")
+        log_b1 = new_tile([P, PACK, M], F32, "log_b1")
+        for i in range(CHUNKS):
+            files = slice(i * P, (i + 1) * P)
+            nc.scalar.activation(out=log_a1[:, :, files], in_=picked1[:, :, files], func=ACT.Ln, bias=half[:])
+            log_b_chunk(log_b1, square_bt1, i)
+        make_z(1, log_b1, log_a1, P)
 
         out_view = out.rearrange("(g p) m -> p g m", p=P)
-        levels = keep.tile([P, M // P, N // P, P], F32, name="levels", tag="half")
-        for i in range(M // P):
+        levels = new_tile([P, CHUNKS, N // P, P], F32, "levels", "half")
+        for i in range(CHUNKS):
             y = psum.tile([P, N // P, P], F32, name="y", tag="low%d" % i)
-            for b in range(B):
-                for g in range(N // P):
-                    nc.tensor.matmul_mx(
-                        out=y[:, g, :],
-                        lhsT=w3_sb[b][:, g * P:(g + 1) * P].bitcast(FP8X4),
-                        lhsT_scale=w3_planes[:, b * N + g * P:b * N + (g + 1) * P],
-                        rhs=z_codes[b, i].bitcast(FP8X4),
-                        rhs_scale=z_planes[b, i],
-                        start=(b == 0 and g == 0), stop=(b == B - 1 and g == N // P - 1),
-                    )
+            for blk, g in itertools.product(range(BLOCKS), range(N // P)):
+                cols = slice(blk * N + g * P, blk * N + (g + 1) * P)
+                nc.tensor.matmul_mx(
+                    out=y[:, g, :],
+                    lhsT=w3_sb[:, cols].bitcast(FP8X4),
+                    lhsT_scale=w3_planes[:, cols],
+                    rhs=z_codes[blk, i].bitcast(FP8X4),
+                    rhs_scale=z_planes[blk, i],
+                    start=(blk == 0 and g == 0), stop=(blk == BLOCKS - 1 and g == N // P - 1),
+                )
             nc.scalar.activation(out=levels[:, i], in_=y[:], func=ACT.Sigmoid)
             nc.sync.dma_start(out=out_view[:, :, i * P:(i + 1) * P], in_=levels[:, i])

@@ -69,9 +69,6 @@ def tile_list_ransomware_alarm_levels_kernel(
         for planes in (v_planes, v2_planes):
             nc.vector.memset(planes[:].bitcast(I32), 0)
 
-        warm = new_tile([P, 1], F32, "warm")
-        nc.scalar.activation(out=warm[:], in_=half[:], func=ACT.Ln)
-
         def load_w1(blk, a, after=None):
             raw = new_tile([P, PACK, PASS], F32, "w1_raw%d%d" % (blk, a), after)
             rows = w1[a * PASS:(a + 1) * PASS, blk * PASS:(blk + 1) * PASS]
@@ -91,11 +88,11 @@ def tile_list_ransomware_alarm_levels_kernel(
                     in_=scales[:, r:SCALE_ROWS:ROWS, :].bitcast(I32).rearrange("a q c -> q a c"),
                 )
 
-        def carry_planes(planes, gathered, lowest, passes):
+        def carry_planes(queue, planes, gathered, lowest, passes):
             view = planes[:].bitcast(I32).rearrange("p (a c) -> p a c", a=passes)
             for q in range(QUADS):
                 start = lowest + q * ROWS * passes
-                nc.sync.dma_start(
+                queue.dma_start(
                     out=view[q * QUAD:q * QUAD + ROWS], in_=gathered[:].bitcast(I32)[start:start + ROWS * passes]
                 )
 
@@ -138,7 +135,7 @@ def tile_list_ransomware_alarm_levels_kernel(
 
         quantise_w1(0, 0, nc.scalar.copy)
         quantise_w1(0, 1, nc.vector.tensor_copy, "tab_sc")
-        carry_planes(v_planes, v_sc, top, PASSES)
+        carry_planes(nc.scalar, v_planes, v_sc, top, PASSES)
 
         v_codes = {}
         for a, u in itertools.product(range(PASSES), range(HALVES)):
@@ -154,7 +151,7 @@ def tile_list_ransomware_alarm_levels_kernel(
         w1_raw[1, 0] = load_w1(1, 0, "w1_raw01")
         w1_raw[1, 1] = load_w1(1, 1, "tab_sc")
         tab2_sb = [load_tab2(0, "tab0")]
-        carry_planes(v2_planes, v2_sc, top2, PASSES2)
+        carry_planes(nc.sync, v2_planes, v2_sc, top2, PASSES2)
         w2_planes = zeroed_planes(PASSES2 * H, "w2_planes", "v_sc")
         load_planes(w2_planes, w2_scales, PASSES2)
         tab2_sb.append(load_tab2(1, "tab1"))
@@ -237,7 +234,9 @@ def tile_list_ransomware_alarm_levels_kernel(
         first = new_tile([P, M], F32, "first", "w1_bf10")
         others = new_tile([P, PACK - 1, M], F32, "others", "w1_bf11")
         picked0 = [first[:]] + [others[:, t, :] for t in range(PACK - 1)]
-        for t in range(PACK):
+        nc.vector.tensor_copy(picked0[0], h0[0][:].indirect(pos_sb[:]))
+        nc.vector.tensor_tensor(picked0[0], picked0[0], picked0[0], ALU.mult)
+        for t in range(1, PACK):
             nc.vector.tensor_copy(picked0[t], h0[t][:].indirect(pos_sb[:]))
 
         w3_planes = zeroed_planes(BLOCKS * N, "w3_planes", "h00")
@@ -255,7 +254,8 @@ def tile_list_ransomware_alarm_levels_kernel(
 
         log_a0 = new_tile([P, PACK, M], F32, "log_a0")
         for t in range(PACK):
-            nc.scalar.activation(out=picked0[t], in_=picked0[t], func=ACT.Square)
+            if t > 0:
+                nc.scalar.activation(out=picked0[t], in_=picked0[t], func=ACT.Square)
             nc.scalar.activation(out=log_a0[:, t, :], in_=picked0[t], func=ACT.Ln, bias=half[:])
 
         picked1 = new_tile([P, PACK, M], F32, "picked1", "tab_sc")

@@ -33,8 +33,7 @@ HALVES = S // BANK
 CHUNKS = M // P
 LINE = 4
 
-VECTOR_SQUARES = 3
-WIDE = 2 * P
+KIB = 1024
 
 
 def words_of(packed):
@@ -48,36 +47,56 @@ def tile_list_ransomware_alarm_levels_kernel(
     nc = tc.nc
     with ExitStack() as ctx:
         sbuf = ctx.enter_context(tc.tile_pool(name="sbuf", bufs=1))
+        arena = ctx.enter_context(tc.tile_pool(name="arena", bufs=1))
         psum = ctx.enter_context(tc.psum_pool(name="psum", bufs=1))
 
         def new_tile(shape, dtype, name, after=None):
             return sbuf.tile(shape, dtype, name=name, tag=after or name, align_bytes=64)
+
+        def placed(shape, dtype, name, offset):
+            return arena.tile(shape, dtype, name=name, tag=name, offset=offset, align_bytes=64)
+
+        def bank(shape, name, b):
+            return psum.tile(shape, F32, name=name, tag="bank%d" % b)
+
+        at_tab0, at_tab1 = 0, 35 * KIB // 2
+        at_raw01 = at_tab1 + 16 * KIB
+        at_tab2_sc = at_raw01
+        at_raw00 = at_raw01 + 8 * KIB
+        at_bf01 = at_raw00 + 8 * KIB
+        at_bf00 = at_bf01 + 4 * KIB
+        at_late = at_bf00 + 4 * KIB
+        at_bf11 = at_late + 5 * KIB
+        at_log_a0 = at_bf11 + (4) * KIB
+        at_h02 = at_log_a0 + 8 * KIB
+        at_w2 = [at_raw01 + 5 * KIB, at_raw01]
+        at_raw10, at_v2_planes, at_raw11 = at_tab0, at_tab0 + 8 * KIB, at_tab0 + 19 * KIB // 2
 
         offs_sb = sbuf.tile([P, S // GROUP], U16, name="offs_sb")
         pos_sb = sbuf.tile([P, M // GROUP], U16, name="pos_sb")
         offs2_sb = sbuf.tile([P, M // GROUP], U16, name="offs2_sb")
 
         tab_sc = new_tile([P, T], U8, "tab_sc")
-        tab2_sc = new_tile([P, T2], U8, "tab2_sc")
+        tab2_sc = placed([P, T2], U8, "tab2_sc", at_tab2_sc)
         v_planes = new_tile([P, PASSES * S], U8, "v_planes")
-        v2_planes = new_tile([P, PASSES2 * M], U8, "v2_planes")
         top, top2 = P - SCALE_ROWS * PASSES, P - SCALE_ROWS * PASSES2
         half = new_tile([P, 1], F32, "half")
         nc.vector.memset(half[:], 0.5)
         nc.vector.memset(tab_sc[:].bitcast(I32)[:top], 0)
         nc.vector.memset(tab2_sc[:].bitcast(I32)[:top2], 0)
-        for planes in (v_planes, v2_planes):
-            nc.vector.memset(planes[:].bitcast(I32), 0)
+        nc.vector.memset(v_planes[:].bitcast(I32), 0)
+        warm = new_tile([P, 1], F32, "warm")
+        nc.scalar.activation(out=warm[:], in_=half[:], func=ACT.Ln, bias=half[:])
 
-        def load_w1(blk, a, after=None):
-            raw = new_tile([P, PACK, PASS], F32, "w1_raw%d%d" % (blk, a), after)
+        def load_w1(blk, a, offset):
+            raw = placed([P, PACK, PASS], F32, "w1_raw%d%d" % (blk, a), offset)
             rows = w1[a * PASS:(a + 1) * PASS, blk * PASS:(blk + 1) * PASS]
             nc.sync.dma_start(out=raw[:], in_=rows.rearrange("(p j) c -> p j c", j=PACK))
             return raw
 
-        def load_tab2(a, after):
-            words = new_tile([P, T2], I32, "tab2_%d" % a, after)
-            nc.sync.dma_start(out=words[:], in_=words_of(tab2_words[a]))
+        def load_words(packed, name, offset):
+            words = placed([P, packed.shape[1]], I32, name, offset)
+            nc.sync.dma_start(out=words[:], in_=words_of(packed))
             return words
 
         def load_planes(planes, scales, passes):
@@ -90,7 +109,7 @@ def tile_list_ransomware_alarm_levels_kernel(
 
         def carry_planes(queue, planes, gathered, lowest, passes):
             view = planes[:].bitcast(I32).rearrange("p (a c) -> p a c", a=passes)
-            for q in range(QUADS):
+            for q in (0, 2, 1, 3):
                 start = lowest + q * ROWS * passes
                 queue.dma_start(
                     out=view[q * QUAD:q * QUAD + ROWS], in_=gathered[:].bitcast(I32)[start:start + ROWS * passes]
@@ -99,120 +118,158 @@ def tile_list_ransomware_alarm_levels_kernel(
         w1_raw = {}
         nc.sync.dma_start(out=tab_sc[:].bitcast(I32)[top:], in_=tab_scales.bitcast(I32).rearrange("a q c -> q a c"))
         nc.sync.dma_start(offs_sb[:], offs)
-        w1_raw[0, 0] = load_w1(0, 0)
-        nc.scalar.dma_start(
+        tab_sb = [load_words(tab_words[0], "tab0", at_tab0)]
+        nc.sync.dma_start(offs2_sb[:], offs2)
+        nc.sync.dma_start(
             out=tab2_sc[:].bitcast(I32)[top2:], in_=tab2_scales.bitcast(I32).rearrange("a q c -> q a c")
         )
-        w1_raw[0, 1] = load_w1(0, 1)
-        nc.sync.dma_start(offs2_sb[:], offs2)
         nc.sync.dma_start(pos_sb[:], pos1)
-        gain_sb = new_tile([P, BLOCKS, PACK], F32, "gain_sb")
-        nc.sync.dma_start(out=gain_sb[:], in_=gain.rearrange("(b p t) -> p b t", b=BLOCKS, t=PACK))
-        tab_sb = [new_tile([P, T], I32, "tab%d" % a) for a in range(PASSES)]
-        for a in range(PASSES):
-            for c0 in range(0, T, T // 2):
-                nc.sync.dma_start(out=tab_sb[a][:, c0:c0 + T // 2], in_=words_of(tab_words[a])[:, c0:c0 + T // 2])
+        w1_raw[0, 0] = load_w1(0, 0, at_raw00)
+        tab_sb.append(load_words(tab_words[1], "tab1", at_tab1))
 
         ident = new_tile([P, P], F32, "ident")
         make_identity(nc, ident[:])
 
         v_sc = new_tile([P, S], U8, "v_sc")
         nc.vector.tensor_copy(v_sc[:], tab_sc[:].indirect(offs_sb[:]))
+        carry_planes(nc.sync, v_planes, v_sc, top, PASSES)
         v2_sc = new_tile([P, M], U8, "v2_sc")
         nc.vector.tensor_copy(v2_sc[:], tab2_sc[:].indirect(offs2_sb[:]))
 
+        w1_raw[0, 1] = load_w1(0, 1, at_raw01)
+
+        v_codes = {}
+
+        def gather_v(a):
+            for u in range(HALVES):
+                v_codes[a, u] = new_tile([P, BANK], U32, "v%d%d" % (a, u))
+                entries = offs_sb[:, u * BANK // GROUP:(u + 1) * BANK // GROUP]
+                nc.vector.tensor_copy(v_codes[a, u][:], tab_sb[a][:].bitcast(U32).indirect(entries))
+
+        gather_v(0)
+        w1_raw[1, 0] = load_w1(1, 0, at_raw10)
+        w1_raw[1, 1] = load_w1(1, 1, at_raw11)
+        v2_planes = placed([P, PASSES2 * M], U8, "v2_planes", at_v2_planes)
+        nc.vector.memset(v2_planes[:].bitcast(I32), 0)
+        carry_planes(nc.sync, v2_planes, v2_sc, top2, PASSES2)
+        gather_v(1)
+
         w1_codes, w1_planes = {}, {}
 
-        def quantise_w1(blk, a, copy, after=None):
-            grouped = new_tile([P, PACK * PASS], BF16, "w1_bf%d%d" % (blk, a), after)
+        def quantise_w1(blk, a, copy, offset=None):
+            name = "w1_bf%d%d" % (blk, a)
+            grouped = new_tile([P, PACK * PASS], BF16, name) if offset is None else placed([P, PACK * PASS], BF16, name, offset)
             copy(
                 grouped[:].rearrange("p (u e m j) -> p u m j e", u=2, e=2, j=PACK),
                 w1_raw[blk, a][:].rearrange("p j (m u e) -> p u m j e", u=2, e=2),
             )
-            w1_codes[blk, a] = new_tile([P, PASS], U32, "w1_codes%d%d" % (blk, a))
-            w1_planes[blk, a] = new_tile([P, PASS], U8, "w1_planes%d%d" % (blk, a))
-            nc.vector.quantize_mx(out=w1_codes[blk, a][:].bitcast(FP8X4), scales=w1_planes[blk, a][:], in_=grouped[:])
+            codes = new_tile([P, PASS], U32, "w1_codes%d%d" % (blk, a))
+            planes = new_tile([P, PASS], U8, "w1_planes%d%d" % (blk, a))
+            nc.vector.quantize_mx(out=codes[:].bitcast(FP8X4), scales=planes[:], in_=grouped[:])
+            for t in range(PACK):
+                w1_codes[blk, a, t] = codes[:, t * P:(t + 1) * P]
+                w1_planes[blk, a, t] = planes[:, t * P:(t + 1) * P]
 
-        quantise_w1(0, 0, nc.scalar.copy)
-        quantise_w1(0, 1, nc.vector.tensor_copy, "tab_sc")
-        carry_planes(nc.scalar, v_planes, v_sc, top, PASSES)
+        def quantise_w1_halves(blk, a, offset):
+            pairs = w1_raw[blk, a][:].rearrange("p j (m u e) -> p u m j e", u=2, e=2)
+            grouped = [placed([P, 2 * PASS], BF16, "w1_bf%d%d%d" % (blk, a, u), offset + u * 2 * KIB) for u in range(2)]
+            for u, copy in enumerate((nc.vector.tensor_copy, nc.scalar.copy)):
+                copy(grouped[u][:].rearrange("p (e m j) -> p m j e", e=2, j=PACK), pairs[:, u])
+            for u in range(2):
+                codes = new_tile([P, 2 * P], U32, "w1_codes%d%d%d" % (blk, a, u))
+                planes = new_tile([P, 2 * P], U8, "w1_planes%d%d%d" % (blk, a, u))
+                nc.vector.quantize_mx(out=codes[:].bitcast(FP8X4), scales=planes[:], in_=grouped[u][:])
+                for e in range(2):
+                    w1_codes[blk, a, 2 * u + e] = codes[:, e * P:(e + 1) * P]
+                    w1_planes[blk, a, 2 * u + e] = planes[:, e * P:(e + 1) * P]
 
-        v_codes = {}
-        for a, u in itertools.product(range(PASSES), range(HALVES)):
-            v_codes[a, u] = new_tile([P, BANK], U32, "v%d%d" % (a, u))
-            entries = offs_sb[:, u * BANK // GROUP:(u + 1) * BANK // GROUP]
-            nc.vector.tensor_copy(v_codes[a, u][:], tab_sb[a][:].bitcast(U32).indirect(entries))
-
-        def zeroed_planes(width, name, after):
-            planes = new_tile([P, width], U8, name, after)
-            nc.gpsimd.memset(planes[:].bitcast(I32), 0)
-            return planes
-
-        w1_raw[1, 0] = load_w1(1, 0, "w1_raw01")
-        w1_raw[1, 1] = load_w1(1, 1, "tab_sc")
-        tab2_sb = [load_tab2(0, "tab0")]
-        carry_planes(nc.sync, v2_planes, v2_sc, top2, PASSES2)
-        w2_planes = zeroed_planes(PASSES2 * H, "w2_planes", "v_sc")
+        quantise_w1(0, 0, nc.scalar.copy, at_bf00)
+        tab2_sb = [load_words(tab2_words[0], "tab2_0", at_raw00)]
+        w2_planes = placed([P, PASSES2 * H], U8, "w2_planes", at_bf00)
+        nc.gpsimd.memset(w2_planes[:].bitcast(I32), 0)
         load_planes(w2_planes, w2_scales, PASSES2)
-        tab2_sb.append(load_tab2(1, "tab1"))
-        w2_sb = new_tile([P, PASSES2 * 2 * H], U8, "w2_sb", "w1_raw01")
-        nc.sync.dma_start(
-            out=w2_sb[:].bitcast(I32).rearrange("p (a c) -> p a c", a=PASSES2),
-            in_=w2_words.bitcast(I32).rearrange("a p c -> p a c"),
-        )
-        tab2_sb.append(load_tab2(2, "tab_sc"))
+        for a in range(1, PASSES2):
+            tab2_sb.append(load_words(tab2_words[a], "tab2_%d" % a, at_tab1 + (a - 1) * 8 * KIB))
+        quantise_w1_halves(0, 1, at_bf01)
+        w2_sb = []
+        for blk in range(BLOCKS):
+            w2_sb.append(placed([P, PASSES2 * 2 * PASS], U8, "w2_sb%d" % blk, at_w2[blk]))
+            nc.sync.dma_start(
+                out=w2_sb[blk][:].bitcast(I32).rearrange("p (a c) -> p a c", a=PASSES2),
+                in_=w2_words[:, :, 2 * blk * PASS:2 * (blk + 1) * PASS].bitcast(I32).rearrange("a p c -> p a c"),
+            )
+        gain_sb = placed([P, BLOCKS, PACK], F32, "gain_sb", at_raw01 + 3 * KIB)
+        nc.sync.dma_start(out=gain_sb[:], in_=gain.rearrange("(b p t) -> p b t", b=BLOCKS, t=PACK))
 
-        def first_stage(blk):
-            h = [new_tile([P, S], F32, "h%d%d" % (blk, t)) for t in range(PACK)]
-            for t0 in range(0, PACK, 2):
-                for u, e in itertools.product(range(HALVES), range(2)):
-                    cols = slice((t0 + e) * P, (t0 + e + 1) * P)
-                    acc = psum.tile([P, BANK], F32, name="acc", tag="low%d" % (2 * u + e))
-                    for a in range(PASSES):
-                        nc.tensor.matmul_mx(
-                            out=acc[:],
-                            lhsT=w1_codes[blk, a][:, cols].bitcast(FP8X4),
-                            lhsT_scale=w1_planes[blk, a][:, cols],
-                            rhs=v_codes[a, u][:].bitcast(FP8X4),
-                            rhs_scale=v_planes[:, a * S + u * BANK:a * S + (u + 1) * BANK],
-                            start=(a == 0), stop=(a == PASSES - 1),
-                        )
-                    nc.scalar.copy(h[t0 + e][:, u * BANK:(u + 1) * BANK], acc[:])
+        def first_stage(blk, on_vector):
+            h = [
+                placed([P, S], F32, "h02", at_h02) if (blk, t) == (0, 2) else new_tile([P, S], F32, "h%d%d" % (blk, t))
+                for t in range(PACK)
+            ]
+            acc = {}
+            for t, u, a in itertools.product(range(PACK), range(HALVES), range(PASSES)):
+                if a == 0:
+                    acc[t, u] = bank([P, BANK], "acc", HALVES * t + u)
+                nc.tensor.matmul_mx(
+                    out=acc[t, u][:],
+                    lhsT=w1_codes[blk, a, t].bitcast(FP8X4),
+                    lhsT_scale=w1_planes[blk, a, t],
+                    rhs=v_codes[a, u][:].bitcast(FP8X4),
+                    rhs_scale=v_planes[:, a * S + u * BANK:a * S + (u + 1) * BANK],
+                    start=(a == 0), stop=(a == PASSES - 1),
+                )
+                if a == PASSES - 1:
+                    copy = nc.vector.tensor_copy if (t, u) in on_vector else nc.scalar.copy
+                    copy(h[t][:, u * BANK:(u + 1) * BANK], acc[t, u][:])
             return h
 
-        def project_files(blk):
-            square_bt = new_tile([P, CHUNKS, PACK, P], F32, "square_bt%d" % blk)
+        def pick(picked, h, t):
+            nc.vector.tensor_copy(picked[:, t, :], h[t][:].indirect(pos_sb[:]))
+
+        def square(engine, squared, values):
+            if engine == "s":
+                nc.scalar.activation(out=squared, in_=values, func=ACT.Square)
+            elif engine == "v":
+                nc.vector.tensor_tensor(squared, values, values, ALU.mult)
+            else:
+                nc.gpsimd.tensor_tensor(squared, values, values, ALU.mult)
+
+        def project_files(blk, before=None):
+            log_bt = new_tile([P, CHUNKS, PACK, P], F32, "log_bt%d" % blk)
+            log_b = []
             for i in range(CHUNKS):
-                bt = psum.tile([P, BANK], F32, name="bt", tag="low%d" % i)
+                if before:
+                    before(i)
+                bt = bank([P, BANK], "bt", i)
                 for a in range(PASSES2):
                     c0 = a * H + blk * PASS
                     nc.tensor.matmul_mx(
                         out=bt[:],
                         lhsT=v2_codes[a][:, i * P:(i + 1) * P].bitcast(FP8X4),
                         lhsT_scale=v2_planes[:, a * M + i * P:a * M + (i + 1) * P],
-                        rhs=w2_sb[:, 2 * c0:2 * (c0 + PASS)].bitcast(FP4X4),
+                        rhs=w2_sb[blk][:, 2 * a * PASS:2 * (a + 1) * PASS].bitcast(FP4X4),
                         rhs_scale=w2_planes[:, c0:c0 + PASS],
                         start=(a == 0), stop=(a == PASSES2 - 1),
                     )
                 nc.scalar.activation(
-                    out=square_bt[:, i].rearrange("m (u e) p -> m u p e", u=2),
+                    out=log_bt[:, i].rearrange("m (u e) p -> m u p e", u=2),
                     in_=bt[:].rearrange("m (p u e) -> m u p e", u=2, e=2),
                     func=ACT.Square,
                 )
-            return square_bt
-
-        def log_b_chunk(log_b, square_bt, i):
-            square_b = psum.tile([P, PACK, P], F32, name="square_b", tag="high%d" % i)
-            for t in range(PACK):
-                nc.tensor.transpose(square_b[:, t, :], square_bt[:, i, t, :], ident[:])
-            nc.scalar.activation(out=log_b[:, :, i * P:(i + 1) * P], in_=square_b[:], func=ACT.Ln, bias=half[:])
+                nc.scalar.activation(out=log_bt[:, i], in_=log_bt[:, i], func=ACT.Ln, bias=half[:])
+            return log_bt
 
         z_codes, z_planes = {}, {}
 
-        def make_z(blk, log_b, log_a, width):
+        def make_z(blk, log_bt, picked, width):
             for m0 in range(0, M, width):
-                diff = log_b[:, :, m0:m0 + width]
-                nc.vector.tensor_tensor(diff, diff, log_a[:, :, m0:m0 + width], ALU.subtract)
+                for i in range(m0 // P, (m0 + width) // P):
+                    log_b = bank([P, PACK, P], "log_b", CHUNKS + i)
+                    for t in range(PACK):
+                        nc.tensor.transpose(log_b[:, t, :], log_bt[:, i, t, :], ident[:])
+                    chunk = picked[:, :, i * P:(i + 1) * P]
+                    nc.vector.tensor_tensor(chunk, log_b[:], chunk, ALU.subtract)
+                diff = picked[:, :, m0:m0 + width]
                 z = sbuf.tile([P, PACK * width], BF16, name="z", tag="z", align_bytes=64, bufs=3)
                 nc.vector.tensor_tensor(
                     z[:].rearrange("p (c e t) -> p c t e", e=LINE, t=PACK),
@@ -227,63 +284,55 @@ def tile_list_ransomware_alarm_levels_kernel(
                     z_codes[blk, (m0 + c0) // P] = codes[:, c0:c0 + P]
                     z_planes[blk, (m0 + c0) // P] = plane[:, c0:c0 + P]
 
-        h0 = first_stage(0)
-        for a in range(PASSES):
-            quantise_w1(1, a, nc.vector.tensor_copy)
-
-        first = new_tile([P, M], F32, "first", "w1_bf10")
-        others = new_tile([P, PACK - 1, M], F32, "others", "w1_bf11")
-        picked0 = [first[:]] + [others[:, t, :] for t in range(PACK - 1)]
-        nc.vector.tensor_copy(picked0[0], h0[0][:].indirect(pos_sb[:]))
-        nc.vector.tensor_tensor(picked0[0], picked0[0], picked0[0], ALU.mult)
-        for t in range(1, PACK):
-            nc.vector.tensor_copy(picked0[t], h0[t][:].indirect(pos_sb[:]))
-
-        w3_planes = zeroed_planes(BLOCKS * N, "w3_planes", "h00")
-        load_planes(w3_planes, w3_scales, BLOCKS)
-        w3_sb = new_tile([P, BLOCKS * N], I32, "w3_sb", "v_planes")
+        h0 = first_stage(0, [])
+        early = new_tile([P, 1, M], F32, "early")
+        for t in range(1):
+            pick(early, h0, t)
+        quantise_w1(1, 0, nc.vector.tensor_copy)
+        quantise_w1(1, 1, nc.vector.tensor_copy, at_bf11)
+        w3_sb = placed([P, BLOCKS * N], I32, "w3_sb", at_raw11)
         nc.sync.dma_start(
             out=w3_sb[:].rearrange("p (b c) -> p b c", b=BLOCKS),
             in_=w3_words.rearrange("b p c i -> p b (c i)").bitcast(I32),
         )
+        w3_planes = placed([P, BLOCKS * N], U8, "w3_planes", at_raw11 + 4 * KIB)
+        nc.vector.memset(w3_planes[:].bitcast(I32), 0)
+        load_planes(w3_planes, w3_scales, BLOCKS)
+        late = placed([P, PACK - 1, M], F32, "late", at_bf11 + KIB - (PACK - 1) * 2 * KIB)
+        for t in range(1, PACK):
+            nc.vector.tensor_copy(late[:, t - 1, :], h0[t][:].indirect(pos_sb[:]))
 
-        h1 = first_stage(1)
+        h1 = first_stage(1, [])
+        picked0 = placed([P, PACK, M], F32, "log_a0", at_log_a0)
+        for t in range(PACK):
+            row = early[:, t, :] if t < 1 else late[:, t - 1, :]
+            square("ssss"[t], picked0[:, t, :], row)
+            nc.scalar.activation(out=picked0[:, t, :], in_=picked0[:, t, :], func=ACT.Ln, bias=half[:])
         v2_codes = [new_tile([P, M], U32, "v2_%d" % a) for a in range(PASSES2)]
         for a in range(PASSES2):
             nc.vector.tensor_copy(v2_codes[a][:], tab2_sb[a][:].bitcast(U32).indirect(offs2_sb[:]))
 
-        log_a0 = new_tile([P, PACK, M], F32, "log_a0")
+        log_bt0 = project_files(0)
+        picked1 = placed([P, PACK, M], F32, "picked1", at_tab1 + 8 * KIB)
+        log_a1 = placed([P, PACK, M], F32, "log_a1", at_w2[0])
         for t in range(PACK):
-            if t > 0:
-                nc.scalar.activation(out=picked0[t], in_=picked0[t], func=ACT.Square)
-            nc.scalar.activation(out=log_a0[:, t, :], in_=picked0[t], func=ACT.Ln, bias=half[:])
+            pick(picked1, h1, t)
 
-        picked1 = new_tile([P, PACK, M], F32, "picked1", "tab_sc")
-        for t in range(PACK):
-            nc.vector.tensor_copy(picked1[:, t, :], h1[t][:].indirect(pos_sb[:]))
-
-        square_bt0 = project_files(0)
-        log_b0 = new_tile([P, PACK, M], F32, "log_b0")
-        for i in range(CHUNKS):
-            log_b_chunk(log_b0, square_bt0, i)
-        square_bt1 = project_files(1)
-        on_vector, on_scalar = picked1[:, :, :VECTOR_SQUARES * P], picked1[:, :, VECTOR_SQUARES * P:]
-        nc.vector.tensor_tensor(on_vector, on_vector, on_vector, ALU.mult)
-        nc.scalar.activation(out=on_scalar, in_=on_scalar, func=ACT.Square)
-        make_z(0, log_b0, log_a0, WIDE)
-
-        log_a1 = new_tile([P, PACK, M], F32, "log_a1")
-        log_b1 = new_tile([P, PACK, M], F32, "log_b1")
-        for i in range(CHUNKS):
+        def log_a1_chunk(i):
             files = slice(i * P, (i + 1) * P)
-            nc.scalar.activation(out=log_a1[:, :, files], in_=picked1[:, :, files], func=ACT.Ln, bias=half[:])
-            log_b_chunk(log_b1, square_bt1, i)
-        make_z(1, log_b1, log_a1, P)
+            square("vvss"[i], log_a1[:, :, files], picked1[:, :, files])
+            nc.scalar.activation(out=log_a1[:, :, files], in_=log_a1[:, :, files], func=ACT.Ln, bias=half[:])
+
+        make_z(0, log_bt0, picked0, 2 * P)
+        log_bt1 = project_files(1)
+        for i in range(CHUNKS):
+            log_a1_chunk(i)
+        make_z(1, log_bt1, log_a1, P)
 
         out_view = out.rearrange("(g p) m -> p g m", p=P)
         levels = new_tile([P, CHUNKS, N // P, P], F32, "levels", "half")
         for i in range(CHUNKS):
-            y = psum.tile([P, N // P, P], F32, name="y", tag="low%d" % i)
+            y = bank([P, N // P, P], "y", i)
             for blk, g in itertools.product(range(BLOCKS), range(N // P)):
                 cols = slice(blk * N + g * P, blk * N + (g + 1) * P)
                 nc.tensor.matmul_mx(

@@ -53,31 +53,31 @@ def tile_list_ransomware_alarm_levels_kernel(
         def new_tile(shape, dtype, name, after=None):
             return sbuf.tile(shape, dtype, name=name, tag=after or name, align_bytes=64)
 
-        def placed(shape, dtype, name, offset):
-            return arena.tile(shape, dtype, name=name, tag=name, offset=offset, align_bytes=64)
+        def placed(shape, dtype, name, kib):
+            return arena.tile(shape, dtype, name=name, tag=name, offset=kib * KIB, align_bytes=64)
 
         def bank(shape, name, b):
             return psum.tile(shape, F32, name=name, tag="bank%d" % b)
 
-        at_tab0, at_tab1 = 0, 35 * KIB // 2
-        at_raw01 = at_tab1 + 16 * KIB
-        at_tab2_sc = at_raw01
-        at_raw00 = at_raw01 + 8 * KIB
-        at_bf01 = at_raw00 + 8 * KIB
-        at_bf00 = at_bf01 + 4 * KIB
-        at_late = at_bf00 + 4 * KIB
-        at_bf11 = at_late + 5 * KIB
-        at_log_a0 = at_bf11 + (4) * KIB
-        at_h02 = at_log_a0 + 8 * KIB
-        at_w2 = [at_raw01 + 5 * KIB, at_raw01]
-        at_raw10, at_v2_planes, at_raw11 = at_tab0, at_tab0 + 8 * KIB, at_tab0 + 19 * KIB // 2
+        at_tab0, at_raw10, at_v2_planes, at_raw11 = 0, 0, 8, 10
+        at_tab1 = 18
+        at_raw01 = 34
+        at_raw00 = 42
+        at_bf01 = 50
+        at_bf00 = 54
+        at_early = 58
+        at_bf10 = at_early + 4 - 1
+        at_bf11 = at_bf10 + 1
+        at_late = at_bf11 + 3
+        at_h11 = at_late + 8
+        at_diff0 = at_h11 + 4
 
         offs_sb = sbuf.tile([P, S // GROUP], U16, name="offs_sb")
         pos_sb = sbuf.tile([P, M // GROUP], U16, name="pos_sb")
         offs2_sb = sbuf.tile([P, M // GROUP], U16, name="offs2_sb")
 
         tab_sc = new_tile([P, T], U8, "tab_sc")
-        tab2_sc = placed([P, T2], U8, "tab2_sc", at_tab2_sc)
+        tab2_sc = placed([P, T2], U8, "tab2_sc", at_raw01)
         v_planes = new_tile([P, PASSES * S], U8, "v_planes")
         top, top2 = P - SCALE_ROWS * PASSES, P - SCALE_ROWS * PASSES2
         half = new_tile([P, 1], F32, "half")
@@ -88,14 +88,14 @@ def tile_list_ransomware_alarm_levels_kernel(
         warm = new_tile([P, 1], F32, "warm")
         nc.scalar.activation(out=warm[:], in_=half[:], func=ACT.Ln, bias=half[:])
 
-        def load_w1(blk, a, offset):
-            raw = placed([P, PACK, PASS], F32, "w1_raw%d%d" % (blk, a), offset)
+        def load_w1(blk, a, kib):
+            raw = placed([P, PACK, PASS], F32, "w1_raw%d%d" % (blk, a), kib)
             rows = w1[a * PASS:(a + 1) * PASS, blk * PASS:(blk + 1) * PASS]
             nc.sync.dma_start(out=raw[:], in_=rows.rearrange("(p j) c -> p j c", j=PACK))
             return raw
 
-        def load_words(packed, name, offset):
-            words = placed([P, packed.shape[1]], I32, name, offset)
+        def load_words(packed, name, kib):
+            words = placed([P, packed.shape[1]], I32, name, kib)
             nc.sync.dma_start(out=words[:], in_=words_of(packed))
             return words
 
@@ -107,11 +107,11 @@ def tile_list_ransomware_alarm_levels_kernel(
                     in_=scales[:, r:SCALE_ROWS:ROWS, :].bitcast(I32).rearrange("a q c -> q a c"),
                 )
 
-        def carry_planes(queue, planes, gathered, lowest, passes):
+        def carry_planes(planes, gathered, lowest, passes):
             view = planes[:].bitcast(I32).rearrange("p (a c) -> p a c", a=passes)
             for q in (0, 2, 1, 3):
                 start = lowest + q * ROWS * passes
-                queue.dma_start(
+                nc.sync.dma_start(
                     out=view[q * QUAD:q * QUAD + ROWS], in_=gathered[:].bitcast(I32)[start:start + ROWS * passes]
                 )
 
@@ -132,10 +132,9 @@ def tile_list_ransomware_alarm_levels_kernel(
 
         v_sc = new_tile([P, S], U8, "v_sc")
         nc.vector.tensor_copy(v_sc[:], tab_sc[:].indirect(offs_sb[:]))
-        carry_planes(nc.sync, v_planes, v_sc, top, PASSES)
+        carry_planes(v_planes, v_sc, top, PASSES)
         v2_sc = new_tile([P, M], U8, "v2_sc")
         nc.vector.tensor_copy(v2_sc[:], tab2_sc[:].indirect(offs2_sb[:]))
-
         w1_raw[0, 1] = load_w1(0, 1, at_raw01)
 
         v_codes = {}
@@ -151,61 +150,64 @@ def tile_list_ransomware_alarm_levels_kernel(
         w1_raw[1, 1] = load_w1(1, 1, at_raw11)
         v2_planes = placed([P, PASSES2 * M], U8, "v2_planes", at_v2_planes)
         nc.vector.memset(v2_planes[:].bitcast(I32), 0)
-        carry_planes(nc.sync, v2_planes, v2_sc, top2, PASSES2)
+        carry_planes(v2_planes, v2_sc, top2, PASSES2)
         gather_v(1)
 
         w1_codes, w1_planes = {}, {}
 
-        def quantise_w1(blk, a, copy, offset=None):
-            name = "w1_bf%d%d" % (blk, a)
-            grouped = new_tile([P, PACK * PASS], BF16, name) if offset is None else placed([P, PACK * PASS], BF16, name, offset)
-            copy(
-                grouped[:].rearrange("p (u e m j) -> p u m j e", u=2, e=2, j=PACK),
-                w1_raw[blk, a][:].rearrange("p j (m u e) -> p u m j e", u=2, e=2),
+        def by_pairs(raw):
+            return raw[:].rearrange("p j (m u e) -> p u m j e", u=2, e=2)
+
+        def round_by_pairs(copy):
+            return lambda grouped, raw: copy(
+                grouped[:].rearrange("p (u e m j) -> p u m j e", u=2, e=2, j=PACK), by_pairs(raw)
             )
-            codes = new_tile([P, PASS], U32, "w1_codes%d%d" % (blk, a))
-            planes = new_tile([P, PASS], U8, "w1_planes%d%d" % (blk, a))
+
+        def round_on_gpsimd(grouped, raw):
+            nc.gpsimd.tensor_scalar(
+                grouped[:].rearrange("p (t m j) -> p t m j", t=PACK, j=PACK),
+                raw[:].rearrange("p j (m t) -> p t m j", t=PACK),
+                1.0, 0.0, ALU.mult, ALU.add,
+            )
+
+        def quantise_rounded(blk, a, t0, grouped, sets):
+            codes = new_tile([P, sets * P], U32, "w1_codes%d%d%d" % (blk, a, t0))
+            planes = new_tile([P, sets * P], U8, "w1_planes%d%d%d" % (blk, a, t0))
             nc.vector.quantize_mx(out=codes[:].bitcast(FP8X4), scales=planes[:], in_=grouped[:])
-            for t in range(PACK):
-                w1_codes[blk, a, t] = codes[:, t * P:(t + 1) * P]
-                w1_planes[blk, a, t] = planes[:, t * P:(t + 1) * P]
+            for e in range(sets):
+                w1_codes[blk, a, t0 + e] = codes[:, e * P:(e + 1) * P]
+                w1_planes[blk, a, t0 + e] = planes[:, e * P:(e + 1) * P]
 
-        def quantise_w1_halves(blk, a, offset):
-            pairs = w1_raw[blk, a][:].rearrange("p j (m u e) -> p u m j e", u=2, e=2)
-            grouped = [placed([P, 2 * PASS], BF16, "w1_bf%d%d%d" % (blk, a, u), offset + u * 2 * KIB) for u in range(2)]
+        def quantise_w1(blk, a, rounding, kib):
+            grouped = placed([P, PACK * PASS], BF16, "w1_bf%d%d" % (blk, a), kib)
+            rounding(grouped, w1_raw[blk, a])
+            quantise_rounded(blk, a, 0, grouped, PACK)
+
+        def quantise_w1_halves(blk, a, kib):
+            grouped = [placed([P, 2 * PASS], BF16, "w1_bf%d%d%d" % (blk, a, u), kib + 2 * u) for u in range(2)]
             for u, copy in enumerate((nc.vector.tensor_copy, nc.scalar.copy)):
-                copy(grouped[u][:].rearrange("p (e m j) -> p m j e", e=2, j=PACK), pairs[:, u])
+                copy(grouped[u][:].rearrange("p (e m j) -> p m j e", e=2, j=PACK), by_pairs(w1_raw[blk, a])[:, u])
             for u in range(2):
-                codes = new_tile([P, 2 * P], U32, "w1_codes%d%d%d" % (blk, a, u))
-                planes = new_tile([P, 2 * P], U8, "w1_planes%d%d%d" % (blk, a, u))
-                nc.vector.quantize_mx(out=codes[:].bitcast(FP8X4), scales=planes[:], in_=grouped[u][:])
-                for e in range(2):
-                    w1_codes[blk, a, 2 * u + e] = codes[:, e * P:(e + 1) * P]
-                    w1_planes[blk, a, 2 * u + e] = planes[:, e * P:(e + 1) * P]
+                quantise_rounded(blk, a, 2 * u, grouped[u], 2)
 
-        quantise_w1(0, 0, nc.scalar.copy, at_bf00)
+        quantise_w1(0, 0, round_by_pairs(nc.scalar.copy), at_bf00)
         tab2_sb = [load_words(tab2_words[0], "tab2_0", at_raw00)]
         w2_planes = placed([P, PASSES2 * H], U8, "w2_planes", at_bf00)
         nc.gpsimd.memset(w2_planes[:].bitcast(I32), 0)
         load_planes(w2_planes, w2_scales, PASSES2)
-        for a in range(1, PASSES2):
-            tab2_sb.append(load_words(tab2_words[a], "tab2_%d" % a, at_tab1 + (a - 1) * 8 * KIB))
+        tab2_sb.append(load_words(tab2_words[1], "tab2_1", at_tab1))
         quantise_w1_halves(0, 1, at_bf01)
-        w2_sb = []
-        for blk in range(BLOCKS):
-            w2_sb.append(placed([P, PASSES2 * 2 * PASS], U8, "w2_sb%d" % blk, at_w2[blk]))
+        def load_w2(blk, kib):
+            words = placed([P, PASSES2 * 2 * PASS], U8, "w2_sb%d" % blk, kib)
             nc.sync.dma_start(
-                out=w2_sb[blk][:].bitcast(I32).rearrange("p (a c) -> p a c", a=PASSES2),
+                out=words[:].bitcast(I32).rearrange("p (a c) -> p a c", a=PASSES2),
                 in_=w2_words[:, :, 2 * blk * PASS:2 * (blk + 1) * PASS].bitcast(I32).rearrange("a p c -> p a c"),
             )
-        gain_sb = placed([P, BLOCKS, PACK], F32, "gain_sb", at_raw01 + 3 * KIB)
-        nc.sync.dma_start(out=gain_sb[:], in_=gain.rearrange("(b p t) -> p b t", b=BLOCKS, t=PACK))
+            return words
 
-        def first_stage(blk, on_vector):
-            h = [
-                placed([P, S], F32, "h02", at_h02) if (blk, t) == (0, 2) else new_tile([P, S], F32, "h%d%d" % (blk, t))
-                for t in range(PACK)
-            ]
+        w2_sb = [load_w2(0, at_raw01)]
+
+        def first_stage(blk, h, on_vector):
             acc = {}
             for t, u, a in itertools.product(range(PACK), range(HALVES), range(PASSES)):
                 if a == 0:
@@ -221,10 +223,9 @@ def tile_list_ransomware_alarm_levels_kernel(
                 if a == PASSES - 1:
                     copy = nc.vector.tensor_copy if (t, u) in on_vector else nc.scalar.copy
                     copy(h[t][:, u * BANK:(u + 1) * BANK], acc[t, u][:])
-            return h
 
-        def pick(picked, h, t):
-            nc.vector.tensor_copy(picked[:, t, :], h[t][:].indirect(pos_sb[:]))
+        def pick(row, h):
+            nc.vector.tensor_copy(row, h[:].indirect(pos_sb[:]))
 
         def square(engine, squared, values):
             if engine == "s":
@@ -234,114 +235,159 @@ def tile_list_ransomware_alarm_levels_kernel(
             else:
                 nc.gpsimd.tensor_tensor(squared, values, values, ALU.mult)
 
-        def project_files(blk, before=None):
-            log_bt = new_tile([P, CHUNKS, PACK, P], F32, "log_bt%d" % blk)
-            log_b = []
-            for i in range(CHUNKS):
-                if before:
-                    before(i)
-                bt = bank([P, BANK], "bt", i)
-                for a in range(PASSES2):
-                    c0 = a * H + blk * PASS
-                    nc.tensor.matmul_mx(
-                        out=bt[:],
-                        lhsT=v2_codes[a][:, i * P:(i + 1) * P].bitcast(FP8X4),
-                        lhsT_scale=v2_planes[:, a * M + i * P:a * M + (i + 1) * P],
-                        rhs=w2_sb[blk][:, 2 * a * PASS:2 * (a + 1) * PASS].bitcast(FP4X4),
-                        rhs_scale=w2_planes[:, c0:c0 + PASS],
-                        start=(a == 0), stop=(a == PASSES2 - 1),
-                    )
-                nc.scalar.activation(
-                    out=log_bt[:, i].rearrange("m (u e) p -> m u p e", u=2),
-                    in_=bt[:].rearrange("m (p u e) -> m u p e", u=2, e=2),
-                    func=ACT.Square,
-                )
-                nc.scalar.activation(out=log_bt[:, i], in_=log_bt[:, i], func=ACT.Ln, bias=half[:])
-            return log_bt
+        def log_of(logs, squared):
+            nc.scalar.activation(out=logs, in_=squared, func=ACT.Ln, bias=half[:])
+
+        def gather_v2(a, codes):
+            nc.vector.tensor_copy(codes[:], tab2_sb[a][:].bitcast(U32).indirect(offs2_sb[:]))
+            return codes
+
+        def project(blk, i, a, bt):
+            c0 = a * H + blk * PASS
+            nc.tensor.matmul_mx(
+                out=bt[:],
+                lhsT=v2_codes[a][:, i * P:(i + 1) * P].bitcast(FP8X4),
+                lhsT_scale=v2_planes[:, a * M + i * P:a * M + (i + 1) * P],
+                rhs=w2_sb[blk][:, 2 * a * PASS:2 * (a + 1) * PASS].bitcast(FP4X4),
+                rhs_scale=w2_planes[:, c0:c0 + PASS],
+                start=(a == 0), stop=(a == PASSES2 - 1),
+            )
+
+        def log_b_turned(log_bt, bt, squared=None):
+            squared = log_bt if squared is None else squared
+            nc.scalar.activation(
+                out=squared.rearrange("m (u e p) -> m u p e", u=2, e=2),
+                in_=bt[:].rearrange("m (p u e) -> m u p e", u=2, e=2),
+                func=ACT.Square,
+            )
+            log_of(log_bt, squared)
+
+        def subtract(log_bt, log_a, i, b, diff=None):
+            log_b = bank([P, PACK, P], "log_b", b)
+            for t in range(PACK):
+                nc.tensor.transpose(log_b[:, t, :], log_bt[:, t * P:(t + 1) * P], ident[:])
+            chunk = log_a[:, :, i * P:(i + 1) * P]
+            nc.vector.tensor_tensor(chunk if diff is None else diff, log_b[:], chunk, ALU.subtract)
+
+        def apply_gain(blk, diff, m0, width):
+            z = new_tile([P, PACK * width], BF16, "z%d_%d" % (blk, m0))
+            nc.vector.tensor_tensor(
+                z[:].rearrange("p (c e t) -> p c t e", e=LINE, t=PACK),
+                diff.rearrange("p t (c e) -> p c t e", e=LINE),
+                gain_sb[:, blk, :].unsqueeze(1).unsqueeze(3).to_broadcast([P, width // LINE, PACK, LINE]),
+                ALU.mult,
+            )
+            return blk, z, m0, width
 
         z_codes, z_planes = {}, {}
 
-        def make_z(blk, log_bt, picked, width):
-            for m0 in range(0, M, width):
-                for i in range(m0 // P, (m0 + width) // P):
-                    log_b = bank([P, PACK, P], "log_b", CHUNKS + i)
-                    for t in range(PACK):
-                        nc.tensor.transpose(log_b[:, t, :], log_bt[:, i, t, :], ident[:])
-                    chunk = picked[:, :, i * P:(i + 1) * P]
-                    nc.vector.tensor_tensor(chunk, log_b[:], chunk, ALU.subtract)
-                diff = picked[:, :, m0:m0 + width]
-                z = sbuf.tile([P, PACK * width], BF16, name="z", tag="z", align_bytes=64, bufs=3)
-                nc.vector.tensor_tensor(
-                    z[:].rearrange("p (c e t) -> p c t e", e=LINE, t=PACK),
-                    diff.rearrange("p t (c e) -> p c t e", e=LINE),
-                    gain_sb[:, blk, :].unsqueeze(1).unsqueeze(3).to_broadcast([P, width // LINE, PACK, LINE]),
-                    ALU.mult,
-                )
-                codes = new_tile([P, width], U32, "z_codes%d_%d" % (blk, m0))
-                plane = new_tile([P, width], U8, "z_planes%d_%d" % (blk, m0))
-                nc.vector.quantize_mx(out=codes[:].bitcast(FP8X4), scales=plane[:], in_=z[:])
-                for c0 in range(0, width, P):
-                    z_codes[blk, (m0 + c0) // P] = codes[:, c0:c0 + P]
-                    z_planes[blk, (m0 + c0) // P] = plane[:, c0:c0 + P]
+        def quantise_z(blk, z, m0, width):
+            codes = new_tile([P, width], U32, "z_codes%d_%d" % (blk, m0))
+            plane = new_tile([P, width], U8, "z_planes%d_%d" % (blk, m0))
+            nc.vector.quantize_mx(out=codes[:].bitcast(FP8X4), scales=plane[:], in_=z[:])
+            for c0 in range(0, width, P):
+                z_codes[blk, (m0 + c0) // P] = codes[:, c0:c0 + P]
+                z_planes[blk, (m0 + c0) // P] = plane[:, c0:c0 + P]
 
-        h0 = first_stage(0, [])
-        early = new_tile([P, 1, M], F32, "early")
-        for t in range(1):
-            pick(early, h0, t)
-        quantise_w1(1, 0, nc.vector.tensor_copy)
-        quantise_w1(1, 1, nc.vector.tensor_copy, at_bf11)
+        h0 = [new_tile([P, S], F32, "h0%d" % t) for t in range(PACK)]
+        first_stage(0, h0, [])
+        quantise_w1(1, 0, round_by_pairs(nc.vector.tensor_copy), at_bf10)
+        tab2_sb.append(load_words(tab2_words[2], "tab2_2", at_raw10))
+        early = placed([P, 2, M], F32, "early", at_early)
+        for t in range(2):
+            pick(early[:, t, :], h0[t])
+        quantise_w1(1, 1, round_on_gpsimd, at_bf11)
+        w2_sb.append(load_w2(1, at_raw11 + 5))
         w3_sb = placed([P, BLOCKS * N], I32, "w3_sb", at_raw11)
         nc.sync.dma_start(
             out=w3_sb[:].rearrange("p (b c) -> p b c", b=BLOCKS),
             in_=w3_words.rearrange("b p c i -> p b (c i)").bitcast(I32),
         )
-        w3_planes = placed([P, BLOCKS * N], U8, "w3_planes", at_raw11 + 4 * KIB)
+        gain_sb = placed([P, BLOCKS, PACK], F32, "gain_sb", at_bf11)
+        nc.sync.dma_start(out=gain_sb[:], in_=gain.rearrange("(b p t) -> p b t", b=BLOCKS, t=PACK))
+        w3_planes = placed([P, BLOCKS * N], U8, "w3_planes", at_raw11 + 4)
         nc.vector.memset(w3_planes[:].bitcast(I32), 0)
         load_planes(w3_planes, w3_scales, BLOCKS)
-        late = placed([P, PACK - 1, M], F32, "late", at_bf11 + KIB - (PACK - 1) * 2 * KIB)
+        late = placed([P, PACK - 2, M], F32, "late", at_late)
+        for t in range(2, PACK):
+            pick(late[:, t - 2, :], h0[t])
+
+        h1 = [
+            placed([P, S], F32, "h1%d" % t, at_h11) if t == 1 - 1 else new_tile([P, S], F32, "h1%d" % t)
+            for t in range(PACK)
+        ]
+        first_stage(1, h1, [])
+        log_a0 = new_tile([P, PACK, M], F32, "log_a0")
+        for t in range(PACK):
+            row = early[:, t, :] if t < 2 else late[:, t - 2, :]
+            square("ssgg"[t], log_a0[:, t, :], row)
+            log_of(log_a0[:, t, :], log_a0[:, t, :])
+        v2_codes = [gather_v2(0, placed([P, M], U32, "v2_0", at_bf11 + 1)), gather_v2(1, new_tile([P, M], U32, "v2_1"))]
+
+        log_a1 = new_tile([P, PACK, M], F32, "log_a1")
+        before = new_tile([P, 1, M], F32, "before")
+        for t in range(1):
+            pick(before[:, t, :], h1[t])
+            square("sggg"[t], log_a1[:, t, :], before[:, t, :])
+            log_of(log_a1[:, t, :], log_a1[:, t, :])
+        v2_codes.append(gather_v2(2, placed([P, M], U32, "v2_2", at_h11)))
+        after = placed([P, PACK - 1, M], F32, "after", at_raw10)
         for t in range(1, PACK):
-            nc.vector.tensor_copy(late[:, t - 1, :], h0[t][:].indirect(pos_sb[:]))
+            pick(after[:, t - 1, :], h1[t])
+            square("sggg"[t], after[:, t - 1, :], after[:, t - 1, :])
 
-        h1 = first_stage(1, [])
-        picked0 = placed([P, PACK, M], F32, "log_a0", at_log_a0)
-        for t in range(PACK):
-            row = early[:, t, :] if t < 1 else late[:, t - 1, :]
-            square("ssss"[t], picked0[:, t, :], row)
-            nc.scalar.activation(out=picked0[:, t, :], in_=picked0[:, t, :], func=ACT.Ln, bias=half[:])
-        v2_codes = [new_tile([P, M], U32, "v2_%d" % a) for a in range(PASSES2)]
-        for a in range(PASSES2):
-            nc.vector.tensor_copy(v2_codes[a][:], tab2_sb[a][:].bitcast(U32).indirect(offs2_sb[:]))
-
-        log_bt0 = project_files(0)
-        picked1 = placed([P, PACK, M], F32, "picked1", at_tab1 + 8 * KIB)
-        log_a1 = placed([P, PACK, M], F32, "log_a1", at_w2[0])
-        for t in range(PACK):
-            pick(picked1, h1, t)
-
-        def log_a1_chunk(i):
-            files = slice(i * P, (i + 1) * P)
-            square("vvss"[i], log_a1[:, :, files], picked1[:, :, files])
-            nc.scalar.activation(out=log_a1[:, :, files], in_=log_a1[:, :, files], func=ACT.Ln, bias=half[:])
-
-        make_z(0, log_bt0, picked0, 2 * P)
-        log_bt1 = project_files(1)
+        spare = new_tile([P, 1, PASS], F32, "spare")
+        log_bt0 = [spare[:, i, :] if i < 1 else log_a1[:, i, :] for i in range(CHUNKS)]
+        bt0 = [bank([P, BANK], "bt", i) for i in range(CHUNKS)]
+        for a, i in itertools.product(range(PASSES2), range(CHUNKS)):
+            project(0, i, a, bt0[i])
+        gate = placed([P, PASS], F32, "gate", at_diff0)
         for i in range(CHUNKS):
-            log_a1_chunk(i)
-        make_z(1, log_bt1, log_a1, P)
+            log_b_turned(log_bt0[i], bt0[i], gate[:] if i == 2 else None)
+        diff0 = placed([P, PACK, M], F32, "diff0", at_diff0)
+        rounded = None
+        for i in range(CHUNKS):
+            subtract(log_bt0[i], log_a0, i, CHUNKS + i, diff0[:, :, i * P:(i + 1) * P])
+            if i % 2 == 0 and rounded:
+                quantise_z(*rounded)
+            if i % 2 == 2 - 1:
+                m0 = (i + 1 - 2) * P
+                rounded = apply_gain(0, diff0[:, :, m0:(i + 1) * P], m0, 2 * P)
+        for t in range(1, PACK):
+            log_of(log_a1[:, t, :], after[:, t - 1, :])
+
+        log_bt1 = new_tile([P, CHUNKS, PASS], F32, "log_bt1")
+        for i in range(CHUNKS):
+            bt = bank([P, BANK], "bt", i)
+            for a in range(PASSES2):
+                project(1, i, a, bt)
+            log_b_turned(log_bt1[:, i, :], bt)
+            diff = new_tile([P, PACK, P], F32, "diff1%d" % i, "diff1%d" % min(i, 2))
+            subtract(log_bt1[:, i, :], log_a1, i, CHUNKS + i, diff[:])
+            quantise_z(*rounded)
+            rounded = apply_gain(1, diff[:], i * P, P)
+        quantise_z(*rounded)
 
         out_view = out.rearrange("(g p) m -> p g m", p=P)
         levels = new_tile([P, CHUNKS, N // P, P], F32, "levels", "half")
-        for i in range(CHUNKS):
-            y = bank([P, N // P, P], "y", i)
-            for blk, g in itertools.product(range(BLOCKS), range(N // P)):
+
+        def alarm(i, groups, b):
+            y = bank([P, len(groups), P], "y", b)
+            for blk, g in itertools.product(range(BLOCKS), groups):
                 cols = slice(blk * N + g * P, blk * N + (g + 1) * P)
                 nc.tensor.matmul_mx(
-                    out=y[:, g, :],
+                    out=y[:, g - groups[0], :],
                     lhsT=w3_sb[:, cols].bitcast(FP8X4),
                     lhsT_scale=w3_planes[:, cols],
                     rhs=z_codes[blk, i].bitcast(FP8X4),
                     rhs_scale=z_planes[blk, i],
-                    start=(blk == 0 and g == 0), stop=(blk == BLOCKS - 1 and g == N // P - 1),
+                    start=(blk == 0 and g == groups[0]), stop=(blk == BLOCKS - 1 and g == groups[-1]),
                 )
-            nc.scalar.activation(out=levels[:, i], in_=y[:], func=ACT.Sigmoid)
-            nc.sync.dma_start(out=out_view[:, :, i * P:(i + 1) * P], in_=levels[:, i])
+            rows = slice(groups[0], groups[-1] + 1)
+            nc.scalar.activation(out=levels[:, i, rows], in_=y[:], func=ACT.Sigmoid)
+            nc.sync.dma_start(out=out_view[:, rows, i * P:(i + 1) * P], in_=levels[:, i, rows])
+
+        for i in range(CHUNKS - 1):
+            alarm(i, range(N // P), i)
+        alarm(CHUNKS - 1, range(0, 2), CHUNKS - 1)
+        alarm(CHUNKS - 1, range(2, 4), CHUNKS)

@@ -66,11 +66,12 @@ def tile_list_ransomware_alarm_levels_kernel(
         at_bf01 = 50
         at_bf00 = 54
         at_early = 58
-        at_bf10 = at_early + 4 - 1
-        at_bf11 = at_bf10 + 1
+        at_bf10 = at_early + 6
+        at_bf11 = at_bf10 + 4
         at_late = at_bf11 + 3
         at_h11 = at_late + 8
         at_diff0 = at_h11 + 4
+        at_h13 = at_diff0 + 8
 
         offs_sb = sbuf.tile([P, S // GROUP], U16, name="offs_sb")
         pos_sb = sbuf.tile([P, M // GROUP], U16, name="pos_sb")
@@ -183,9 +184,9 @@ def tile_list_ransomware_alarm_levels_kernel(
             rounding(grouped, w1_raw[blk, a])
             quantise_rounded(blk, a, 0, grouped, PACK)
 
-        def quantise_w1_halves(blk, a, kib):
+        def quantise_w1_halves(blk, a, kib, copies):
             grouped = [placed([P, 2 * PASS], BF16, "w1_bf%d%d%d" % (blk, a, u), kib + 2 * u) for u in range(2)]
-            for u, copy in enumerate((nc.vector.tensor_copy, nc.scalar.copy)):
+            for u, copy in enumerate(copies):
                 copy(grouped[u][:].rearrange("p (e m j) -> p m j e", e=2, j=PACK), by_pairs(w1_raw[blk, a])[:, u])
             for u in range(2):
                 quantise_rounded(blk, a, 2 * u, grouped[u], 2)
@@ -196,7 +197,7 @@ def tile_list_ransomware_alarm_levels_kernel(
         nc.gpsimd.memset(w2_planes[:].bitcast(I32), 0)
         load_planes(w2_planes, w2_scales, PASSES2)
         tab2_sb.append(load_words(tab2_words[1], "tab2_1", at_tab1))
-        quantise_w1_halves(0, 1, at_bf01)
+        quantise_w1_halves(0, 1, at_bf01, (nc.vector.tensor_copy, nc.scalar.copy))
         def load_w2(blk, kib):
             words = placed([P, PASSES2 * 2 * PASS], U8, "w2_sb%d" % blk, kib)
             nc.sync.dma_start(
@@ -291,12 +292,13 @@ def tile_list_ransomware_alarm_levels_kernel(
 
         h0 = [new_tile([P, S], F32, "h0%d" % t) for t in range(PACK)]
         first_stage(0, h0, [])
+        early = placed([P, 3, M], F32, "early", at_early)
+        pick(early[:, 0, :], h0[0])
         quantise_w1(1, 0, round_by_pairs(nc.vector.tensor_copy), at_bf10)
         tab2_sb.append(load_words(tab2_words[2], "tab2_2", at_raw10))
-        early = placed([P, 2, M], F32, "early", at_early)
-        for t in range(2):
+        for t in range(1, 3):
             pick(early[:, t, :], h0[t])
-        quantise_w1(1, 1, round_on_gpsimd, at_bf11)
+        quantise_w1_halves(1, 1, at_bf11, (nc.vector.tensor_copy, nc.vector.tensor_copy))
         w2_sb.append(load_w2(1, at_raw11 + 5))
         w3_sb = placed([P, BLOCKS * N], I32, "w3_sb", at_raw11)
         nc.sync.dma_start(
@@ -308,33 +310,44 @@ def tile_list_ransomware_alarm_levels_kernel(
         w3_planes = placed([P, BLOCKS * N], U8, "w3_planes", at_raw11 + 4)
         nc.vector.memset(w3_planes[:].bitcast(I32), 0)
         load_planes(w3_planes, w3_scales, BLOCKS)
-        late = placed([P, PACK - 2, M], F32, "late", at_late)
-        for t in range(2, PACK):
-            pick(late[:, t - 2, :], h0[t])
+        late = placed([P, PACK - 3, M], F32, "late", at_late)
+        for t in range(3, PACK):
+            pick(late[:, t - 3, :], h0[t])
 
+        for t in range(3, PACK):
+            if "ssss"[t] == "v":
+                square("v", late[:, t - 3, :], late[:, t - 3, :])
+        log_a0 = new_tile([P, PACK, M], F32, "log_a0")
+        for t in range(3):
+            square("ssss"[t], log_a0[:, t, :], early[:, t, :])
+            log_of(log_a0[:, t, :], log_a0[:, t, :])
         h1 = [
-            placed([P, S], F32, "h1%d" % t, at_h11) if t == 1 - 1 else new_tile([P, S], F32, "h1%d" % t)
+            placed([P, S], F32, "h1%d" % t, {1: at_h11, 3: at_h13}[t]) if t % 2 else new_tile([P, S], F32, "h1%d" % t)
             for t in range(PACK)
         ]
         first_stage(1, h1, [])
-        log_a0 = new_tile([P, PACK, M], F32, "log_a0")
-        for t in range(PACK):
-            row = early[:, t, :] if t < 2 else late[:, t - 2, :]
-            square("ssgg"[t], log_a0[:, t, :], row)
-            log_of(log_a0[:, t, :], log_a0[:, t, :])
+        for t in range(3, PACK):
+            row = late[:, t - 3, :]
+            if "ssss"[t] == "s":
+                square("s", log_a0[:, t, :], row)
+                log_of(log_a0[:, t, :], log_a0[:, t, :])
+            else:
+                log_of(log_a0[:, t, :], row)
         v2_codes = [gather_v2(0, placed([P, M], U32, "v2_0", at_bf11 + 1)), gather_v2(1, new_tile([P, M], U32, "v2_1"))]
 
         log_a1 = new_tile([P, PACK, M], F32, "log_a1")
-        before = new_tile([P, 1, M], F32, "before")
-        for t in range(1):
+        before = new_tile([P, 2, M], F32, "before")
+        for t in range(2):
             pick(before[:, t, :], h1[t])
-            square("sggg"[t], log_a1[:, t, :], before[:, t, :])
-            log_of(log_a1[:, t, :], log_a1[:, t, :])
+        square("s", log_a1[:, 0, :], before[:, 0, :])
+        log_of(log_a1[:, 0, :], log_a1[:, 0, :])
         v2_codes.append(gather_v2(2, placed([P, M], U32, "v2_2", at_h11)))
-        after = placed([P, PACK - 1, M], F32, "after", at_raw10)
-        for t in range(1, PACK):
-            pick(after[:, t - 1, :], h1[t])
-            square("sggg"[t], after[:, t - 1, :], after[:, t - 1, :])
+        after = placed([P, PACK - 2, M], F32, "after", at_raw10)
+        for t in range(2, PACK):
+            pick(after[:, t - 2, :], h1[t])
+        squares = placed([P, PACK - 1, M], F32, "squares", at_h13)
+        square("v", squares[:, 0, :], before[:, 1, :])
+        square("v", squares[:, 1:, :], after[:])
 
         spare = new_tile([P, 1, PASS], F32, "spare")
         log_bt0 = [spare[:, i, :] if i < 1 else log_a1[:, i, :] for i in range(CHUNKS)]
@@ -343,25 +356,25 @@ def tile_list_ransomware_alarm_levels_kernel(
             project(0, i, a, bt0[i])
         gate = placed([P, PASS], F32, "gate", at_diff0)
         for i in range(CHUNKS):
-            log_b_turned(log_bt0[i], bt0[i], gate[:] if i == 2 else None)
+            log_b_turned(log_bt0[i], bt0[i], gate[:] if i == 0 else None)
         diff0 = placed([P, PACK, M], F32, "diff0", at_diff0)
         rounded = None
         for i in range(CHUNKS):
             subtract(log_bt0[i], log_a0, i, CHUNKS + i, diff0[:, :, i * P:(i + 1) * P])
-            if i % 2 == 0 and rounded:
+            if i % 1 == 0 and rounded:
                 quantise_z(*rounded)
-            if i % 2 == 2 - 1:
-                m0 = (i + 1 - 2) * P
-                rounded = apply_gain(0, diff0[:, :, m0:(i + 1) * P], m0, 2 * P)
-        for t in range(1, PACK):
-            log_of(log_a1[:, t, :], after[:, t - 1, :])
-
+            if i % 1 == 1 - 1:
+                m0 = (i + 1 - 1) * P
+                rounded = apply_gain(0, diff0[:, :, m0:(i + 1) * P], m0, 1 * P)
         log_bt1 = new_tile([P, CHUNKS, PASS], F32, "log_bt1")
         for i in range(CHUNKS):
             bt = bank([P, BANK], "bt", i)
             for a in range(PASSES2):
                 project(1, i, a, bt)
             log_b_turned(log_bt1[:, i, :], bt)
+            if i == 2 - 1:
+                log_of(log_a1[:, 1:, :], squares[:])
+        for i in range(CHUNKS):
             diff = new_tile([P, PACK, P], F32, "diff1%d" % i, "diff1%d" % min(i, 2))
             subtract(log_bt1[:, i, :], log_a1, i, CHUNKS + i, diff[:])
             quantise_z(*rounded)

@@ -157,11 +157,12 @@ def tile_list_ransomware_alarm_levels_kernel(
         w1_codes, w1_planes = {}, {}
 
         def by_pairs(raw):
-            return raw[:].rearrange("p j (m u e) -> p u m j e", u=2, e=2)
+            return raw[:].rearrange("p j (m u e) -> p u m e j", u=2, e=2)
 
         def round_by_pairs(copy):
             return lambda grouped, raw: copy(
-                grouped[:].rearrange("p (u e m j) -> p u m j e", u=2, e=2, j=PACK), by_pairs(raw)
+                grouped[:].rearrange("p (t m j) -> p m t j", t=PACK, j=PACK),
+                raw[:].rearrange("p j (m t) -> p m t j", t=PACK),
             )
 
         def round_on_gpsimd(grouped, raw):
@@ -187,7 +188,7 @@ def tile_list_ransomware_alarm_levels_kernel(
         def quantise_w1_halves(blk, a, kib, copies):
             grouped = [placed([P, 2 * PASS], BF16, "w1_bf%d%d%d" % (blk, a, u), kib + 2 * u) for u in range(2)]
             for u, copy in enumerate(copies):
-                copy(grouped[u][:].rearrange("p (e m j) -> p m j e", e=2, j=PACK), by_pairs(w1_raw[blk, a])[:, u])
+                copy(grouped[u][:].rearrange("p (e m j) -> p m e j", e=2, j=PACK), by_pairs(w1_raw[blk, a])[:, u])
             for u in range(2):
                 quantise_rounded(blk, a, 2 * u, grouped[u], 2)
 
@@ -257,8 +258,8 @@ def tile_list_ransomware_alarm_levels_kernel(
         def log_b_turned(log_bt, bt, squared=None):
             squared = log_bt if squared is None else squared
             nc.scalar.activation(
-                out=squared.rearrange("m (u e p) -> m u p e", u=2, e=2),
-                in_=bt[:].rearrange("m (p u e) -> m u p e", u=2, e=2),
+                out=squared.rearrange("m (t p) -> m t p", t=PACK),
+                in_=bt[:].rearrange("m (p t) -> m t p", t=PACK),
                 func=ACT.Square,
             )
             log_of(log_bt, squared)
@@ -267,15 +268,19 @@ def tile_list_ransomware_alarm_levels_kernel(
             log_b = bank([P, PACK, P], "log_b", b)
             for t in range(PACK):
                 nc.tensor.transpose(log_b[:, t, :], log_bt[:, t * P:(t + 1) * P], ident[:])
-            chunk = log_a[:, :, i * P:(i + 1) * P]
-            nc.vector.tensor_tensor(chunk if diff is None else diff, log_b[:], chunk, ALU.subtract)
+            nc.vector.tensor_tensor(
+                diff,
+                log_b[:].rearrange("p (u e) m -> p u m e", u=2),
+                log_a[:, :, i * P:(i + 1) * P].rearrange("p (u e) m -> p u m e", u=2),
+                ALU.subtract,
+            )
 
         def apply_gain(blk, diff, m0, width):
             z = new_tile([P, PACK * width], BF16, "z%d_%d" % (blk, m0))
             nc.vector.tensor_tensor(
-                z[:].rearrange("p (c e t) -> p c t e", e=LINE, t=PACK),
-                diff.rearrange("p t (c e) -> p c t e", e=LINE),
-                gain_sb[:, blk, :].unsqueeze(1).unsqueeze(3).to_broadcast([P, width // LINE, PACK, LINE]),
+                z[:].rearrange("p (m u e) -> p m u e", u=2, e=2),
+                diff.rearrange("p u m e -> p m u e"),
+                gain_sb[:, blk, :].rearrange("p (u e) -> p u e", u=2).unsqueeze(1).to_broadcast([P, width, 2, 2]),
                 ALU.mult,
             )
             return blk, z, m0, width
@@ -357,15 +362,15 @@ def tile_list_ransomware_alarm_levels_kernel(
         gate = placed([P, PASS], F32, "gate", at_diff0)
         for i in range(CHUNKS):
             log_b_turned(log_bt0[i], bt0[i], gate[:] if i == 0 else None)
-        diff0 = placed([P, PACK, M], F32, "diff0", at_diff0)
+        diff0 = placed([P, 2, M, 2], F32, "diff0", at_diff0)
         rounded = None
         for i in range(CHUNKS):
-            subtract(log_bt0[i], log_a0, i, CHUNKS + i, diff0[:, :, i * P:(i + 1) * P])
+            subtract(log_bt0[i], log_a0, i, CHUNKS + i, diff0[:, :, i * P:(i + 1) * P, :])
             if i % 1 == 0 and rounded:
                 quantise_z(*rounded)
             if i % 1 == 1 - 1:
                 m0 = (i + 1 - 1) * P
-                rounded = apply_gain(0, diff0[:, :, m0:(i + 1) * P], m0, 1 * P)
+                rounded = apply_gain(0, diff0[:, :, m0:(i + 1) * P, :], m0, 1 * P)
         log_bt1 = new_tile([P, CHUNKS, PASS], F32, "log_bt1")
         for i in range(CHUNKS):
             bt = bank([P, BANK], "bt", i)
@@ -375,7 +380,7 @@ def tile_list_ransomware_alarm_levels_kernel(
             if i == 2 - 1:
                 log_of(log_a1[:, 1:, :], squares[:])
         for i in range(CHUNKS):
-            diff = new_tile([P, PACK, P], F32, "diff1%d" % i, "diff1%d" % min(i, 2))
+            diff = new_tile([P, 2, P, 2], F32, "diff1%d" % i, "diff1%d" % min(i, 2))
             subtract(log_bt1[:, i, :], log_a1, i, CHUNKS + i, diff[:])
             quantise_z(*rounded)
             rounded = apply_gain(1, diff[:], i * P, P)

@@ -31,9 +31,11 @@ GROUP = 16
 PASSES, PASSES2, BLOCKS = K // PASS, K2 // PASS, H // PASS
 HALVES = S // BANK
 CHUNKS = M // P
-LINE = 4
-
+PAIRS = PACK // 2
 KIB = 1024
+EARLY = 3
+AHEAD = 2
+ON_SCALAR = 1
 
 
 def words_of(packed):
@@ -50,8 +52,8 @@ def tile_list_ransomware_alarm_levels_kernel(
         arena = ctx.enter_context(tc.tile_pool(name="arena", bufs=1))
         psum = ctx.enter_context(tc.psum_pool(name="psum", bufs=1))
 
-        def new_tile(shape, dtype, name, after=None):
-            return sbuf.tile(shape, dtype, name=name, tag=after or name, align_bytes=64)
+        def new_tile(shape, dtype, name, tag=None):
+            return sbuf.tile(shape, dtype, name=name, tag=tag or name, align_bytes=64)
 
         def placed(shape, dtype, name, kib):
             return arena.tile(shape, dtype, name=name, tag=name, offset=kib * KIB, align_bytes=64)
@@ -59,19 +61,21 @@ def tile_list_ransomware_alarm_levels_kernel(
         def bank(shape, name, b):
             return psum.tile(shape, F32, name=name, tag="bank%d" % b)
 
-        at_tab0, at_raw10, at_v2_planes, at_raw11 = 0, 0, 8, 10
+        at_tab0 = 0
+        at_raw10 = 0
+        at_v2_planes = 8
+        at_raw11 = 10
         at_tab1 = 18
         at_raw01 = 34
         at_raw00 = 42
-        at_bf01 = 50
-        at_bf00 = 54
+        at_rounded01 = 50
+        at_rounded00 = 54
         at_early = 58
-        at_bf10 = at_early + 6
-        at_bf11 = at_bf10 + 4
-        at_late = at_bf11 + 3
-        at_h11 = at_late + 8
-        at_diff0 = at_h11 + 4
-        at_h13 = at_diff0 + 8
+        at_rounded10 = 64
+        at_rounded11 = 68
+        at_h11 = 79
+        at_diff0 = 83
+        at_h13 = 91
 
         offs_sb = sbuf.tile([P, S // GROUP], U16, name="offs_sb")
         pos_sb = sbuf.tile([P, M // GROUP], U16, name="pos_sb")
@@ -86,8 +90,6 @@ def tile_list_ransomware_alarm_levels_kernel(
         nc.vector.memset(tab_sc[:].bitcast(I32)[:top], 0)
         nc.vector.memset(tab2_sc[:].bitcast(I32)[:top2], 0)
         nc.vector.memset(v_planes[:].bitcast(I32), 0)
-        warm = new_tile([P, 1], F32, "warm")
-        nc.scalar.activation(out=warm[:], in_=half[:], func=ACT.Ln, bias=half[:])
 
         def load_w1(blk, a, kib):
             raw = placed([P, PACK, PASS], F32, "w1_raw%d%d" % (blk, a), kib)
@@ -100,6 +102,14 @@ def tile_list_ransomware_alarm_levels_kernel(
             nc.sync.dma_start(out=words[:], in_=words_of(packed))
             return words
 
+        def load_w2(blk, kib):
+            words = placed([P, PASSES2 * 2 * PASS], U8, "w2_sb%d" % blk, kib)
+            nc.sync.dma_start(
+                out=words[:].bitcast(I32).rearrange("p (a c) -> p a c", a=PASSES2),
+                in_=w2_words[:, :, 2 * blk * PASS:2 * (blk + 1) * PASS].bitcast(I32).rearrange("a p c -> p a c"),
+            )
+            return words
+
         def load_planes(planes, scales, passes):
             view = planes[:].bitcast(I32).rearrange("p (a c) -> p a c", a=passes)
             for r in range(ROWS):
@@ -110,7 +120,8 @@ def tile_list_ransomware_alarm_levels_kernel(
 
         def carry_planes(planes, gathered, lowest, passes):
             view = planes[:].bitcast(I32).rearrange("p (a c) -> p a c", a=passes)
-            for q in (0, 2, 1, 3):
+            for low, upper in itertools.product(range(QUADS // 2), range(2)):
+                q = low + upper * QUADS // 2
                 start = lowest + q * ROWS * passes
                 nc.sync.dma_start(
                     out=view[q * QUAD:q * QUAD + ROWS], in_=gathered[:].bitcast(I32)[start:start + ROWS * passes]
@@ -156,89 +167,69 @@ def tile_list_ransomware_alarm_levels_kernel(
 
         w1_codes, w1_planes = {}, {}
 
-        def by_pairs(raw):
-            return raw[:].rearrange("p j (m u e) -> p u m e j", u=2, e=2)
-
-        def round_by_pairs(copy):
-            return lambda grouped, raw: copy(
-                grouped[:].rearrange("p (t m j) -> p m t j", t=PACK, j=PACK),
-                raw[:].rearrange("p j (m t) -> p m t j", t=PACK),
-            )
-
-        def round_on_gpsimd(grouped, raw):
-            nc.gpsimd.tensor_scalar(
-                grouped[:].rearrange("p (t m j) -> p t m j", t=PACK, j=PACK),
-                raw[:].rearrange("p j (m t) -> p t m j", t=PACK),
-                1.0, 0.0, ALU.mult, ALU.add,
-            )
-
-        def quantise_rounded(blk, a, t0, grouped, sets):
+        def quantise_rounded(blk, a, t0, rounded, sets):
             codes = new_tile([P, sets * P], U32, "w1_codes%d%d%d" % (blk, a, t0))
             planes = new_tile([P, sets * P], U8, "w1_planes%d%d%d" % (blk, a, t0))
-            nc.vector.quantize_mx(out=codes[:].bitcast(FP8X4), scales=planes[:], in_=grouped[:])
+            nc.vector.quantize_mx(out=codes[:].bitcast(FP8X4), scales=planes[:], in_=rounded[:])
             for e in range(sets):
                 w1_codes[blk, a, t0 + e] = codes[:, e * P:(e + 1) * P]
                 w1_planes[blk, a, t0 + e] = planes[:, e * P:(e + 1) * P]
 
-        def quantise_w1(blk, a, rounding, kib):
-            grouped = placed([P, PACK * PASS], BF16, "w1_bf%d%d" % (blk, a), kib)
-            rounding(grouped, w1_raw[blk, a])
-            quantise_rounded(blk, a, 0, grouped, PACK)
+        def quantise_w1(blk, a, copy, rounded):
+            copy(
+                rounded[:].rearrange("p (t m j) -> p m t j", t=PACK, j=PACK),
+                w1_raw[blk, a][:].rearrange("p j (m t) -> p m t j", t=PACK),
+            )
+            quantise_rounded(blk, a, 0, rounded, PACK)
 
-        def quantise_w1_halves(blk, a, kib, copies):
-            grouped = [placed([P, 2 * PASS], BF16, "w1_bf%d%d%d" % (blk, a, u), kib + 2 * u) for u in range(2)]
-            for u, copy in enumerate(copies):
-                copy(grouped[u][:].rearrange("p (e m j) -> p m e j", e=2, j=PACK), by_pairs(w1_raw[blk, a])[:, u])
-            for u in range(2):
-                quantise_rounded(blk, a, 2 * u, grouped[u], 2)
+        def quantise_w1_by_pairs(blk, a, copies, rounded):
+            pairs = w1_raw[blk, a][:].rearrange("p j (m u e) -> p u m e j", u=PAIRS, e=2)
+            for u in range(PAIRS):
+                copies[u](rounded[u][:].rearrange("p (e m j) -> p m e j", e=2, j=PACK), pairs[:, u])
+            for u in range(PAIRS):
+                quantise_rounded(blk, a, 2 * u, rounded[u], 2)
 
-        quantise_w1(0, 0, round_by_pairs(nc.scalar.copy), at_bf00)
+        quantise_w1(0, 0, nc.scalar.copy, placed([P, PACK * PASS], BF16, "w1_bf00", at_rounded00))
         tab2_sb = [load_words(tab2_words[0], "tab2_0", at_raw00)]
-        w2_planes = placed([P, PASSES2 * H], U8, "w2_planes", at_bf00)
+        w2_planes = placed([P, PASSES2 * H], U8, "w2_planes", at_rounded00)
         nc.gpsimd.memset(w2_planes[:].bitcast(I32), 0)
         load_planes(w2_planes, w2_scales, PASSES2)
         tab2_sb.append(load_words(tab2_words[1], "tab2_1", at_tab1))
-        quantise_w1_halves(0, 1, at_bf01, (nc.vector.tensor_copy, nc.scalar.copy))
-        def load_w2(blk, kib):
-            words = placed([P, PASSES2 * 2 * PASS], U8, "w2_sb%d" % blk, kib)
-            nc.sync.dma_start(
-                out=words[:].bitcast(I32).rearrange("p (a c) -> p a c", a=PASSES2),
-                in_=w2_words[:, :, 2 * blk * PASS:2 * (blk + 1) * PASS].bitcast(I32).rearrange("a p c -> p a c"),
-            )
-            return words
-
+        quantise_w1_by_pairs(
+            0, 1, (nc.vector.tensor_copy, nc.scalar.copy),
+            [placed([P, 2 * PASS], BF16, "w1_bf01%d" % u, at_rounded01 + 2 * u) for u in range(PAIRS)],
+        )
         w2_sb = [load_w2(0, at_raw01)]
 
-        def first_stage(blk, h, on_vector):
-            acc = {}
-            for t, u, a in itertools.product(range(PACK), range(HALVES), range(PASSES)):
-                if a == 0:
-                    acc[t, u] = bank([P, BANK], "acc", HALVES * t + u)
-                nc.tensor.matmul_mx(
-                    out=acc[t, u][:],
-                    lhsT=w1_codes[blk, a, t].bitcast(FP8X4),
-                    lhsT_scale=w1_planes[blk, a, t],
-                    rhs=v_codes[a, u][:].bitcast(FP8X4),
-                    rhs_scale=v_planes[:, a * S + u * BANK:a * S + (u + 1) * BANK],
-                    start=(a == 0), stop=(a == PASSES - 1),
-                )
-                if a == PASSES - 1:
-                    copy = nc.vector.tensor_copy if (t, u) in on_vector else nc.scalar.copy
-                    copy(h[t][:, u * BANK:(u + 1) * BANK], acc[t, u][:])
+        def first_stage(blk, places):
+            h = [
+                placed([P, S], F32, "h%d%d" % (blk, t), places[t]) if t in places
+                else new_tile([P, S], F32, "h%d%d" % (blk, t))
+                for t in range(PACK)
+            ]
+            for t, u in itertools.product(range(PACK), range(HALVES)):
+                acc = bank([P, BANK], "acc", HALVES * t + u)
+                for a in range(PASSES):
+                    nc.tensor.matmul_mx(
+                        out=acc[:],
+                        lhsT=w1_codes[blk, a, t].bitcast(FP8X4),
+                        lhsT_scale=w1_planes[blk, a, t],
+                        rhs=v_codes[a, u][:].bitcast(FP8X4),
+                        rhs_scale=v_planes[:, a * S + u * BANK:a * S + (u + 1) * BANK],
+                        start=(a == 0), stop=(a == PASSES - 1),
+                    )
+                nc.scalar.copy(h[t][:, u * BANK:(u + 1) * BANK], acc[:])
+            return h
 
-        def pick(row, h):
-            nc.vector.tensor_copy(row, h[:].indirect(pos_sb[:]))
+        def pick(row, window):
+            nc.vector.tensor_copy(row, window[:].indirect(pos_sb[:]))
 
-        def square(engine, squared, values):
-            if engine == "s":
-                nc.scalar.activation(out=squared, in_=values, func=ACT.Square)
-            elif engine == "v":
-                nc.vector.tensor_tensor(squared, values, values, ALU.mult)
-            else:
-                nc.gpsimd.tensor_tensor(squared, values, values, ALU.mult)
+        def log_half_plus(logs, squares):
+            nc.scalar.activation(out=logs, in_=squares, func=ACT.Ln, bias=half[:])
 
-        def log_of(logs, squared):
-            nc.scalar.activation(out=logs, in_=squared, func=ACT.Ln, bias=half[:])
+        def log_on_scalar(logs, values):
+            nc.scalar.activation(out=logs, in_=values, func=ACT.Square)
+            log_half_plus(logs, logs)
 
         def gather_v2(a, codes):
             nc.vector.tensor_copy(codes[:], tab2_sb[a][:].bitcast(U32).indirect(offs2_sb[:]))
@@ -255,157 +246,146 @@ def tile_list_ransomware_alarm_levels_kernel(
                 start=(a == 0), stop=(a == PASSES2 - 1),
             )
 
-        def log_b_turned(log_bt, bt, squared=None):
-            squared = log_bt if squared is None else squared
+        def log_of_bt(log_bt, squares, bt):
             nc.scalar.activation(
-                out=squared.rearrange("m (t p) -> m t p", t=PACK),
+                out=squares.rearrange("m (t p) -> m t p", t=PACK),
                 in_=bt[:].rearrange("m (p t) -> m t p", t=PACK),
                 func=ACT.Square,
             )
-            log_of(log_bt, squared)
+            log_half_plus(log_bt, squares)
 
-        def subtract(log_bt, log_a, i, b, diff=None):
-            log_b = bank([P, PACK, P], "log_b", b)
-            for t in range(PACK):
-                nc.tensor.transpose(log_b[:, t, :], log_bt[:, t * P:(t + 1) * P], ident[:])
-            nc.vector.tensor_tensor(
-                diff,
-                log_b[:].rearrange("p (u e) m -> p u m e", u=2),
-                log_a[:, :, i * P:(i + 1) * P].rearrange("p (u e) m -> p u m e", u=2),
-                ALU.subtract,
-            )
-
-        def apply_gain(blk, diff, m0, width):
-            z = new_tile([P, PACK * width], BF16, "z%d_%d" % (blk, m0))
-            nc.vector.tensor_tensor(
-                z[:].rearrange("p (m u e) -> p m u e", u=2, e=2),
-                diff.rearrange("p u m e -> p m u e"),
-                gain_sb[:, blk, :].rearrange("p (u e) -> p u e", u=2).unsqueeze(1).to_broadcast([P, width, 2, 2]),
-                ALU.mult,
-            )
-            return blk, z, m0, width
-
-        z_codes, z_planes = {}, {}
-
-        def quantise_z(blk, z, m0, width):
-            codes = new_tile([P, width], U32, "z_codes%d_%d" % (blk, m0))
-            plane = new_tile([P, width], U8, "z_planes%d_%d" % (blk, m0))
-            nc.vector.quantize_mx(out=codes[:].bitcast(FP8X4), scales=plane[:], in_=z[:])
-            for c0 in range(0, width, P):
-                z_codes[blk, (m0 + c0) // P] = codes[:, c0:c0 + P]
-                z_planes[blk, (m0 + c0) // P] = plane[:, c0:c0 + P]
-
-        h0 = [new_tile([P, S], F32, "h0%d" % t) for t in range(PACK)]
-        first_stage(0, h0, [])
-        early = placed([P, 3, M], F32, "early", at_early)
+        h0 = first_stage(0, {})
+        early = placed([P, EARLY, M], F32, "early", at_early)
         pick(early[:, 0, :], h0[0])
-        quantise_w1(1, 0, round_by_pairs(nc.vector.tensor_copy), at_bf10)
+        quantise_w1(1, 0, nc.vector.tensor_copy, placed([P, PACK * PASS], BF16, "w1_bf10", at_rounded10))
         tab2_sb.append(load_words(tab2_words[2], "tab2_2", at_raw10))
-        for t in range(1, 3):
+        for t in range(1, EARLY):
             pick(early[:, t, :], h0[t])
-        quantise_w1_halves(1, 1, at_bf11, (nc.vector.tensor_copy, nc.vector.tensor_copy))
+        quantise_w1_by_pairs(
+            1, 1, (nc.vector.tensor_copy, nc.vector.tensor_copy),
+            [placed([P, 2 * PASS], BF16, "w1_bf11%d" % u, at_rounded11 + 2 * u) for u in range(PAIRS)],
+        )
         w2_sb.append(load_w2(1, at_raw11 + 5))
         w3_sb = placed([P, BLOCKS * N], I32, "w3_sb", at_raw11)
         nc.sync.dma_start(
             out=w3_sb[:].rearrange("p (b c) -> p b c", b=BLOCKS),
             in_=w3_words.rearrange("b p c i -> p b (c i)").bitcast(I32),
         )
-        gain_sb = placed([P, BLOCKS, PACK], F32, "gain_sb", at_bf11)
+        gain_sb = placed([P, BLOCKS, PACK], F32, "gain_sb", at_rounded11)
         nc.sync.dma_start(out=gain_sb[:], in_=gain.rearrange("(b p t) -> p b t", b=BLOCKS, t=PACK))
         w3_planes = placed([P, BLOCKS * N], U8, "w3_planes", at_raw11 + 4)
         nc.vector.memset(w3_planes[:].bitcast(I32), 0)
         load_planes(w3_planes, w3_scales, BLOCKS)
-        late = placed([P, PACK - 3, M], F32, "late", at_late)
-        for t in range(3, PACK):
-            pick(late[:, t - 3, :], h0[t])
+        late = placed([P, PACK - EARLY, M], F32, "late", at_rounded11 + 3)
+        for t in range(EARLY, PACK):
+            pick(late[:, t - EARLY, :], h0[t])
 
-        for t in range(3, PACK):
-            if "ssss"[t] == "v":
-                square("v", late[:, t - 3, :], late[:, t - 3, :])
         log_a0 = new_tile([P, PACK, M], F32, "log_a0")
-        for t in range(3):
-            square("ssss"[t], log_a0[:, t, :], early[:, t, :])
-            log_of(log_a0[:, t, :], log_a0[:, t, :])
-        h1 = [
-            placed([P, S], F32, "h1%d" % t, {1: at_h11, 3: at_h13}[t]) if t % 2 else new_tile([P, S], F32, "h1%d" % t)
-            for t in range(PACK)
+        for t in range(EARLY):
+            log_on_scalar(log_a0[:, t, :], early[:, t, :])
+        h1 = first_stage(1, {AHEAD - 1: at_h11, PACK - 1: at_h13})
+        for t in range(EARLY, PACK):
+            log_on_scalar(log_a0[:, t, :], late[:, t - EARLY, :])
+        v2_codes = [
+            gather_v2(0, placed([P, M], U32, "v2_0", at_rounded11 + 1)),
+            gather_v2(1, new_tile([P, M], U32, "v2_1")),
         ]
-        first_stage(1, h1, [])
-        for t in range(3, PACK):
-            row = late[:, t - 3, :]
-            if "ssss"[t] == "s":
-                square("s", log_a0[:, t, :], row)
-                log_of(log_a0[:, t, :], log_a0[:, t, :])
-            else:
-                log_of(log_a0[:, t, :], row)
-        v2_codes = [gather_v2(0, placed([P, M], U32, "v2_0", at_bf11 + 1)), gather_v2(1, new_tile([P, M], U32, "v2_1"))]
 
         log_a1 = new_tile([P, PACK, M], F32, "log_a1")
-        before = new_tile([P, 2, M], F32, "before")
-        for t in range(2):
+        before = new_tile([P, AHEAD, M], F32, "before")
+        for t in range(AHEAD):
             pick(before[:, t, :], h1[t])
-        square("s", log_a1[:, 0, :], before[:, 0, :])
-        log_of(log_a1[:, 0, :], log_a1[:, 0, :])
+        for t in range(ON_SCALAR):
+            log_on_scalar(log_a1[:, t, :], before[:, t, :])
         v2_codes.append(gather_v2(2, placed([P, M], U32, "v2_2", at_h11)))
-        after = placed([P, PACK - 2, M], F32, "after", at_raw10)
-        for t in range(2, PACK):
-            pick(after[:, t - 2, :], h1[t])
-        squares = placed([P, PACK - 1, M], F32, "squares", at_h13)
-        square("v", squares[:, 0, :], before[:, 1, :])
-        square("v", squares[:, 1:, :], after[:])
+        after = placed([P, PACK - AHEAD, M], F32, "after", at_raw10)
+        for t in range(AHEAD, PACK):
+            pick(after[:, t - AHEAD, :], h1[t])
+        squares = placed([P, PACK - ON_SCALAR, M], F32, "squares", at_h13)
+        for t in range(ON_SCALAR, AHEAD):
+            nc.vector.tensor_tensor(squares[:, t - ON_SCALAR, :], before[:, t, :], before[:, t, :], ALU.mult)
+        nc.vector.tensor_tensor(squares[:, AHEAD - ON_SCALAR:, :], after[:], after[:], ALU.mult)
 
-        spare = new_tile([P, 1, PASS], F32, "spare")
-        log_bt0 = [spare[:, i, :] if i < 1 else log_a1[:, i, :] for i in range(CHUNKS)]
+        z_codes, z_planes = {}, {}
+
+        def difference(diff, log_bt, log_a, i):
+            log_b = bank([P, PACK, P], "log_b", CHUNKS + i)
+            for t in range(PACK):
+                nc.tensor.transpose(log_b[:, t, :], log_bt[:, t * P:(t + 1) * P], ident[:])
+            nc.vector.tensor_tensor(
+                diff,
+                log_b[:].rearrange("p (u e) m -> p u m e", u=PAIRS),
+                log_a[:, :, i * P:(i + 1) * P].rearrange("p (u e) m -> p u m e", u=PAIRS),
+                ALU.subtract,
+            )
+
+        def round_z(blk, i, diff):
+            z = new_tile([P, PACK * P], BF16, "z%d_%d" % (blk, i * P))
+            nc.vector.tensor_tensor(
+                z[:].rearrange("p (m u e) -> p m u e", u=PAIRS, e=2),
+                diff.rearrange("p u m e -> p m u e"),
+                gain_sb[:, blk, :].rearrange("p (u e) -> p u e", u=PAIRS).unsqueeze(1).to_broadcast([P, P, PAIRS, 2]),
+                ALU.mult,
+            )
+            return blk, i, z
+
+        def quantise_z(blk, i, z):
+            z_codes[blk, i] = new_tile([P, P], U32, "z_codes%d_%d" % (blk, i * P))
+            z_planes[blk, i] = new_tile([P, P], U8, "z_planes%d_%d" % (blk, i * P))
+            nc.vector.quantize_mx(out=z_codes[blk, i][:].bitcast(FP8X4), scales=z_planes[blk, i][:], in_=z[:])
+
+        spare = new_tile([P, ON_SCALAR, PASS], F32, "spare")
+        log_bt0 = [spare[:, i, :] if i < ON_SCALAR else log_a1[:, i, :] for i in range(CHUNKS)]
         bt0 = [bank([P, BANK], "bt", i) for i in range(CHUNKS)]
         for a, i in itertools.product(range(PASSES2), range(CHUNKS)):
             project(0, i, a, bt0[i])
-        gate = placed([P, PASS], F32, "gate", at_diff0)
+        first_squares = placed([P, PASS], F32, "first_squares", at_diff0)
         for i in range(CHUNKS):
-            log_b_turned(log_bt0[i], bt0[i], gate[:] if i == 0 else None)
-        diff0 = placed([P, 2, M, 2], F32, "diff0", at_diff0)
+            log_of_bt(log_bt0[i], first_squares[:] if i == 0 else log_bt0[i], bt0[i])
+
+        diff0 = placed([P, PAIRS, M, 2], F32, "diff0", at_diff0)
         rounded = None
         for i in range(CHUNKS):
-            subtract(log_bt0[i], log_a0, i, CHUNKS + i, diff0[:, :, i * P:(i + 1) * P, :])
-            if i % 1 == 0 and rounded:
+            diff = diff0[:, :, i * P:(i + 1) * P, :]
+            difference(diff, log_bt0[i], log_a0, i)
+            if rounded:
                 quantise_z(*rounded)
-            if i % 1 == 1 - 1:
-                m0 = (i + 1 - 1) * P
-                rounded = apply_gain(0, diff0[:, :, m0:(i + 1) * P, :], m0, 1 * P)
+            rounded = round_z(0, i, diff)
+
         log_bt1 = new_tile([P, CHUNKS, PASS], F32, "log_bt1")
         for i in range(CHUNKS):
             bt = bank([P, BANK], "bt", i)
             for a in range(PASSES2):
                 project(1, i, a, bt)
-            log_b_turned(log_bt1[:, i, :], bt)
-            if i == 2 - 1:
-                log_of(log_a1[:, 1:, :], squares[:])
+            log_of_bt(log_bt1[:, i, :], log_bt1[:, i, :], bt)
+            if i == CHUNKS // 2 - 1:
+                log_half_plus(log_a1[:, ON_SCALAR:, :], squares[:])
         for i in range(CHUNKS):
-            diff = new_tile([P, 2, P, 2], F32, "diff1%d" % i, "diff1%d" % min(i, 2))
-            subtract(log_bt1[:, i, :], log_a1, i, CHUNKS + i, diff[:])
+            diff1 = new_tile([P, PAIRS, P, 2], F32, "diff1%d" % i, "diff1%d" % min(i, CHUNKS - 2))
+            difference(diff1[:], log_bt1[:, i, :], log_a1, i)
             quantise_z(*rounded)
-            rounded = apply_gain(1, diff[:], i * P, P)
+            rounded = round_z(1, i, diff1[:])
         quantise_z(*rounded)
 
         out_view = out.rearrange("(g p) m -> p g m", p=P)
         levels = new_tile([P, CHUNKS, N // P, P], F32, "levels", "half")
 
-        def alarm(i, groups, b):
-            y = bank([P, len(groups), P], "y", b)
-            for blk, g in itertools.product(range(BLOCKS), groups):
-                cols = slice(blk * N + g * P, blk * N + (g + 1) * P)
+        def alarm(i, g0, groups, b):
+            y = bank([P, groups, P], "y", b)
+            for blk, g in itertools.product(range(BLOCKS), range(groups)):
+                cols = slice(blk * N + (g0 + g) * P, blk * N + (g0 + g + 1) * P)
                 nc.tensor.matmul_mx(
-                    out=y[:, g - groups[0], :],
+                    out=y[:, g, :],
                     lhsT=w3_sb[:, cols].bitcast(FP8X4),
                     lhsT_scale=w3_planes[:, cols],
-                    rhs=z_codes[blk, i].bitcast(FP8X4),
-                    rhs_scale=z_planes[blk, i],
-                    start=(blk == 0 and g == groups[0]), stop=(blk == BLOCKS - 1 and g == groups[-1]),
+                    rhs=z_codes[blk, i][:].bitcast(FP8X4),
+                    rhs_scale=z_planes[blk, i][:],
+                    start=(blk == 0 and g == 0), stop=(blk == BLOCKS - 1 and g == groups - 1),
                 )
-            rows = slice(groups[0], groups[-1] + 1)
-            nc.scalar.activation(out=levels[:, i, rows], in_=y[:], func=ACT.Sigmoid)
-            nc.sync.dma_start(out=out_view[:, rows, i * P:(i + 1) * P], in_=levels[:, i, rows])
+            nc.scalar.activation(out=levels[:, i, g0:g0 + groups], in_=y[:], func=ACT.Sigmoid)
+            nc.sync.dma_start(out=out_view[:, g0:g0 + groups, i * P:(i + 1) * P], in_=levels[:, i, g0:g0 + groups])
 
         for i in range(CHUNKS - 1):
-            alarm(i, range(N // P), i)
-        alarm(CHUNKS - 1, range(0, 2), CHUNKS - 1)
-        alarm(CHUNKS - 1, range(2, 4), CHUNKS)
+            alarm(i, 0, N // P, i)
+        for piece in range(2):
+            alarm(CHUNKS - 1, piece * N // P // 2, N // P // 2, CHUNKS - 1 + piece)

@@ -182,6 +182,11 @@ def tile_list_ransomware_alarm_levels_kernel(
             )
             quantise_rounded(blk, a, 0, rounded, PACK)
 
+        def round_on_gpsimd(rounded, raw):
+            nc.gpsimd.tensor_scalar(
+                rounded.rearrange("p m e j -> p e m j"), raw.rearrange("p m e j -> p e m j"), 1.0, 0.0, ALU.mult, ALU.add
+            )
+
         def quantise_w1_by_pairs(blk, a, copies, rounded):
             pairs = w1_raw[blk, a][:].rearrange("p j (m u e) -> p u m e j", u=PAIRS, e=2)
             for u in range(PAIRS):
@@ -262,7 +267,7 @@ def tile_list_ransomware_alarm_levels_kernel(
         for t in range(1, EARLY):
             pick(early[:, t, :], h0[t])
         quantise_w1_by_pairs(
-            1, 1, (nc.vector.tensor_copy, nc.vector.tensor_copy),
+            1, 1, (round_on_gpsimd, round_on_gpsimd),
             [placed([P, 2 * PASS], BF16, "w1_bf11%d" % u, at_rounded11 + 2 * u) for u in range(PAIRS)],
         )
         w2_sb.append(load_w2(1, at_raw11 + 5))

@@ -31,11 +31,9 @@ GROUP = 16
 PASSES, PASSES2, BLOCKS = K // PASS, K2 // PASS, H // PASS
 HALVES = S // BANK
 CHUNKS = M // P
-PAIRS = PACK // 2
 KIB = 1024
-EARLY = 3
+PAIRS = PACK // 2
 AHEAD = 2
-ON_SCALAR = 1
 
 
 def words_of(packed):
@@ -61,28 +59,26 @@ def tile_list_ransomware_alarm_levels_kernel(
         def bank(shape, name, b):
             return psum.tile(shape, F32, name=name, tag="bank%d" % b)
 
-        at_tab0 = 0
+        at_raw00 = 0
         at_raw10 = 0
-        at_v2_planes = 8
-        at_raw11 = 10
-        at_tab1 = 18
-        at_raw01 = 34
-        at_raw00 = 42
-        at_rounded01 = 50
-        at_rounded00 = 54
-        at_early = 58
-        at_rounded10 = 64
-        at_rounded11 = 68
-        at_h11 = 79
-        at_diff0 = 83
-        at_h13 = 91
+        at_v2_planes = 9
+        at_rounded00 = 10
+        at_raw11 = 12
+        at_tab1 = 20
+        at_raw01 = 36
+        at_rounded01 = 44
+        at_h03 = 48
+        at_h11 = 52
+        at_rounded11 = 56
+        at_h02 = 64
+        at_tab0 = 68
 
         offs_sb = sbuf.tile([P, S // GROUP], U16, name="offs_sb")
         pos_sb = sbuf.tile([P, M // GROUP], U16, name="pos_sb")
         offs2_sb = sbuf.tile([P, M // GROUP], U16, name="offs2_sb")
 
         tab_sc = new_tile([P, T], U8, "tab_sc")
-        tab2_sc = placed([P, T2], U8, "tab2_sc", at_raw01)
+        tab2_sc = new_tile([P, T2], U8, "tab2_sc")
         v_planes = new_tile([P, PASSES * S], U8, "v_planes")
         top, top2 = P - SCALE_ROWS * PASSES, P - SCALE_ROWS * PASSES2
         half = new_tile([P, 1], F32, "half")
@@ -90,6 +86,9 @@ def tile_list_ransomware_alarm_levels_kernel(
         nc.vector.memset(tab_sc[:].bitcast(I32)[:top], 0)
         nc.vector.memset(tab2_sc[:].bitcast(I32)[:top2], 0)
         nc.vector.memset(v_planes[:].bitcast(I32), 0)
+
+        warm_up = new_tile([P, 1], F32, "warm_up")
+        nc.scalar.activation(out=warm_up[:], in_=half[:], func=ACT.Ln)
 
         def load_w1(blk, a, kib):
             raw = placed([P, PACK, PASS], F32, "w1_raw%d%d" % (blk, a), kib)
@@ -138,6 +137,7 @@ def tile_list_ransomware_alarm_levels_kernel(
         nc.sync.dma_start(pos_sb[:], pos1)
         w1_raw[0, 0] = load_w1(0, 0, at_raw00)
         tab_sb.append(load_words(tab_words[1], "tab1", at_tab1))
+        w1_raw[0, 1] = load_w1(0, 1, at_raw01)
 
         ident = new_tile([P, P], F32, "ident")
         make_identity(nc, ident[:])
@@ -147,7 +147,6 @@ def tile_list_ransomware_alarm_levels_kernel(
         carry_planes(v_planes, v_sc, top, PASSES)
         v2_sc = new_tile([P, M], U8, "v2_sc")
         nc.vector.tensor_copy(v2_sc[:], tab2_sc[:].indirect(offs2_sb[:]))
-        w1_raw[0, 1] = load_w1(0, 1, at_raw01)
 
         v_codes = {}
 
@@ -158,55 +157,55 @@ def tile_list_ransomware_alarm_levels_kernel(
                 nc.vector.tensor_copy(v_codes[a, u][:], tab_sb[a][:].bitcast(U32).indirect(entries))
 
         gather_v(0)
-        w1_raw[1, 0] = load_w1(1, 0, at_raw10)
-        w1_raw[1, 1] = load_w1(1, 1, at_raw11)
-        v2_planes = placed([P, PASSES2 * M], U8, "v2_planes", at_v2_planes)
-        nc.vector.memset(v2_planes[:].bitcast(I32), 0)
-        carry_planes(v2_planes, v2_sc, top2, PASSES2)
-        gather_v(1)
 
         w1_codes, w1_planes = {}, {}
-
-        def quantise_rounded(blk, a, t0, rounded, sets):
-            codes = new_tile([P, sets * P], U32, "w1_codes%d%d%d" % (blk, a, t0))
-            planes = new_tile([P, sets * P], U8, "w1_planes%d%d%d" % (blk, a, t0))
-            nc.vector.quantize_mx(out=codes[:].bitcast(FP8X4), scales=planes[:], in_=rounded[:])
-            for e in range(sets):
-                w1_codes[blk, a, t0 + e] = codes[:, e * P:(e + 1) * P]
-                w1_planes[blk, a, t0 + e] = planes[:, e * P:(e + 1) * P]
-
-        def quantise_w1(blk, a, copy, rounded):
-            copy(
-                rounded[:].rearrange("p (t m j) -> p m t j", t=PACK, j=PACK),
-                w1_raw[blk, a][:].rearrange("p j (m t) -> p m t j", t=PACK),
-            )
-            quantise_rounded(blk, a, 0, rounded, PACK)
 
         def round_on_gpsimd(rounded, raw):
             nc.gpsimd.tensor_scalar(
                 rounded.rearrange("p m e j -> p e m j"), raw.rearrange("p m e j -> p e m j"), 1.0, 0.0, ALU.mult, ALU.add
             )
 
-        def quantise_w1_by_pairs(blk, a, copies, rounded):
+        def round_block(blk, a, copy, rounded):
+            copy(
+                rounded[:].rearrange("p (t m j) -> p m t j", t=PACK, j=PACK),
+                w1_raw[blk, a][:].rearrange("p j (m t) -> p m t j", t=PACK),
+            )
+
+        def round_pair(blk, a, u, copy, rounded):
             pairs = w1_raw[blk, a][:].rearrange("p j (m u e) -> p u m e j", u=PAIRS, e=2)
-            for u in range(PAIRS):
-                copies[u](rounded[u][:].rearrange("p (e m j) -> p m e j", e=2, j=PACK), pairs[:, u])
-            for u in range(PAIRS):
-                quantise_rounded(blk, a, 2 * u, rounded[u], 2)
+            copy(rounded.rearrange("p (e m j) -> p m e j", e=2, j=PACK), pairs[:, u])
 
-        quantise_w1(0, 0, nc.scalar.copy, placed([P, PACK * PASS], BF16, "w1_bf00", at_rounded00))
-        tab2_sb = [load_words(tab2_words[0], "tab2_0", at_raw00)]
-        w2_planes = placed([P, PASSES2 * H], U8, "w2_planes", at_rounded00)
-        nc.gpsimd.memset(w2_planes[:].bitcast(I32), 0)
-        load_planes(w2_planes, w2_scales, PASSES2)
-        tab2_sb.append(load_words(tab2_words[1], "tab2_1", at_tab1))
-        quantise_w1_by_pairs(
-            0, 1, (nc.vector.tensor_copy, nc.scalar.copy),
-            [placed([P, 2 * PASS], BF16, "w1_bf01%d" % u, at_rounded01 + 2 * u) for u in range(PAIRS)],
-        )
+        def quantise_w1(blk, a, t0, rounded, sets, codes):
+            planes = new_tile([P, sets * P], U8, "w1_planes%d%d%d" % (blk, a, t0))
+            nc.vector.quantize_mx(out=codes[:].bitcast(FP8X4), scales=planes[:], in_=rounded)
+            for e in range(sets):
+                w1_codes[blk, a, t0 + e] = codes[:, e * P:(e + 1) * P]
+                w1_planes[blk, a, t0 + e] = planes[:, e * P:(e + 1) * P]
+
+        def codes_tile(blk, a, t0, sets):
+            return new_tile([P, sets * P], U32, "w1_codes%d%d%d" % (blk, a, t0))
+
+        rounded = placed([P, PACK * PASS], BF16, "w1_bf00", at_rounded00)
+        round_block(0, 0, nc.scalar.copy, rounded)
+        w1_raw[1, 0] = load_w1(1, 0, at_raw10)
+        quantise_w1(0, 0, 0, rounded[:], PACK, codes_tile(0, 0, 0, PACK))
+        w1_raw[1, 1] = load_w1(1, 1, at_raw11)
+        v2_planes = placed([P, PASSES2 * M], U8, "v2_planes", at_v2_planes)
+        nc.vector.memset(v2_planes[:].bitcast(I32), 0)
+        carry_planes(v2_planes, v2_sc, top2, PASSES2)
+        gather_v(1)
+        tab2_sb = [load_words(tab2_words[a], "tab2_%d" % a, at_tab1 + 8 * a) for a in range(2)]
+        rounded = [placed([P, 2 * PASS], BF16, "w1_bf010", at_rounded01), new_tile([P, 2 * PASS], BF16, "w1_bf011")]
+        for u, copy in enumerate((nc.vector.tensor_copy, nc.scalar.copy)):
+            round_pair(0, 1, u, copy, rounded[u][:])
+        for u in range(PAIRS):
+            quantise_w1(0, 1, 2 * u, rounded[u][:], 2, codes_tile(0, 1, 2 * u, 2))
         w2_sb = [load_w2(0, at_raw01)]
+        w2_planes = placed([P, PASSES2 * H], U8, "w2_planes", at_rounded01)
+        nc.vector.memset(w2_planes[:].bitcast(I32), 0)
+        load_planes(w2_planes, w2_scales, PASSES2)
 
-        def first_stage(blk, places):
+        def first_stage(blk, passes, places):
             h = [
                 placed([P, S], F32, "h%d%d" % (blk, t), places[t]) if t in places
                 else new_tile([P, S], F32, "h%d%d" % (blk, t))
@@ -214,14 +213,14 @@ def tile_list_ransomware_alarm_levels_kernel(
             ]
             for t, u in itertools.product(range(PACK), range(HALVES)):
                 acc = bank([P, BANK], "acc", HALVES * t + u)
-                for a in range(PASSES):
+                for a in passes:
                     nc.tensor.matmul_mx(
                         out=acc[:],
                         lhsT=w1_codes[blk, a, t].bitcast(FP8X4),
                         lhsT_scale=w1_planes[blk, a, t],
                         rhs=v_codes[a, u][:].bitcast(FP8X4),
                         rhs_scale=v_planes[:, a * S + u * BANK:a * S + (u + 1) * BANK],
-                        start=(a == 0), stop=(a == PASSES - 1),
+                        start=(a == passes[0]), stop=(a == passes[-1]),
                     )
                 nc.scalar.copy(h[t][:, u * BANK:(u + 1) * BANK], acc[:])
             return h
@@ -232,13 +231,12 @@ def tile_list_ransomware_alarm_levels_kernel(
         def log_half_plus(logs, squares):
             nc.scalar.activation(out=logs, in_=squares, func=ACT.Ln, bias=half[:])
 
-        def log_on_scalar(logs, values):
-            nc.scalar.activation(out=logs, in_=values, func=ACT.Square)
-            log_half_plus(logs, logs)
+        def square_on_gpsimd(squares, values):
+            nc.gpsimd.tensor_tensor(squares, values, values, ALU.mult)
 
-        def gather_v2(a, codes):
-            nc.vector.tensor_copy(codes[:], tab2_sb[a][:].bitcast(U32).indirect(offs2_sb[:]))
-            return codes
+        def gather_v2(a, codes, first, count):
+            entries = offs2_sb[:, first // GROUP:(first + count) // GROUP]
+            nc.vector.tensor_copy(codes[:, first:first + count], tab2_sb[a][:].bitcast(U32).indirect(entries))
 
         def project(blk, i, a, bt):
             c0 = a * H + blk * PASS
@@ -251,126 +249,129 @@ def tile_list_ransomware_alarm_levels_kernel(
                 start=(a == 0), stop=(a == PASSES2 - 1),
             )
 
-        def log_of_bt(log_bt, squares, bt):
+        def square_of_bt(squares, bt):
             nc.scalar.activation(
                 out=squares.rearrange("m (t p) -> m t p", t=PACK),
                 in_=bt[:].rearrange("m (p t) -> m t p", t=PACK),
                 func=ACT.Square,
             )
-            log_half_plus(log_bt, squares)
 
-        h0 = first_stage(0, {})
-        early = placed([P, EARLY, M], F32, "early", at_early)
-        pick(early[:, 0, :], h0[0])
-        quantise_w1(1, 0, nc.vector.tensor_copy, placed([P, PACK * PASS], BF16, "w1_bf10", at_rounded10))
+        h0 = first_stage(0, (1, 0), {2: at_h02, 3: at_h03})
+        rounded = new_tile([P, PACK * PASS], BF16, "w1_bf10")
+        round_block(1, 0, nc.vector.tensor_copy, rounded)
         tab2_sb.append(load_words(tab2_words[2], "tab2_2", at_raw10))
-        for t in range(1, EARLY):
-            pick(early[:, t, :], h0[t])
-        quantise_w1_by_pairs(
-            1, 1, (round_on_gpsimd, round_on_gpsimd),
-            [placed([P, 2 * PASS], BF16, "w1_bf11%d" % u, at_rounded11 + 2 * u) for u in range(PAIRS)],
-        )
+        a0 = [new_tile([P, M], F32, "a0%d" % t) for t in range(PACK - 1)]
+        pick(a0[0][:], h0[0])
+        quantise_w1(1, 0, 0, rounded[:], PACK, codes_tile(1, 0, 0, PACK))
+        rounded = placed([P, PACK * PASS], BF16, "w1_bf11", at_rounded11)
+        for u in range(PAIRS):
+            round_pair(1, 1, u, round_on_gpsimd, rounded[:, u * 2 * PASS:(u + 1) * 2 * PASS])
+        for t in range(1, PACK - 1):
+            pick(a0[t][:], h0[t])
+        quantise_w1(1, 1, 0, rounded[:], PACK, placed([P, PASS], U32, "w1_codes11", at_h02 + 2))
+        a0.append(placed([P, M], F32, "a03", at_rounded11))
+        pick(a0[PACK - 1][:], h0[PACK - 1])
+        square_on_gpsimd(a0[PACK - 1][:], a0[PACK - 1][:])
         w2_sb.append(load_w2(1, at_raw11 + 5))
         w3_sb = placed([P, BLOCKS * N], I32, "w3_sb", at_raw11)
         nc.sync.dma_start(
             out=w3_sb[:].rearrange("p (b c) -> p b c", b=BLOCKS),
             in_=w3_words.rearrange("b p c i -> p b (c i)").bitcast(I32),
         )
-        gain_sb = placed([P, BLOCKS, PACK], F32, "gain_sb", at_rounded11)
+        gain_sb = placed([P, BLOCKS, PACK], F32, "gain_sb", at_h02)
         nc.sync.dma_start(out=gain_sb[:], in_=gain.rearrange("(b p t) -> p b t", b=BLOCKS, t=PACK))
-        w3_planes = placed([P, BLOCKS * N], U8, "w3_planes", at_raw11 + 4)
-        nc.vector.memset(w3_planes[:].bitcast(I32), 0)
+        w3_planes = placed([P, BLOCKS * N], U8, "w3_planes", at_h03)
+        nc.gpsimd.memset(w3_planes[:].bitcast(I32), 0)
         load_planes(w3_planes, w3_scales, BLOCKS)
-        late = placed([P, PACK - EARLY, M], F32, "late", at_rounded11 + 3)
-        for t in range(EARLY, PACK):
-            pick(late[:, t - EARLY, :], h0[t])
 
-        log_a0 = new_tile([P, PACK, M], F32, "log_a0")
-        for t in range(EARLY):
-            log_on_scalar(log_a0[:, t, :], early[:, t, :])
-        h1 = first_stage(1, {AHEAD - 1: at_h11, PACK - 1: at_h13})
-        for t in range(EARLY, PACK):
-            log_on_scalar(log_a0[:, t, :], late[:, t - EARLY, :])
-        v2_codes = [
-            gather_v2(0, placed([P, M], U32, "v2_0", at_rounded11 + 1)),
-            gather_v2(1, new_tile([P, M], U32, "v2_1")),
-        ]
+        log_a = [new_tile([P, PACK, M], F32, "log_a%d" % blk) for blk in range(BLOCKS)]
+        for t in range(PACK - 1):
+            nc.scalar.activation(out=log_a[0][:, t, :], in_=a0[t][:], func=ACT.Square)
+            log_half_plus(log_a[0][:, t, :], log_a[0][:, t, :])
+        h1 = first_stage(1, (0, 1), {AHEAD - 1: at_h11})
+        log_half_plus(log_a[0][:, PACK - 1, :], a0[PACK - 1][:])
 
-        log_a1 = new_tile([P, PACK, M], F32, "log_a1")
+        v2_codes = [placed([P, M], U32, "v2_0", at_rounded11 + 2), new_tile([P, M], U32, "v2_1")]
+        for a in range(2):
+            gather_v2(a, v2_codes[a], 0, M)
         before = new_tile([P, AHEAD, M], F32, "before")
+        squares = new_tile([P, PACK, M], F32, "squares")
         for t in range(AHEAD):
             pick(before[:, t, :], h1[t])
-        for t in range(ON_SCALAR):
-            log_on_scalar(log_a1[:, t, :], before[:, t, :])
-        v2_codes.append(gather_v2(2, placed([P, M], U32, "v2_2", at_h11)))
+            square_on_gpsimd(squares[:, t, :], before[:, t, :])
+        log_half_plus(log_a[1][:, 0, :], squares[:, 0, :])
+        v2_codes.append(placed([P, M], U32, "v2_2", at_h11))
+        for first in range(0, M, M // 2):
+            gather_v2(2, v2_codes[2], first, M // 2)
         after = placed([P, PACK - AHEAD, M], F32, "after", at_raw10)
-        for t in range(AHEAD, PACK):
-            pick(after[:, t - AHEAD, :], h1[t])
-        squares = placed([P, PACK - ON_SCALAR, M], F32, "squares", at_h13)
-        for t in range(ON_SCALAR, AHEAD):
-            nc.vector.tensor_tensor(squares[:, t - ON_SCALAR, :], before[:, t, :], before[:, t, :], ALU.mult)
-        nc.vector.tensor_tensor(squares[:, AHEAD - ON_SCALAR:, :], after[:], after[:], ALU.mult)
+        for t in range(PACK - AHEAD):
+            pick(after[:, t, :], h1[AHEAD + t])
+            square_on_gpsimd(squares[:, AHEAD + t, :], after[:, t, :])
 
         z_codes, z_planes = {}, {}
 
-        def difference(diff, log_bt, log_a, i):
+        def difference(blk, i, log_bt):
             log_b = bank([P, PACK, P], "log_b", CHUNKS + i)
             for t in range(PACK):
                 nc.tensor.transpose(log_b[:, t, :], log_bt[:, t * P:(t + 1) * P], ident[:])
+            diff = new_tile([P, PAIRS, P, 2], F32, "diff%d%d" % (blk, i))
             nc.vector.tensor_tensor(
-                diff,
+                diff[:],
                 log_b[:].rearrange("p (u e) m -> p u m e", u=PAIRS),
-                log_a[:, :, i * P:(i + 1) * P].rearrange("p (u e) m -> p u m e", u=PAIRS),
+                log_a[blk][:, :, i * P:(i + 1) * P].rearrange("p (u e) m -> p u m e", u=PAIRS),
                 ALU.subtract,
             )
+            return diff
 
         def round_z(blk, i, diff):
-            z = new_tile([P, PACK * P], BF16, "z%d_%d" % (blk, i * P))
+            z = new_tile([P, PASS], BF16, "z%d%d" % (blk, i))
             nc.vector.tensor_tensor(
                 z[:].rearrange("p (m u e) -> p m u e", u=PAIRS, e=2),
-                diff.rearrange("p u m e -> p m u e"),
+                diff[:].rearrange("p u m e -> p m u e"),
                 gain_sb[:, blk, :].rearrange("p (u e) -> p u e", u=PAIRS).unsqueeze(1).to_broadcast([P, P, PAIRS, 2]),
                 ALU.mult,
             )
             return blk, i, z
 
         def quantise_z(blk, i, z):
-            z_codes[blk, i] = new_tile([P, P], U32, "z_codes%d_%d" % (blk, i * P))
-            z_planes[blk, i] = new_tile([P, P], U8, "z_planes%d_%d" % (blk, i * P))
-            nc.vector.quantize_mx(out=z_codes[blk, i][:].bitcast(FP8X4), scales=z_planes[blk, i][:], in_=z[:])
+            z_codes[blk, i] = new_tile([P, P], U32, "z_codes%d%d" % (blk, i))[:]
+            z_planes[blk, i] = new_tile([P, P], U8, "z_planes%d%d" % (blk, i))[:]
+            nc.vector.quantize_mx(out=z_codes[blk, i].bitcast(FP8X4), scales=z_planes[blk, i], in_=z[:])
 
-        spare = new_tile([P, ON_SCALAR, PASS], F32, "spare")
-        log_bt0 = [spare[:, i, :] if i < ON_SCALAR else log_a1[:, i, :] for i in range(CHUNKS)]
+        log_bt = [new_tile([P, CHUNKS, PASS], F32, "log_bt%d" % blk) for blk in range(BLOCKS)]
         bt0 = [bank([P, BANK], "bt", i) for i in range(CHUNKS)]
         for a, i in itertools.product(range(PASSES2), range(CHUNKS)):
             project(0, i, a, bt0[i])
-        first_squares = placed([P, PASS], F32, "first_squares", at_diff0)
-        for i in range(CHUNKS):
-            log_of_bt(log_bt0[i], first_squares[:] if i == 0 else log_bt0[i], bt0[i])
+        chunk_pairs = [(i, i + 1) for i in range(0, CHUNKS, 2)]
 
-        diff0 = placed([P, PAIRS, M, 2], F32, "diff0", at_diff0)
-        rounded = None
-        for i in range(CHUNKS):
-            diff = diff0[:, :, i * P:(i + 1) * P, :]
-            difference(diff, log_bt0[i], log_a0, i)
-            if rounded:
-                quantise_z(*rounded)
-            rounded = round_z(0, i, diff)
+        def logs_of_bt(blk, pair, banks):
+            for i in pair:
+                square_of_bt(log_bt[blk][:, i, :], banks[i])
+            for i in pair:
+                log_half_plus(log_bt[blk][:, i, :], log_bt[blk][:, i, :])
 
-        log_bt1 = new_tile([P, CHUNKS, PASS], F32, "log_bt1")
-        for i in range(CHUNKS):
-            bt = bank([P, BANK], "bt", i)
-            for a in range(PASSES2):
-                project(1, i, a, bt)
-            log_of_bt(log_bt1[:, i, :], log_bt1[:, i, :], bt)
-            if i == CHUNKS // 2 - 1:
-                log_half_plus(log_a1[:, ON_SCALAR:, :], squares[:])
-        for i in range(CHUNKS):
-            diff1 = new_tile([P, PAIRS, P, 2], F32, "diff1%d" % i, "diff1%d" % min(i, CHUNKS - 2))
-            difference(diff1[:], log_bt1[:, i, :], log_a1, i)
-            quantise_z(*rounded)
-            rounded = round_z(1, i, diff1[:])
-        quantise_z(*rounded)
+        def z_of(blk, pair):
+            diffs = [difference(blk, i, log_bt[blk][:, i, :]) for i in pair]
+            for z in [round_z(blk, i, diff) for i, diff in zip(pair, diffs)]:
+                quantise_z(*z)
+
+        for pair in chunk_pairs:
+            logs_of_bt(0, pair, bt0)
+            z_of(0, pair)
+        log_half_plus(log_a[1][:, 1:, :], squares[:, 1:, :])
+        bt1 = {}
+        for pair in chunk_pairs:
+            for i in pair:
+                if i < CHUNKS - 1:
+                    bt1[i] = bank([P, BANK], "bt", i)
+                    for a in range(PASSES2):
+                        project(1, i, a, bt1[i])
+                else:
+                    bt1[i] = bank([P, BANK], "bt", 0)
+                    for a in range(PASSES2):
+                        project(1, i, a, bt1[i])
+            logs_of_bt(1, pair, bt1)
+            z_of(1, pair)
 
         out_view = out.rearrange("(g p) m -> p g m", p=P)
         levels = new_tile([P, CHUNKS, N // P, P], F32, "levels", "half")
@@ -383,14 +384,14 @@ def tile_list_ransomware_alarm_levels_kernel(
                     out=y[:, g, :],
                     lhsT=w3_sb[:, cols].bitcast(FP8X4),
                     lhsT_scale=w3_planes[:, cols],
-                    rhs=z_codes[blk, i][:].bitcast(FP8X4),
-                    rhs_scale=z_planes[blk, i][:],
+                    rhs=z_codes[blk, i].bitcast(FP8X4),
+                    rhs_scale=z_planes[blk, i],
                     start=(blk == 0 and g == 0), stop=(blk == BLOCKS - 1 and g == groups - 1),
                 )
             nc.scalar.activation(out=levels[:, i, g0:g0 + groups], in_=y[:], func=ACT.Sigmoid)
             nc.sync.dma_start(out=out_view[:, g0:g0 + groups, i * P:(i + 1) * P], in_=levels[:, i, g0:g0 + groups])
 
         for i in range(CHUNKS - 1):
-            alarm(i, 0, N // P, i)
+            alarm(i, 0, N // P, CHUNKS + i)
         for piece in range(2):
-            alarm(CHUNKS - 1, piece * N // P // 2, N // P // 2, CHUNKS - 1 + piece)
+            alarm(CHUNKS - 1, piece * N // P // 2, N // P // 2, 2 * CHUNKS - 1 - piece * CHUNKS)

@@ -78,7 +78,7 @@ def tile_list_ransomware_alarm_levels_kernel(
         offs2_sb = sbuf.tile([P, M // GROUP], U16, name="offs2_sb")
 
         tab_sc = new_tile([P, T], U8, "tab_sc")
-        tab2_sc = new_tile([P, T2], U8, "tab2_sc")
+        tab2_sc = placed([P, T2], U8, "tab2_sc", at_raw01)
         v_planes = new_tile([P, PASSES * S], U8, "v_planes")
         top, top2 = P - SCALE_ROWS * PASSES, P - SCALE_ROWS * PASSES2
         half = new_tile([P, 1], F32, "half")
@@ -137,7 +137,6 @@ def tile_list_ransomware_alarm_levels_kernel(
         nc.sync.dma_start(pos_sb[:], pos1)
         w1_raw[0, 0] = load_w1(0, 0, at_raw00)
         tab_sb.append(load_words(tab_words[1], "tab1", at_tab1))
-        w1_raw[0, 1] = load_w1(0, 1, at_raw01)
 
         ident = new_tile([P, P], F32, "ident")
         make_identity(nc, ident[:])
@@ -147,6 +146,7 @@ def tile_list_ransomware_alarm_levels_kernel(
         carry_planes(v_planes, v_sc, top, PASSES)
         v2_sc = new_tile([P, M], U8, "v2_sc")
         nc.vector.tensor_copy(v2_sc[:], tab2_sc[:].indirect(offs2_sb[:]))
+        w1_raw[0, 1] = load_w1(0, 1, at_raw01)
 
         v_codes = {}
 
@@ -256,20 +256,21 @@ def tile_list_ransomware_alarm_levels_kernel(
                 func=ACT.Square,
             )
 
-        h0 = first_stage(0, (1, 0), {2: at_h02, 3: at_h03})
+        h0 = first_stage(0, (0, 1), {2: at_h02, 3: at_h03})
         rounded = new_tile([P, PACK * PASS], BF16, "w1_bf10")
         round_block(1, 0, nc.vector.tensor_copy, rounded)
         tab2_sb.append(load_words(tab2_words[2], "tab2_2", at_raw10))
         a0 = [new_tile([P, M], F32, "a0%d" % t) for t in range(PACK - 1)]
         pick(a0[0][:], h0[0])
         quantise_w1(1, 0, 0, rounded[:], PACK, codes_tile(1, 0, 0, PACK))
-        rounded = placed([P, PACK * PASS], BF16, "w1_bf11", at_rounded11)
+        rounded = [placed([P, 2 * PASS], BF16, "w1_bf11%d" % u, at_rounded11 + 2 * u) for u in range(PAIRS)]
+        for u, copy in enumerate((nc.vector.tensor_copy, nc.scalar.copy)):
+            round_pair(1, 1, u, copy, rounded[u][:])
+            pick(a0[1 + u][:], h0[1 + u])
+        square_on_gpsimd(a0[2][:], a0[2][:])
         for u in range(PAIRS):
-            round_pair(1, 1, u, round_on_gpsimd, rounded[:, u * 2 * PASS:(u + 1) * 2 * PASS])
-        for t in range(1, PACK - 1):
-            pick(a0[t][:], h0[t])
-        quantise_w1(1, 1, 0, rounded[:], PACK, placed([P, PASS], U32, "w1_codes11", at_h02 + 2))
-        a0.append(placed([P, M], F32, "a03", at_rounded11))
+            quantise_w1(1, 1, 2 * u, rounded[u][:], 2, codes_tile(1, 1, 2 * u, 2))
+        a0.append(new_tile([P, M], F32, "a03"))
         pick(a0[PACK - 1][:], h0[PACK - 1])
         square_on_gpsimd(a0[PACK - 1][:], a0[PACK - 1][:])
         w2_sb.append(load_w2(1, at_raw11 + 5))
@@ -285,28 +286,30 @@ def tile_list_ransomware_alarm_levels_kernel(
         load_planes(w3_planes, w3_scales, BLOCKS)
 
         log_a = [new_tile([P, PACK, M], F32, "log_a%d" % blk) for blk in range(BLOCKS)]
-        for t in range(PACK - 1):
+        for t in range(2):
             nc.scalar.activation(out=log_a[0][:, t, :], in_=a0[t][:], func=ACT.Square)
             log_half_plus(log_a[0][:, t, :], log_a[0][:, t, :])
         h1 = first_stage(1, (0, 1), {AHEAD - 1: at_h11})
-        log_half_plus(log_a[0][:, PACK - 1, :], a0[PACK - 1][:])
 
-        v2_codes = [placed([P, M], U32, "v2_0", at_rounded11 + 2), new_tile([P, M], U32, "v2_1")]
+        v2_codes = [placed([P, M], U32, "v2_0", at_h02 + 2), new_tile([P, M], U32, "v2_1")]
         for a in range(2):
             gather_v2(a, v2_codes[a], 0, M)
         before = new_tile([P, AHEAD, M], F32, "before")
         squares = new_tile([P, PACK, M], F32, "squares")
         for t in range(AHEAD):
             pick(before[:, t, :], h1[t])
-            square_on_gpsimd(squares[:, t, :], before[:, t, :])
+        nc.scalar.activation(out=squares[:, 0, :], in_=before[:, 0, :], func=ACT.Square)
+        for t in range(2, PACK):
+            log_half_plus(log_a[0][:, t, :], a0[t][:])
         log_half_plus(log_a[1][:, 0, :], squares[:, 0, :])
+        square_on_gpsimd(squares[:, 1, :], before[:, 1, :])
         v2_codes.append(placed([P, M], U32, "v2_2", at_h11))
         for first in range(0, M, M // 2):
             gather_v2(2, v2_codes[2], first, M // 2)
         after = placed([P, PACK - AHEAD, M], F32, "after", at_raw10)
         for t in range(PACK - AHEAD):
             pick(after[:, t, :], h1[AHEAD + t])
-            square_on_gpsimd(squares[:, AHEAD + t, :], after[:, t, :])
+        nc.vector.tensor_tensor(squares[:, AHEAD:, :], after[:], after[:], ALU.mult)
 
         z_codes, z_planes = {}, {}
 
@@ -314,7 +317,7 @@ def tile_list_ransomware_alarm_levels_kernel(
             log_b = bank([P, PACK, P], "log_b", CHUNKS + i)
             for t in range(PACK):
                 nc.tensor.transpose(log_b[:, t, :], log_bt[:, t * P:(t + 1) * P], ident[:])
-            diff = new_tile([P, PAIRS, P, 2], F32, "diff%d%d" % (blk, i))
+            diff = new_tile([P, PAIRS, P, 2], F32, "diff%d%d" % (blk, i), "diff%d%d" % (blk, min(i, CHUNKS - 1 - blk)))
             nc.vector.tensor_tensor(
                 diff[:],
                 log_b[:].rearrange("p (u e) m -> p u m e", u=PAIRS),
@@ -362,16 +365,14 @@ def tile_list_ransomware_alarm_levels_kernel(
         bt1 = {}
         for pair in chunk_pairs:
             for i in pair:
-                if i < CHUNKS - 1:
-                    bt1[i] = bank([P, BANK], "bt", i)
-                    for a in range(PASSES2):
-                        project(1, i, a, bt1[i])
-                else:
-                    bt1[i] = bank([P, BANK], "bt", 0)
-                    for a in range(PASSES2):
-                        project(1, i, a, bt1[i])
+                bt1[i] = bank([P, BANK], "bt", i)
+                for a in range(PASSES2):
+                    project(1, i, a, bt1[i])
             logs_of_bt(1, pair, bt1)
-            z_of(1, pair)
+        z_of(1, chunk_pairs[0])
+        last = [round_z(1, i, difference(1, i, log_bt[1][:, i, :])) for i in chunk_pairs[1]]
+        for z in last:
+            quantise_z(*z)
 
         out_view = out.rearrange("(g p) m -> p g m", p=P)
         levels = new_tile([P, CHUNKS, N // P, P], F32, "levels", "half")
@@ -392,6 +393,6 @@ def tile_list_ransomware_alarm_levels_kernel(
             nc.sync.dma_start(out=out_view[:, g0:g0 + groups, i * P:(i + 1) * P], in_=levels[:, i, g0:g0 + groups])
 
         for i in range(CHUNKS - 1):
-            alarm(i, 0, N // P, CHUNKS + i)
+            alarm(i, 0, N // P, i)
         for piece in range(2):
-            alarm(CHUNKS - 1, piece * N // P // 2, N // P // 2, 2 * CHUNKS - 1 - piece * CHUNKS)
+            alarm(CHUNKS - 1, piece * N // P // 2, N // P // 2, CHUNKS - 1 + piece)

@@ -246,7 +246,7 @@ def tile_list_ransomware_alarm_levels_kernel(
                 lhsT_scale=v2_planes[:, a * M + i * P:a * M + (i + 1) * P],
                 rhs=w2_sb[blk][:, 2 * a * PASS:2 * (a + 1) * PASS].bitcast(FP4X4),
                 rhs_scale=w2_planes[:, c0:c0 + PASS],
-                start=(a == 0), stop=(a == PASSES2 - 1),
+                start=(a == blk * (PASSES2 - 1)), stop=(a == (1 - blk) * (PASSES2 - 1)),
             )
 
         def square_of_bt(squares, bt):
@@ -314,7 +314,7 @@ def tile_list_ransomware_alarm_levels_kernel(
         z_codes, z_planes = {}, {}
 
         def difference(blk, i, log_bt):
-            log_b = bank([P, PACK, P], "log_b", CHUNKS + i)
+            log_b = bank([P, PACK, P], "log_b", blk * CHUNKS + i)
             for t in range(PACK):
                 nc.tensor.transpose(log_b[:, t, :], log_bt[:, t * P:(t + 1) * P], ident[:])
             diff = new_tile([P, PAIRS, P, 2], F32, "diff%d%d" % (blk, i), "diff%d%d" % (blk, min(i, CHUNKS - 1 - blk)))
@@ -361,14 +361,15 @@ def tile_list_ransomware_alarm_levels_kernel(
         for pair in chunk_pairs:
             logs_of_bt(0, pair, bt0)
             z_of(0, pair)
-        log_half_plus(log_a[1][:, 1:, :], squares[:, 1:, :])
         bt1 = {}
         for pair in chunk_pairs:
             for i in pair:
-                bt1[i] = bank([P, BANK], "bt", i)
-                for a in range(PASSES2):
+                bt1[i] = bank([P, BANK], "bt", CHUNKS + i)
+                for a in reversed(range(PASSES2)):
                     project(1, i, a, bt1[i])
             logs_of_bt(1, pair, bt1)
+            if pair == chunk_pairs[0]:
+                log_half_plus(log_a[1][:, 1:, :], squares[:, 1:, :])
         z_of(1, chunk_pairs[0])
         last = [round_z(1, i, difference(1, i, log_bt[1][:, i, :])) for i in chunk_pairs[1]]
         for z in last:

@@ -71,7 +71,8 @@ def tile_list_ransomware_alarm_levels_kernel(
         at_h11 = 52
         at_rounded11 = 56
         at_h02 = 64
-        at_tab0 = 68
+        at_h13 = 68
+        at_tab0 = 74
 
         offs_sb = sbuf.tile([P, S // GROUP], U16, name="offs_sb")
         pos_sb = sbuf.tile([P, M // GROUP], U16, name="pos_sb")
@@ -160,11 +161,6 @@ def tile_list_ransomware_alarm_levels_kernel(
 
         w1_codes, w1_planes = {}, {}
 
-        def round_on_gpsimd(rounded, raw):
-            nc.gpsimd.tensor_scalar(
-                rounded.rearrange("p m e j -> p e m j"), raw.rearrange("p m e j -> p e m j"), 1.0, 0.0, ALU.mult, ALU.add
-            )
-
         def round_block(blk, a, copy, rounded):
             copy(
                 rounded[:].rearrange("p (t m j) -> p m t j", t=PACK, j=PACK),
@@ -231,9 +227,6 @@ def tile_list_ransomware_alarm_levels_kernel(
         def log_half_plus(logs, squares):
             nc.scalar.activation(out=logs, in_=squares, func=ACT.Ln, bias=half[:])
 
-        def square_on_gpsimd(squares, values):
-            nc.gpsimd.tensor_tensor(squares, values, values, ALU.mult)
-
         def gather_v2(a, codes, first, count):
             entries = offs2_sb[:, first // GROUP:(first + count) // GROUP]
             nc.vector.tensor_copy(codes[:, first:first + count], tab2_sb[a][:].bitcast(U32).indirect(entries))
@@ -267,12 +260,10 @@ def tile_list_ransomware_alarm_levels_kernel(
         for u, copy in enumerate((nc.vector.tensor_copy, nc.scalar.copy)):
             round_pair(1, 1, u, copy, rounded[u][:])
             pick(a0[1 + u][:], h0[1 + u])
-        square_on_gpsimd(a0[2][:], a0[2][:])
         for u in range(PAIRS):
             quantise_w1(1, 1, 2 * u, rounded[u][:], 2, codes_tile(1, 1, 2 * u, 2))
         a0.append(new_tile([P, M], F32, "a03"))
         pick(a0[PACK - 1][:], h0[PACK - 1])
-        square_on_gpsimd(a0[PACK - 1][:], a0[PACK - 1][:])
         w2_sb.append(load_w2(1, at_raw11 + 5))
         w3_sb = placed([P, BLOCKS * N], I32, "w3_sb", at_raw11)
         nc.sync.dma_start(
@@ -289,27 +280,30 @@ def tile_list_ransomware_alarm_levels_kernel(
         for t in range(2):
             nc.scalar.activation(out=log_a[0][:, t, :], in_=a0[t][:], func=ACT.Square)
             log_half_plus(log_a[0][:, t, :], log_a[0][:, t, :])
-        h1 = first_stage(1, (0, 1), {AHEAD - 1: at_h11})
+        h1 = first_stage(1, (0, 1), {AHEAD - 1: at_h11, PACK - 1: at_h13})
 
         v2_codes = [placed([P, M], U32, "v2_0", at_h02 + 2), new_tile([P, M], U32, "v2_1")]
         for a in range(2):
             gather_v2(a, v2_codes[a], 0, M)
         before = new_tile([P, AHEAD, M], F32, "before")
-        squares = new_tile([P, PACK, M], F32, "squares")
+        squares = new_tile([P, 1, M], F32, "squares")
         for t in range(AHEAD):
             pick(before[:, t, :], h1[t])
         nc.scalar.activation(out=squares[:, 0, :], in_=before[:, 0, :], func=ACT.Square)
         for t in range(2, PACK):
-            log_half_plus(log_a[0][:, t, :], a0[t][:])
+            nc.scalar.activation(out=log_a[0][:, t, :], in_=a0[t][:], func=ACT.Square)
         log_half_plus(log_a[1][:, 0, :], squares[:, 0, :])
-        square_on_gpsimd(squares[:, 1, :], before[:, 1, :])
+        for t in range(2, PACK):
+            log_half_plus(log_a[0][:, t, :], log_a[0][:, t, :])
         v2_codes.append(placed([P, M], U32, "v2_2", at_h11))
         for first in range(0, M, M // 2):
             gather_v2(2, v2_codes[2], first, M // 2)
         after = placed([P, PACK - AHEAD, M], F32, "after", at_raw10)
         for t in range(PACK - AHEAD):
             pick(after[:, t, :], h1[AHEAD + t])
-        nc.vector.tensor_tensor(squares[:, AHEAD:, :], after[:], after[:], ALU.mult)
+        later = placed([P, PACK - 1, M], F32, "later", at_h13)
+        nc.vector.tensor_tensor(later[:, 0, :], before[:, 1, :], before[:, 1, :], ALU.mult)
+        nc.vector.tensor_tensor(later[:, 1:, :], after[:], after[:], ALU.mult)
 
         z_codes, z_planes = {}, {}
 
@@ -369,7 +363,7 @@ def tile_list_ransomware_alarm_levels_kernel(
                     project(1, i, a, bt1[i])
             logs_of_bt(1, pair, bt1)
             if pair == chunk_pairs[0]:
-                log_half_plus(log_a[1][:, 1:, :], squares[:, 1:, :])
+                log_half_plus(log_a[1][:, 1:, :], later[:])
         z_of(1, chunk_pairs[0])
         last = [round_z(1, i, difference(1, i, log_bt[1][:, i, :])) for i in chunk_pairs[1]]
         for z in last:

@@ -31,9 +31,8 @@ GROUP = 16
 PASSES, PASSES2, BLOCKS = K // PASS, K2 // PASS, H // PASS
 HALVES = S // BANK
 CHUNKS = M // P
-KIB = 1024
+UNIT = 512
 PAIRS = PACK // 2
-AHEAD = 2
 
 
 def words_of(packed):
@@ -53,68 +52,66 @@ def tile_list_ransomware_alarm_levels_kernel(
         def new_tile(shape, dtype, name, tag=None):
             return sbuf.tile(shape, dtype, name=name, tag=tag or name, align_bytes=64)
 
-        def placed(shape, dtype, name, kib):
-            return arena.tile(shape, dtype, name=name, tag=name, offset=kib * KIB, align_bytes=64)
+        def placed(shape, dtype, name, at):
+            return arena.tile(shape, dtype, name=name, tag=name, offset=at * UNIT, align_bytes=64)
 
         def bank(shape, name, b):
             return psum.tile(shape, F32, name=name, tag="bank%d" % b)
 
-        at_raw00 = 0
-        at_raw10 = 0
-        at_v2_planes = 9
-        at_rounded00 = 10
-        at_raw11 = 12
-        at_tab1 = 20
-        at_raw01 = 36
-        at_rounded01 = 44
-        at_h03 = 48
-        at_h11 = 52
-        at_rounded11 = 56
-        at_h02 = 64
-        at_h13 = 68
-        at_tab0 = 74
+        at_w2_0 = 1
+        at_raw00 = 6
+        at_tab2_1 = 7
+        at_raw11 = 24
+        at_rounded00 = 39
+        at_tab2_0 = 41
+        at_tab1 = 48
+        at_tab2_2 = 59
+        at_rounded10 = 74
+        at_w2_planes = 81
+        at_tab_sc = 82
+        at_raw01 = 89
+        at_rounded01 = 106
+        at_tab0 = 112
 
         offs_sb = sbuf.tile([P, S // GROUP], U16, name="offs_sb")
         pos_sb = sbuf.tile([P, M // GROUP], U16, name="pos_sb")
         offs2_sb = sbuf.tile([P, M // GROUP], U16, name="offs2_sb")
 
-        tab_sc = new_tile([P, T], U8, "tab_sc")
-        tab2_sc = placed([P, T2], U8, "tab2_sc", at_raw01)
+        tab_sc = placed([P, T], U8, "tab_sc", at_tab_sc)
         v_planes = new_tile([P, PASSES * S], U8, "v_planes")
         top, top2 = P - SCALE_ROWS * PASSES, P - SCALE_ROWS * PASSES2
         half = new_tile([P, 1], F32, "half")
         nc.vector.memset(half[:], 0.5)
         nc.vector.memset(tab_sc[:].bitcast(I32)[:top], 0)
-        nc.vector.memset(tab2_sc[:].bitcast(I32)[:top2], 0)
         nc.vector.memset(v_planes[:].bitcast(I32), 0)
 
         warm_up = new_tile([P, 1], F32, "warm_up")
         nc.scalar.activation(out=warm_up[:], in_=half[:], func=ACT.Ln)
 
-        def load_w1(blk, a, kib):
-            raw = placed([P, PACK, PASS], F32, "w1_raw%d%d" % (blk, a), kib)
+        def load_w1(blk, a, at):
+            raw = placed([P, PACK, PASS], F32, "w1_raw%d%d" % (blk, a), at)
             rows = w1[a * PASS:(a + 1) * PASS, blk * PASS:(blk + 1) * PASS]
             nc.sync.dma_start(out=raw[:], in_=rows.rearrange("(p j) c -> p j c", j=PACK))
             return raw
 
-        def load_words(packed, name, kib):
-            words = placed([P, packed.shape[1]], I32, name, kib)
+        def load_words(packed, name, at):
+            words = placed([P, packed.shape[1]], I32, name, at)
             nc.sync.dma_start(out=words[:], in_=words_of(packed))
             return words
 
-        def load_w2(blk, kib):
-            words = placed([P, PASSES2 * 2 * PASS], U8, "w2_sb%d" % blk, kib)
+        def load_w2(blk, at):
+            words = placed([P, PASSES2 * 2 * PASS], U8, "w2_sb%d" % blk, at)
             nc.sync.dma_start(
                 out=words[:].bitcast(I32).rearrange("p (a c) -> p a c", a=PASSES2),
                 in_=w2_words[:, :, 2 * blk * PASS:2 * (blk + 1) * PASS].bitcast(I32).rearrange("a p c -> p a c"),
             )
             return words
 
-        def load_planes(planes, scales, passes):
+        def load_planes(planes, scales, passes, first_row):
             view = planes[:].bitcast(I32).rearrange("p (a c) -> p a c", a=passes)
             for r in range(ROWS):
                 nc.sync.dma_start(
-                    out=view[r:P:QUAD],
+                    out=view[first_row + r:P:QUAD],
                     in_=scales[:, r:SCALE_ROWS:ROWS, :].bitcast(I32).rearrange("a q c -> q a c"),
                 )
 
@@ -132,9 +129,6 @@ def tile_list_ransomware_alarm_levels_kernel(
         nc.sync.dma_start(offs_sb[:], offs)
         tab_sb = [load_words(tab_words[0], "tab0", at_tab0)]
         nc.sync.dma_start(offs2_sb[:], offs2)
-        nc.sync.dma_start(
-            out=tab2_sc[:].bitcast(I32)[top2:], in_=tab2_scales.bitcast(I32).rearrange("a q c -> q a c")
-        )
         nc.sync.dma_start(pos_sb[:], pos1)
         w1_raw[0, 0] = load_w1(0, 0, at_raw00)
         tab_sb.append(load_words(tab_words[1], "tab1", at_tab1))
@@ -145,8 +139,6 @@ def tile_list_ransomware_alarm_levels_kernel(
         v_sc = new_tile([P, S], U8, "v_sc")
         nc.vector.tensor_copy(v_sc[:], tab_sc[:].indirect(offs_sb[:]))
         carry_planes(v_planes, v_sc, top, PASSES)
-        v2_sc = new_tile([P, M], U8, "v2_sc")
-        nc.vector.tensor_copy(v2_sc[:], tab2_sc[:].indirect(offs2_sb[:]))
         w1_raw[0, 1] = load_w1(0, 1, at_raw01)
 
         v_codes = {}
@@ -158,6 +150,11 @@ def tile_list_ransomware_alarm_levels_kernel(
                 nc.vector.tensor_copy(v_codes[a, u][:], tab_sb[a][:].bitcast(U32).indirect(entries))
 
         gather_v(0)
+        tab2_sc = placed([P, T2], U8, "tab2_sc", at_tab0)
+        nc.vector.memset(tab2_sc[:].bitcast(I32)[:top2], 0)
+        nc.sync.dma_start(
+            out=tab2_sc[:].bitcast(I32)[top2:], in_=tab2_scales.bitcast(I32).rearrange("a q c -> q a c")
+        )
 
         w1_codes, w1_planes = {}, {}
 
@@ -171,65 +168,71 @@ def tile_list_ransomware_alarm_levels_kernel(
             pairs = w1_raw[blk, a][:].rearrange("p j (m u e) -> p u m e j", u=PAIRS, e=2)
             copy(rounded.rearrange("p (e m j) -> p m e j", e=2, j=PACK), pairs[:, u])
 
-        def quantise_w1(blk, a, t0, rounded, sets, codes):
+        def quantise_w1(blk, a, t0, rounded, sets):
+            codes = new_tile([P, sets * P], U32, "w1_codes%d%d%d" % (blk, a, t0))
             planes = new_tile([P, sets * P], U8, "w1_planes%d%d%d" % (blk, a, t0))
             nc.vector.quantize_mx(out=codes[:].bitcast(FP8X4), scales=planes[:], in_=rounded)
             for e in range(sets):
                 w1_codes[blk, a, t0 + e] = codes[:, e * P:(e + 1) * P]
                 w1_planes[blk, a, t0 + e] = planes[:, e * P:(e + 1) * P]
 
-        def codes_tile(blk, a, t0, sets):
-            return new_tile([P, sets * P], U32, "w1_codes%d%d%d" % (blk, a, t0))
-
         rounded = placed([P, PACK * PASS], BF16, "w1_bf00", at_rounded00)
         round_block(0, 0, nc.scalar.copy, rounded)
-        w1_raw[1, 0] = load_w1(1, 0, at_raw10)
-        quantise_w1(0, 0, 0, rounded[:], PACK, codes_tile(0, 0, 0, PACK))
+        w1_raw[1, 0] = load_w1(1, 0, at_raw00)
+        quantise_w1(0, 0, 0, rounded[:], PACK)
         w1_raw[1, 1] = load_w1(1, 1, at_raw11)
-        v2_planes = placed([P, PASSES2 * M], U8, "v2_planes", at_v2_planes)
-        nc.vector.memset(v2_planes[:].bitcast(I32), 0)
-        carry_planes(v2_planes, v2_sc, top2, PASSES2)
         gather_v(1)
-        tab2_sb = [load_words(tab2_words[a], "tab2_%d" % a, at_tab1 + 8 * a) for a in range(2)]
-        rounded = [placed([P, 2 * PASS], BF16, "w1_bf010", at_rounded01), new_tile([P, 2 * PASS], BF16, "w1_bf011")]
+        tab2_sb = [load_words(tab2_words[0], "tab2_0", at_tab2_0)]
+        rounded = [new_tile([P, 2 * PASS], BF16, "w1_bf010"), placed([P, 2 * PASS], BF16, "w1_bf011", at_rounded01)]
         for u, copy in enumerate((nc.vector.tensor_copy, nc.scalar.copy)):
             round_pair(0, 1, u, copy, rounded[u][:])
         for u in range(PAIRS):
-            quantise_w1(0, 1, 2 * u, rounded[u][:], 2, codes_tile(0, 1, 2 * u, 2))
-        w2_sb = [load_w2(0, at_raw01)]
-        w2_planes = placed([P, PASSES2 * H], U8, "w2_planes", at_rounded01)
-        nc.vector.memset(w2_planes[:].bitcast(I32), 0)
-        load_planes(w2_planes, w2_scales, PASSES2)
+            quantise_w1(0, 1, 2 * u, rounded[u][:], 2)
+        v2_sc = placed([P, M], U8, "v2_sc", at_rounded01)
+        nc.vector.tensor_copy(v2_sc[:], tab2_sc[:].indirect(offs2_sb[:]))
+        v2_planes = placed([P, PASSES2 * M], U8, "v2_planes", at_tab0)
+        carry_planes(v2_planes, v2_sc, top2, PASSES2)
 
-        def first_stage(blk, passes, places):
-            h = [
-                placed([P, S], F32, "h%d%d" % (blk, t), places[t]) if t in places
-                else new_tile([P, S], F32, "h%d%d" % (blk, t))
-                for t in range(PACK)
-            ]
-            for t, u in itertools.product(range(PACK), range(HALVES)):
+        def first_stage(blk, h, order):
+            for t, u in order:
                 acc = bank([P, BANK], "acc", HALVES * t + u)
-                for a in passes:
+                for a in range(PASSES):
                     nc.tensor.matmul_mx(
                         out=acc[:],
                         lhsT=w1_codes[blk, a, t].bitcast(FP8X4),
                         lhsT_scale=w1_planes[blk, a, t],
                         rhs=v_codes[a, u][:].bitcast(FP8X4),
                         rhs_scale=v_planes[:, a * S + u * BANK:a * S + (u + 1) * BANK],
-                        start=(a == passes[0]), stop=(a == passes[-1]),
+                        start=(a == 0), stop=(a == PASSES - 1),
                     )
                 nc.scalar.copy(h[t][:, u * BANK:(u + 1) * BANK], acc[:])
-            return h
-
-        def pick(row, window):
-            nc.vector.tensor_copy(row, window[:].indirect(pos_sb[:]))
 
         def log_half_plus(logs, squares):
             nc.scalar.activation(out=logs, in_=squares, func=ACT.Ln, bias=half[:])
 
-        def gather_v2(a, codes, first, count):
+        log_a = [new_tile([P, PACK, M], F32, "log_a%d" % blk) for blk in range(BLOCKS)]
+        picked = {}
+
+        def pick(blk, t, window, at=None):
+            name = "a%d%d" % (blk, t)
+            picked[blk, t] = new_tile([P, M], F32, name) if at is None else placed([P, M], F32, name, at)
+            nc.vector.tensor_copy(picked[blk, t][:], window[:].indirect(pos_sb[:]))
+
+        def square(blk, t, engine):
+            row = picked[blk, t]
+            if engine is nc.scalar:
+                nc.scalar.activation(out=log_a[blk][:, t, :], in_=row[:], func=ACT.Square)
+            else:
+                engine.tensor_tensor(log_a[blk][:, t, :], row[:], row[:], ALU.mult)
+
+        def log_of_a(blk, t):
+            log_half_plus(log_a[blk][:, t, :], log_a[blk][:, t, :])
+
+        v2_codes = [new_tile([P, M], U32, "v2_%d" % a) for a in range(PASSES2)]
+
+        def gather_v2(a, first, count):
             entries = offs2_sb[:, first // GROUP:(first + count) // GROUP]
-            nc.vector.tensor_copy(codes[:, first:first + count], tab2_sb[a][:].bitcast(U32).indirect(entries))
+            nc.vector.tensor_copy(v2_codes[a][:, first:first + count], tab2_sb[a][:].bitcast(U32).indirect(entries))
 
         def project(blk, i, a, bt):
             c0 = a * H + blk * PASS
@@ -239,7 +242,7 @@ def tile_list_ransomware_alarm_levels_kernel(
                 lhsT_scale=v2_planes[:, a * M + i * P:a * M + (i + 1) * P],
                 rhs=w2_sb[blk][:, 2 * a * PASS:2 * (a + 1) * PASS].bitcast(FP4X4),
                 rhs_scale=w2_planes[:, c0:c0 + PASS],
-                start=(a == blk * (PASSES2 - 1)), stop=(a == (1 - blk) * (PASSES2 - 1)),
+                start=(a == 0), stop=(a == PASSES2 - 1),
             )
 
         def square_of_bt(squares, bt):
@@ -249,82 +252,61 @@ def tile_list_ransomware_alarm_levels_kernel(
                 func=ACT.Square,
             )
 
-        h0 = first_stage(0, (0, 1), {2: at_h02, 3: at_h03})
-        rounded = new_tile([P, PACK * PASS], BF16, "w1_bf10")
+        h0 = [placed([P, S], F32, "h0%d" % t, at_tab0 + 4 + 8 * t) for t in range(PACK)]
+        first_stage(0, h0, itertools.product(range(PACK), range(HALVES)))
+        rounded = placed([P, PACK * PASS], BF16, "w1_bf10", at_rounded10)
         round_block(1, 0, nc.vector.tensor_copy, rounded)
-        tab2_sb.append(load_words(tab2_words[2], "tab2_2", at_raw10))
-        a0 = [new_tile([P, M], F32, "a0%d" % t) for t in range(PACK - 1)]
-        pick(a0[0][:], h0[0])
-        quantise_w1(1, 0, 0, rounded[:], PACK, codes_tile(1, 0, 0, PACK))
-        rounded = [placed([P, 2 * PASS], BF16, "w1_bf11%d" % u, at_rounded11 + 2 * u) for u in range(PAIRS)]
+        tab2_sb.append(load_words(tab2_words[1], "tab2_1", at_tab2_1))
+        w2_sb = [load_w2(0, at_w2_0)]
+        pick(0, 0, h0[0])
+        quantise_w1(1, 0, 0, rounded[:], PACK)
+        w2_planes = placed([P, UNIT + PASSES2 * H], U8, "w2_planes", at_w2_planes)[:, UNIT:]
+        load_planes(w2_planes, w2_scales, PASSES2, 0)
+        tab2_sb.append(load_words(tab2_words[2], "tab2_2", at_tab2_2))
+        rounded = [new_tile([P, 2 * PASS], BF16, "w1_bf11%d" % u) for u in range(PAIRS)]
         for u, copy in enumerate((nc.vector.tensor_copy, nc.scalar.copy)):
             round_pair(1, 1, u, copy, rounded[u][:])
-            pick(a0[1 + u][:], h0[1 + u])
-        for u in range(PAIRS):
-            quantise_w1(1, 1, 2 * u, rounded[u][:], 2, codes_tile(1, 1, 2 * u, 2))
-        a0.append(new_tile([P, M], F32, "a03"))
-        pick(a0[PACK - 1][:], h0[PACK - 1])
-        w2_sb.append(load_w2(1, at_raw11 + 5))
-        w3_sb = placed([P, BLOCKS * N], I32, "w3_sb", at_raw11)
+        w2_sb.append(load_w2(1, at_raw11))
+        gain_sb = placed([P, BLOCKS, PACK], F32, "gain_sb", at_raw11 + 6)
+        nc.sync.dma_start(out=gain_sb[:], in_=gain.rearrange("(b p t) -> p b t", b=BLOCKS, t=PACK))
+        w3_sb = placed([P, BLOCKS * N], I32, "w3_sb", at_raw11 + 7)
         nc.sync.dma_start(
             out=w3_sb[:].rearrange("p (b c) -> p b c", b=BLOCKS),
             in_=w3_words.rearrange("b p c i -> p b (c i)").bitcast(I32),
         )
-        gain_sb = placed([P, BLOCKS, PACK], F32, "gain_sb", at_h02)
-        nc.sync.dma_start(out=gain_sb[:], in_=gain.rearrange("(b p t) -> p b t", b=BLOCKS, t=PACK))
-        w3_planes = placed([P, BLOCKS * N], U8, "w3_planes", at_h03)
-        nc.gpsimd.memset(w3_planes[:].bitcast(I32), 0)
-        load_planes(w3_planes, w3_scales, BLOCKS)
-
-        log_a = [new_tile([P, PACK, M], F32, "log_a%d" % blk) for blk in range(BLOCKS)]
+        pick(0, 1, h0[1])
+        for u in range(PAIRS):
+            quantise_w1(1, 1, 2 * u, rounded[u][:], 2)
+        for t in range(2, PACK):
+            pick(0, t, h0[t])
         for t in range(2):
-            nc.scalar.activation(out=log_a[0][:, t, :], in_=a0[t][:], func=ACT.Square)
-            log_half_plus(log_a[0][:, t, :], log_a[0][:, t, :])
-        h1 = first_stage(1, (0, 1), {AHEAD - 1: at_h11, PACK - 1: at_h13})
-
-        v2_codes = [placed([P, M], U32, "v2_0", at_h02 + 2), new_tile([P, M], U32, "v2_1")]
+            square(0, t, nc.scalar)
+            log_of_a(0, t)
+        h1 = [new_tile([P, S], F32, "h1%d" % t) for t in range(PACK)]
+        first_stage(1, h1, itertools.product(range(PACK), range(HALVES)))
+        for t in range(2, PACK):
+            square(0, t, nc.gpsimd)
+            log_of_a(0, t)
+        w3_planes = v_planes[:, :BLOCKS * N]
+        load_planes(w3_planes, w3_scales, BLOCKS, ROWS)
         for a in range(2):
-            gather_v2(a, v2_codes[a], 0, M)
-        before = new_tile([P, AHEAD, M], F32, "before")
-        squares = new_tile([P, 1, M], F32, "squares")
-        for t in range(AHEAD):
-            pick(before[:, t, :], h1[t])
-        nc.scalar.activation(out=squares[:, 0, :], in_=before[:, 0, :], func=ACT.Square)
-        for t in range(2, PACK):
-            nc.scalar.activation(out=log_a[0][:, t, :], in_=a0[t][:], func=ACT.Square)
-        log_half_plus(log_a[1][:, 0, :], squares[:, 0, :])
-        for t in range(2, PACK):
-            log_half_plus(log_a[0][:, t, :], log_a[0][:, t, :])
-        v2_codes.append(placed([P, M], U32, "v2_2", at_h11))
+            gather_v2(a, 0, M)
+        for t in range(1):
+            pick(1, t, h1[t])
         for first in range(0, M, M // 2):
-            gather_v2(2, v2_codes[2], first, M // 2)
-        after = placed([P, PACK - AHEAD, M], F32, "after", at_raw10)
-        for t in range(PACK - AHEAD):
-            pick(after[:, t, :], h1[AHEAD + t])
-        later = placed([P, PACK - 1, M], F32, "later", at_h13)
-        nc.vector.tensor_tensor(later[:, 0, :], before[:, 1, :], before[:, 1, :], ALU.mult)
-        nc.vector.tensor_tensor(later[:, 1:, :], after[:], after[:], ALU.mult)
+            gather_v2(2, first, M // 2)
+        for t in range(1, PACK):
+            pick(1, t, h1[t], at_tab2_2 + 4 * t)
+        for t in range(PACK):
+            square(1, t, nc.gpsimd)
 
         z_codes, z_planes = {}, {}
-
-        def difference(blk, i, log_bt):
-            log_b = bank([P, PACK, P], "log_b", blk * CHUNKS + i)
-            for t in range(PACK):
-                nc.tensor.transpose(log_b[:, t, :], log_bt[:, t * P:(t + 1) * P], ident[:])
-            diff = new_tile([P, PAIRS, P, 2], F32, "diff%d%d" % (blk, i), "diff%d%d" % (blk, min(i, CHUNKS - 1 - blk)))
-            nc.vector.tensor_tensor(
-                diff[:],
-                log_b[:].rearrange("p (u e) m -> p u m e", u=PAIRS),
-                log_a[blk][:, :, i * P:(i + 1) * P].rearrange("p (u e) m -> p u m e", u=PAIRS),
-                ALU.subtract,
-            )
-            return diff
 
         def round_z(blk, i, diff):
             z = new_tile([P, PASS], BF16, "z%d%d" % (blk, i))
             nc.vector.tensor_tensor(
                 z[:].rearrange("p (m u e) -> p m u e", u=PAIRS, e=2),
-                diff[:].rearrange("p u m e -> p m u e"),
+                diff.rearrange("p u m e -> p m u e"),
                 gain_sb[:, blk, :].rearrange("p (u e) -> p u e", u=PAIRS).unsqueeze(1).to_broadcast([P, P, PAIRS, 2]),
                 ALU.mult,
             )
@@ -336,10 +318,24 @@ def tile_list_ransomware_alarm_levels_kernel(
             nc.vector.quantize_mx(out=z_codes[blk, i].bitcast(FP8X4), scales=z_planes[blk, i], in_=z[:])
 
         log_bt = [new_tile([P, CHUNKS, PASS], F32, "log_bt%d" % blk) for blk in range(BLOCKS)]
-        bt0 = [bank([P, BANK], "bt", i) for i in range(CHUNKS)]
-        for a, i in itertools.product(range(PASSES2), range(CHUNKS)):
-            project(0, i, a, bt0[i])
         chunk_pairs = [(i, i + 1) for i in range(0, CHUNKS, 2)]
+
+        def difference(blk, i, b):
+            log_b = bank([P, PACK, P], "log_b", b)
+            for t in range(PACK):
+                nc.tensor.transpose(log_b[:, t, :], log_bt[blk][:, i, t * P:(t + 1) * P], ident[:])
+            diff = new_tile([P, PAIRS, P, 2], F32, "diff%d%d" % (blk, i), "diff%d%d" % (blk, min(i, CHUNKS - 1 - blk)))
+            nc.vector.tensor_tensor(
+                diff[:],
+                log_b[:].rearrange("p (u e) m -> p u m e", u=PAIRS),
+                log_a[blk][:, :, i * P:(i + 1) * P].rearrange("p (u e) m -> p u m e", u=PAIRS),
+                ALU.subtract,
+            )
+            return diff[:]
+
+        def finish_z(blk, pair, diffs):
+            for z in [round_z(blk, i, diff) for i, diff in zip(pair, diffs)]:
+                quantise_z(*z)
 
         def logs_of_bt(blk, pair, banks):
             for i in pair:
@@ -347,27 +343,25 @@ def tile_list_ransomware_alarm_levels_kernel(
             for i in pair:
                 log_half_plus(log_bt[blk][:, i, :], log_bt[blk][:, i, :])
 
-        def z_of(blk, pair):
-            diffs = [difference(blk, i, log_bt[blk][:, i, :]) for i in pair]
-            for z in [round_z(blk, i, diff) for i, diff in zip(pair, diffs)]:
-                quantise_z(*z)
-
-        for pair in chunk_pairs:
-            logs_of_bt(0, pair, bt0)
-            z_of(0, pair)
+        bt0 = [bank([P, BANK], "bt", i) for i in range(CHUNKS)]
+        for a, i in itertools.product(range(PASSES2), range(CHUNKS)):
+            project(0, i, a, bt0[i])
         bt1 = {}
-        for pair in chunk_pairs:
-            for i in pair:
-                bt1[i] = bank([P, BANK], "bt", CHUNKS + i)
-                for a in reversed(range(PASSES2)):
+        for g, pair in enumerate(chunk_pairs):
+            logs_of_bt(0, pair, bt0)
+            diffs = [difference(0, i, (6, 0)[g] + k) for k, i in enumerate(pair)]
+            for k, i in enumerate(pair):
+                bt1[i] = bank([P, BANK], "bt", (4, 2)[g] + k)
+                for a in range(PASSES2):
                     project(1, i, a, bt1[i])
-            logs_of_bt(1, pair, bt1)
-            if pair == chunk_pairs[0]:
-                log_half_plus(log_a[1][:, 1:, :], later[:])
-        z_of(1, chunk_pairs[0])
-        last = [round_z(1, i, difference(1, i, log_bt[1][:, i, :])) for i in chunk_pairs[1]]
-        for z in last:
-            quantise_z(*z)
+            finish_z(0, pair, diffs)
+        logs_of_bt(1, chunk_pairs[0], bt1)
+        for t in range(0, PACK, 2):
+            log_half_plus(log_a[1][:, t:t + 2, :], log_a[1][:, t:t + 2, :])
+        finish_z(1, chunk_pairs[0], [difference(1, i, 6 + i) for i in chunk_pairs[0]])
+        logs_of_bt(1, chunk_pairs[1], bt1)
+        for k, i in enumerate(chunk_pairs[1]):
+            finish_z(1, (i,), [difference(1, i, k)])
 
         out_view = out.rearrange("(g p) m -> p g m", p=P)
         levels = new_tile([P, CHUNKS, N // P, P], F32, "levels", "half")
@@ -379,7 +373,7 @@ def tile_list_ransomware_alarm_levels_kernel(
                 nc.tensor.matmul_mx(
                     out=y[:, g, :],
                     lhsT=w3_sb[:, cols].bitcast(FP8X4),
-                    lhsT_scale=w3_planes[:, cols],
+                    lhsT_scale=w3_planes[ROWS:, cols],
                     rhs=z_codes[blk, i].bitcast(FP8X4),
                     rhs_scale=z_planes[blk, i],
                     start=(blk == 0 and g == 0), stop=(blk == BLOCKS - 1 and g == groups - 1),
@@ -388,6 +382,6 @@ def tile_list_ransomware_alarm_levels_kernel(
             nc.sync.dma_start(out=out_view[:, g0:g0 + groups, i * P:(i + 1) * P], in_=levels[:, i, g0:g0 + groups])
 
         for i in range(CHUNKS - 1):
-            alarm(i, 0, N // P, i)
+            alarm(i, 0, N // P, (4, 5, 2)[i])
         for piece in range(2):
-            alarm(CHUNKS - 1, piece * N // P // 2, N // P // 2, CHUNKS - 1 + piece)
+            alarm(CHUNKS - 1, piece * N // P // 2, N // P // 2, (3, 6)[piece])

@@ -58,31 +58,32 @@ def tile_list_ransomware_alarm_levels_kernel(
         def bank(shape, name, b):
             return psum.tile(shape, F32, name=name, tag="bank%d" % b)
 
-        at_w2_0 = 1
-        at_raw00 = 6
-        at_tab2_1 = 7
-        at_raw11 = 24
-        at_rounded00 = 39
-        at_tab2_0 = 41
-        at_tab1 = 48
-        at_tab2_2 = 59
-        at_rounded10 = 74
-        at_w2_planes = 81
-        at_tab_sc = 82
-        at_raw01 = 89
-        at_rounded01 = 106
-        at_tab0 = 112
+        at_raw00 = 0
+        at_tab2_2 = 0
+        at_raw11 = 16
+        at_rounded00 = 31
+        at_v2_planes = 38
+        at_tab2_sc = 39
+        at_raw01 = 42
+        at_rounded01 = 58
+        at_w2_planes = 61
+        at_tab_sc = 62
+        at_tab1 = 70
+        at_tab0 = 102
 
         offs_sb = sbuf.tile([P, S // GROUP], U16, name="offs_sb")
         pos_sb = sbuf.tile([P, M // GROUP], U16, name="pos_sb")
         offs2_sb = sbuf.tile([P, M // GROUP], U16, name="offs2_sb")
 
         tab_sc = placed([P, T], U8, "tab_sc", at_tab_sc)
+        tab2_sc = placed([P, T2], U8, "tab2_sc", at_tab2_sc)
         v_planes = new_tile([P, PASSES * S], U8, "v_planes")
-        top, top2 = P - SCALE_ROWS * PASSES, P - SCALE_ROWS * PASSES2
+        top, top2 = P - SCALE_ROWS * PASSES, P // 2 - SCALE_ROWS * PASSES2
         half = new_tile([P, 1], F32, "half")
         nc.vector.memset(half[:], 0.5)
         nc.vector.memset(tab_sc[:].bitcast(I32)[:top], 0)
+        nc.vector.memset(tab2_sc[:].bitcast(I32)[:top2], 0)
+        nc.vector.memset(tab2_sc[:].bitcast(I32)[P // 2:], 0)
         nc.vector.memset(v_planes[:].bitcast(I32), 0)
 
         warm_up = new_tile([P, 1], F32, "warm_up")
@@ -129,6 +130,10 @@ def tile_list_ransomware_alarm_levels_kernel(
         nc.sync.dma_start(offs_sb[:], offs)
         tab_sb = [load_words(tab_words[0], "tab0", at_tab0)]
         nc.sync.dma_start(offs2_sb[:], offs2)
+        nc.sync.dma_start(
+            out=tab2_sc[:].bitcast(I32)[top2:top2 + SCALE_ROWS * PASSES2],
+            in_=tab2_scales.bitcast(I32).rearrange("a q c -> q a c"),
+        )
         nc.sync.dma_start(pos_sb[:], pos1)
         w1_raw[0, 0] = load_w1(0, 0, at_raw00)
         tab_sb.append(load_words(tab_words[1], "tab1", at_tab1))
@@ -139,6 +144,8 @@ def tile_list_ransomware_alarm_levels_kernel(
         v_sc = new_tile([P, S], U8, "v_sc")
         nc.vector.tensor_copy(v_sc[:], tab_sc[:].indirect(offs_sb[:]))
         carry_planes(v_planes, v_sc, top, PASSES)
+        v2_sc = new_tile([P, M], U8, "v2_sc")
+        nc.vector.tensor_copy(v2_sc[:], tab2_sc[:].indirect(offs2_sb[:]))
         w1_raw[0, 1] = load_w1(0, 1, at_raw01)
 
         v_codes = {}
@@ -150,11 +157,6 @@ def tile_list_ransomware_alarm_levels_kernel(
                 nc.vector.tensor_copy(v_codes[a, u][:], tab_sb[a][:].bitcast(U32).indirect(entries))
 
         gather_v(0)
-        tab2_sc = placed([P, T2], U8, "tab2_sc", at_tab0)
-        nc.vector.memset(tab2_sc[:].bitcast(I32)[:top2], 0)
-        nc.sync.dma_start(
-            out=tab2_sc[:].bitcast(I32)[top2:], in_=tab2_scales.bitcast(I32).rearrange("a q c -> q a c")
-        )
 
         w1_codes, w1_planes = {}, {}
 
@@ -181,17 +183,18 @@ def tile_list_ransomware_alarm_levels_kernel(
         w1_raw[1, 0] = load_w1(1, 0, at_raw00)
         quantise_w1(0, 0, 0, rounded[:], PACK)
         w1_raw[1, 1] = load_w1(1, 1, at_raw11)
+        v2_planes = placed([P, UNIT + PASSES2 * M], U8, "v2_planes", at_v2_planes)[:, UNIT:]
+        carry_planes(v2_planes, v2_sc, top2, PASSES2)
         gather_v(1)
-        tab2_sb = [load_words(tab2_words[0], "tab2_0", at_tab2_0)]
+        tab2_sb = [load_words(tab2_words[a], "tab2_%d" % a, at_tab1 + 16 * a) for a in range(2)]
         rounded = [new_tile([P, 2 * PASS], BF16, "w1_bf010"), placed([P, 2 * PASS], BF16, "w1_bf011", at_rounded01)]
         for u, copy in enumerate((nc.vector.tensor_copy, nc.scalar.copy)):
             round_pair(0, 1, u, copy, rounded[u][:])
+        w2_sb = [load_w2(0, at_raw01)]
         for u in range(PAIRS):
             quantise_w1(0, 1, 2 * u, rounded[u][:], 2)
-        v2_sc = placed([P, M], U8, "v2_sc", at_rounded01)
-        nc.vector.tensor_copy(v2_sc[:], tab2_sc[:].indirect(offs2_sb[:]))
-        v2_planes = placed([P, PASSES2 * M], U8, "v2_planes", at_tab0)
-        carry_planes(v2_planes, v2_sc, top2, PASSES2)
+        w2_planes = placed([P, UNIT + PASSES2 * H], U8, "w2_planes", at_w2_planes)[:, UNIT:]
+        load_planes(w2_planes, w2_scales, PASSES2, 0)
 
         def first_stage(blk, h, order):
             for t, u in order:
@@ -252,17 +255,13 @@ def tile_list_ransomware_alarm_levels_kernel(
                 func=ACT.Square,
             )
 
-        h0 = [placed([P, S], F32, "h0%d" % t, at_tab0 + 4 + 8 * t) for t in range(PACK)]
+        h0 = [placed([P, S], F32, "h0%d" % t, at_tab0 + 8 * t) for t in range(PACK)]
         first_stage(0, h0, itertools.product(range(PACK), range(HALVES)))
-        rounded = placed([P, PACK * PASS], BF16, "w1_bf10", at_rounded10)
+        rounded = new_tile([P, PACK * PASS], BF16, "w1_bf10")
         round_block(1, 0, nc.vector.tensor_copy, rounded)
-        tab2_sb.append(load_words(tab2_words[1], "tab2_1", at_tab2_1))
-        w2_sb = [load_w2(0, at_w2_0)]
+        tab2_sb.append(load_words(tab2_words[2], "tab2_2", at_tab2_2))
         pick(0, 0, h0[0])
         quantise_w1(1, 0, 0, rounded[:], PACK)
-        w2_planes = placed([P, UNIT + PASSES2 * H], U8, "w2_planes", at_w2_planes)[:, UNIT:]
-        load_planes(w2_planes, w2_scales, PASSES2, 0)
-        tab2_sb.append(load_words(tab2_words[2], "tab2_2", at_tab2_2))
         rounded = [new_tile([P, 2 * PASS], BF16, "w1_bf11%d" % u) for u in range(PAIRS)]
         for u, copy in enumerate((nc.vector.tensor_copy, nc.scalar.copy)):
             round_pair(1, 1, u, copy, rounded[u][:])

@@ -59,7 +59,7 @@ def tile_list_ransomware_alarm_levels_kernel(
             return psum.tile(shape, F32, name=name, tag="bank%d" % b)
 
         at_raw00 = 0
-        at_tab2_2 = 0
+        at_tab2_2 = 134
         at_raw11 = 16
         at_rounded00 = 31
         at_v2_planes = 38
@@ -70,6 +70,8 @@ def tile_list_ransomware_alarm_levels_kernel(
         at_tab_sc = 62
         at_tab1 = 70
         at_tab0 = 102
+        at_rounded10 = (146, 156)
+        at_rounded11 = (154, 158)
 
         offs_sb = sbuf.tile([P, S // GROUP], U16, name="offs_sb")
         pos_sb = sbuf.tile([P, M // GROUP], U16, name="pos_sb")
@@ -231,7 +233,7 @@ def tile_list_ransomware_alarm_levels_kernel(
         def log_of_a(blk, t):
             log_half_plus(log_a[blk][:, t, :], log_a[blk][:, t, :])
 
-        v2_codes = [new_tile([P, M], U32, "v2_%d" % a) for a in range(PASSES2)]
+        v2_codes = {2: new_tile([P, M], U32, "v2_2")}
 
         def gather_v2(a, first, count):
             entries = offs2_sb[:, first // GROUP:(first + count) // GROUP]
@@ -257,14 +259,21 @@ def tile_list_ransomware_alarm_levels_kernel(
 
         h0 = [placed([P, S], F32, "h0%d" % t, at_tab0 + 8 * t) for t in range(PACK)]
         first_stage(0, h0, itertools.product(range(PACK), range(HALVES)))
-        rounded = new_tile([P, PACK * PASS], BF16, "w1_bf10")
-        round_block(1, 0, nc.vector.tensor_copy, rounded)
+        rounded = [placed([P, 2 * PASS], BF16, "w1_bf10%d" % u, at_rounded10[u]) for u in range(PAIRS)]
+        for u in range(PAIRS):
+            round_pair(1, 0, u, nc.vector.tensor_copy, rounded[u][:])
+        for u in range(PAIRS):
+            quantise_w1(1, 0, 2 * u, rounded[u][:], 2)
         tab2_sb.append(load_words(tab2_words[2], "tab2_2", at_tab2_2))
-        pick(0, 0, h0[0])
-        quantise_w1(1, 0, 0, rounded[:], PACK)
-        rounded = [new_tile([P, 2 * PASS], BF16, "w1_bf11%d" % u) for u in range(PAIRS)]
-        for u, copy in enumerate((nc.vector.tensor_copy, nc.scalar.copy)):
-            round_pair(1, 1, u, copy, rounded[u][:])
+        for t in range(PACK):
+            pick(0, t, h0[t], at_raw00 + 4 * t)
+
+        def round_on_gpsimd(rounded, raw):
+            nc.gpsimd.tensor_scalar(rounded, raw, 1.0, 0.0, ALU.mult, ALU.add)
+
+        rounded = [placed([P, 2 * PASS], BF16, "w1_bf11%d" % u, at_rounded11[u]) for u in range(PAIRS)]
+        for u in range(PAIRS):
+            round_pair(1, 1, u, round_on_gpsimd, rounded[u][:])
         w2_sb.append(load_w2(1, at_raw11))
         gain_sb = placed([P, BLOCKS, PACK], F32, "gain_sb", at_raw11 + 6)
         nc.sync.dma_start(out=gain_sb[:], in_=gain.rearrange("(b p t) -> p b t", b=BLOCKS, t=PACK))
@@ -273,25 +282,24 @@ def tile_list_ransomware_alarm_levels_kernel(
             out=w3_sb[:].rearrange("p (b c) -> p b c", b=BLOCKS),
             in_=w3_words.rearrange("b p c i -> p b (c i)").bitcast(I32),
         )
-        pick(0, 1, h0[1])
         for u in range(PAIRS):
             quantise_w1(1, 1, 2 * u, rounded[u][:], 2)
-        for t in range(2, PACK):
-            pick(0, t, h0[t])
         for t in range(2):
             square(0, t, nc.scalar)
             log_of_a(0, t)
+        square(0, 2, nc.scalar)
         h1 = [new_tile([P, S], F32, "h1%d" % t) for t in range(PACK)]
         first_stage(1, h1, itertools.product(range(PACK), range(HALVES)))
-        for t in range(2, PACK):
-            square(0, t, nc.gpsimd)
-            log_of_a(0, t)
+        log_of_a(0, 2)
+        last_squares = placed([P, M], F32, "last_squares", at_rounded11[0] + 1)
+        nc.gpsimd.tensor_tensor(last_squares[:], picked[0, 3][:], picked[0, 3][:], ALU.mult)
+        log_half_plus(log_a[0][:, 3, :], last_squares[:])
         w3_planes = v_planes[:, :BLOCKS * N]
         load_planes(w3_planes, w3_scales, BLOCKS, ROWS)
         for a in range(2):
+            v2_codes[a] = placed([P, M], U32, "v2_%d" % a, (at_rounded11[0] - 3, at_rounded11[1] + 1)[a])
             gather_v2(a, 0, M)
-        for t in range(1):
-            pick(1, t, h1[t])
+        pick(1, 0, h1[0], at_tab1 + 16)
         for first in range(0, M, M // 2):
             gather_v2(2, first, M // 2)
         for t in range(1, PACK):

import itertools
from contextlib import ExitStack

import concourse.mybir as mybir
from concourse.masks import make_identity

K, T, S = 1024, 4096, 1024
K2, T2, M = 1536, 2048, 512
H, N = 1024, 512
FLOPS = 2 * (K * H * S + K2 * H * M + H * N * M)

F32 = mybir.dt.float32
BF16 = mybir.dt.bfloat16
I32 = mybir.dt.int32
U32 = mybir.dt.uint32
U16 = mybir.dt.uint16
U8 = mybir.dt.uint8
FP8X4 = mybir.dt.float8_e4m3fn_x4
FP4X4 = mybir.dt.float4_e2m1fn_x4
ACT = mybir.ActivationFunctionType
ALU = mybir.AluOpType

P = 128
PACK = 4
PASS = P * PACK
BANK = 512
QUADS, QUAD = 4, 32
ROWS = 4
SCALE_ROWS = QUADS * ROWS
GROUP = 16
PASSES, PASSES2, BLOCKS = K // PASS, K2 // PASS, H // PASS
HALVES = S // BANK
CHUNKS = M // P
UNIT = 512
PAIRS = PACK // 2


def words_of(packed):
    return packed.rearrange("p c i -> p (c i)").bitcast(I32)


def tile_list_ransomware_alarm_levels_kernel(
    tc, tab_words, tab_scales, tab2_words, tab2_scales, w1, w2_words, w2_scales,
    w3_words, w3_scales, gain, offs, pos1, offs2, out,
):
    nc = tc.nc
    with ExitStack() as ctx:
        sbuf = ctx.enter_context(tc.tile_pool(name="sbuf", bufs=1))
        arena = ctx.enter_context(tc.tile_pool(name="arena", bufs=1))
        psum = ctx.enter_context(tc.psum_pool(name="psum", bufs=1))

        def new_tile(shape, dtype, name, tag=None):
            return sbuf.tile(shape, dtype, name=name, tag=tag or name, align_bytes=64)

        def placed(shape, dtype, name, at):
            return arena.tile(shape, dtype, name=name, tag=name, offset=at * UNIT, align_bytes=64)

        def bank(shape, name, b):
            return psum.tile(shape, F32, name=name, tag="bank%d" % b)

        at_raw00 = 0
        at_tab2_2 = 134
        at_raw11 = 16
        at_rounded00 = 31
        at_v2_planes = 38
        at_tab2_sc = 39
        at_raw01 = 42
        at_rounded01 = 58
        at_w2_planes = 61
        at_tab_sc = 62
        at_tab1 = 70
        at_tab0 = 102
        at_rounded10 = (146, 156)
        at_rounded11 = (154, 158)

        offs_sb = sbuf.tile([P, S // GROUP], U16, name="offs_sb")
        pos_sb = sbuf.tile([P, M // GROUP], U16, name="pos_sb")
        offs2_sb = sbuf.tile([P, M // GROUP], U16, name="offs2_sb")

        tab_sc = placed([P, T], U8, "tab_sc", at_tab_sc)
        tab2_sc = placed([P, T2], U8, "tab2_sc", at_tab2_sc)
        v_planes = new_tile([P, PASSES * S], U8, "v_planes")
        top, top2 = P - SCALE_ROWS * PASSES, P // 2 - SCALE_ROWS * PASSES2
        half = new_tile([P, 1], F32, "half")
        nc.vector.memset(half[:], 0.5)
        nc.vector.memset(tab_sc[:].bitcast(I32)[:top], 0)
        nc.vector.memset(tab2_sc[:].bitcast(I32)[:top2], 0)
        nc.vector.memset(tab2_sc[:].bitcast(I32)[P // 2:], 0)
        nc.vector.memset(v_planes[:].bitcast(I32), 0)

        warm_up = new_tile([P, 1], F32, "warm_up")
        nc.scalar.activation(out=warm_up[:], in_=half[:], func=ACT.Ln)

        def load_w1(blk, a, at):
            raw = placed([P, PACK, PASS], F32, "w1_raw%d%d" % (blk, a), at)
            rows = w1[a * PASS:(a + 1) * PASS, blk * PASS:(blk + 1) * PASS]
            nc.sync.dma_start(out=raw[:], in_=rows.rearrange("(p j) c -> p j c", j=PACK))
            return raw

        def load_words(packed, name, at):
            words = placed([P, packed.shape[1]], I32, name, at)
            nc.sync.dma_start(out=words[:], in_=words_of(packed))
            return words

        def load_w2(blk, at):
            words = placed([P, PASSES2 * 2 * PASS], U8, "w2_sb%d" % blk, at)
            nc.sync.dma_start(
                out=words[:].bitcast(I32).rearrange("p (a c) -> p a c", a=PASSES2),
                in_=w2_words[:, :, 2 * blk * PASS:2 * (blk + 1) * PASS].bitcast(I32).rearrange("a p c -> p a c"),
            )
            return words

        def load_planes(planes, scales, passes, first_row):
            view = planes[:].bitcast(I32).rearrange("p (a c) -> p a c", a=passes)
            for r in range(ROWS):
                nc.sync.dma_start(
                    out=view[first_row + r:P:QUAD],
                    in_=scales[:, r:SCALE_ROWS:ROWS, :].bitcast(I32).rearrange("a q c -> q a c"),
                )

        def carry_planes(planes, gathered, lowest, passes):
            view = planes[:].bitcast(I32).rearrange("p (a c) -> p a c", a=passes)
            for low, upper in itertools.product(range(QUADS // 2), range(2)):
                q = low + upper * QUADS // 2
                start = lowest + q * ROWS * passes
                nc.sync.dma_start(
                    out=view[q * QUAD:q * QUAD + ROWS], in_=gathered[:].bitcast(I32)[start:start + ROWS * passes]
                )

        w1_raw = {}
        nc.sync.dma_start(out=tab_sc[:].bitcast(I32)[top:], in_=tab_scales.bitcast(I32).rearrange("a q c -> q a c"))
        nc.sync.dma_start(offs_sb[:], offs)
        tab_sb = [load_words(tab_words[0], "tab0", at_tab0)]
        nc.sync.dma_start(offs2_sb[:], offs2)
        nc.sync.dma_start(
            out=tab2_sc[:].bitcast(I32)[top2:top2 + SCALE_ROWS * PASSES2],
            in_=tab2_scales.bitcast(I32).rearrange("a q c -> q a c"),
        )
        nc.sync.dma_start(pos_sb[:], pos1)
        w1_raw[0, 0] = load_w1(0, 0, at_raw00)
        tab_sb.append(load_words(tab_words[1], "tab1", at_tab1))

        ident = new_tile([P, P], F32, "ident")
        make_identity(nc, ident[:])

        v_sc = new_tile([P, S], U8, "v_sc")
        nc.vector.tensor_copy(v_sc[:], tab_sc[:].indirect(offs_sb[:]))
        carry_planes(v_planes, v_sc, top, PASSES)
        v2_sc = new_tile([P, M], U8, "v2_sc")
        nc.vector.tensor_copy(v2_sc[:], tab2_sc[:].indirect(offs2_sb[:]))
        w1_raw[0, 1] = load_w1(0, 1, at_raw01)

        v_codes = {}

        def gather_v(a):
            for u in range(HALVES):
                v_codes[a, u] = new_tile([P, BANK], U32, "v%d%d" % (a, u))
                entries = offs_sb[:, u * BANK // GROUP:(u + 1) * BANK // GROUP]
                nc.vector.tensor_copy(v_codes[a, u][:], tab_sb[a][:].bitcast(U32).indirect(entries))

        gather_v(0)

        w1_codes, w1_planes = {}, {}

        def round_block(blk, a, copy, rounded):
            copy(
                rounded[:].rearrange("p (t m j) -> p m t j", t=PACK, j=PACK),
                w1_raw[blk, a][:].rearrange("p j (m t) -> p m t j", t=PACK),
            )

        def round_pair(blk, a, u, copy, rounded):
            pairs = w1_raw[blk, a][:].rearrange("p j (m u e) -> p u m e j", u=PAIRS, e=2)
            copy(rounded.rearrange("p (e m j) -> p m e j", e=2, j=PACK), pairs[:, u])

        def quantise_w1(blk, a, t0, rounded, sets):
            codes = new_tile([P, sets * P], U32, "w1_codes%d%d%d" % (blk, a, t0))
            planes = new_tile([P, sets * P], U8, "w1_planes%d%d%d" % (blk, a, t0))
            nc.vector.quantize_mx(out=codes[:].bitcast(FP8X4), scales=planes[:], in_=rounded)
            for e in range(sets):
                w1_codes[blk, a, t0 + e] = codes[:, e * P:(e + 1) * P]
                w1_planes[blk, a, t0 + e] = planes[:, e * P:(e + 1) * P]

        rounded = placed([P, PACK * PASS], BF16, "w1_bf00", at_rounded00)
        round_block(0, 0, nc.scalar.copy, rounded)
        w1_raw[1, 0] = load_w1(1, 0, at_raw00)
        quantise_w1(0, 0, 0, rounded[:], PACK)
        w1_raw[1, 1] = load_w1(1, 1, at_raw11)
        v2_planes = placed([P, UNIT + PASSES2 * M], U8, "v2_planes", at_v2_planes)[:, UNIT:]
        carry_planes(v2_planes, v2_sc, top2, PASSES2)
        gather_v(1)
        tab2_sb = [load_words(tab2_words[a], "tab2_%d" % a, at_tab1 + 16 * a) for a in range(2)]
        rounded = [new_tile([P, 2 * PASS], BF16, "w1_bf010"), placed([P, 2 * PASS], BF16, "w1_bf011", at_rounded01)]
        for u, copy in enumerate((nc.vector.tensor_copy, nc.scalar.copy)):
            round_pair(0, 1, u, copy, rounded[u][:])
        w2_sb = [load_w2(0, at_raw01)]
        for u in range(PAIRS):
            quantise_w1(0, 1, 2 * u, rounded[u][:], 2)
        w2_planes = placed([P, UNIT + PASSES2 * H], U8, "w2_planes", at_w2_planes)[:, UNIT:]
        load_planes(w2_planes, w2_scales, PASSES2, 0)

        def first_stage(blk, h, order):
            for t, u in order:
                acc = bank([P, BANK], "acc", HALVES * t + u)
                for a in range(PASSES):
                    nc.tensor.matmul_mx(
                        out=acc[:],
                        lhsT=w1_codes[blk, a, t].bitcast(FP8X4),
                        lhsT_scale=w1_planes[blk, a, t],
                        rhs=v_codes[a, u][:].bitcast(FP8X4),
                        rhs_scale=v_planes[:, a * S + u * BANK:a * S + (u + 1) * BANK],
                        start=(a == 0), stop=(a == PASSES - 1),
                    )
                nc.scalar.copy(h[t][:, u * BANK:(u + 1) * BANK], acc[:])

        def log_half_plus(logs, squares):
            nc.scalar.activation(out=logs, in_=squares, func=ACT.Ln, bias=half[:])

        log_a = [new_tile([P, PACK, M], F32, "log_a%d" % blk) for blk in range(BLOCKS)]
        picked = {}

        def pick(blk, t, window, at=None):
            name = "a%d%d" % (blk, t)
            picked[blk, t] = new_tile([P, M], F32, name) if at is None else placed([P, M], F32, name, at)
            nc.vector.tensor_copy(picked[blk, t][:], window[:].indirect(pos_sb[:]))

        def square(blk, t, engine):
            row = picked[blk, t]
            if engine is nc.scalar:
                nc.scalar.activation(out=log_a[blk][:, t, :], in_=row[:], func=ACT.Square)
            else:
                engine.tensor_tensor(log_a[blk][:, t, :], row[:], row[:], ALU.mult)

        def log_of_a(blk, t):
            log_half_plus(log_a[blk][:, t, :], log_a[blk][:, t, :])

        v2_codes = {2: new_tile([P, M], U32, "v2_2")}

        def gather_v2(a, first, count):
            entries = offs2_sb[:, first // GROUP:(first + count) // GROUP]
            nc.vector.tensor_copy(v2_codes[a][:, first:first + count], tab2_sb[a][:].bitcast(U32).indirect(entries))

        def project(blk, i, a, bt):
            c0 = a * H + blk * PASS
            nc.tensor.matmul_mx(
                out=bt[:],
                lhsT=v2_codes[a][:, i * P:(i + 1) * P].bitcast(FP8X4),
                lhsT_scale=v2_planes[:, a * M + i * P:a * M + (i + 1) * P],
                rhs=w2_sb[blk][:, 2 * a * PASS:2 * (a + 1) * PASS].bitcast(FP4X4),
                rhs_scale=w2_planes[:, c0:c0 + PASS],
                start=(a == 0), stop=(a == PASSES2 - 1),
            )

        def square_of_bt(squares, bt):
            nc.scalar.activation(
                out=squares.rearrange("m (t p) -> m t p", t=PACK),
                in_=bt[:].rearrange("m (p t) -> m t p", t=PACK),
                func=ACT.Square,
            )

        h0 = [placed([P, S], F32, "h0%d" % t, at_tab0 + 8 * t) for t in range(PACK)]
        first_stage(0, h0, itertools.product(range(PACK), range(HALVES)))
        rounded = [placed([P, 2 * PASS], BF16, "w1_bf10%d" % u, at_rounded10[u]) for u in range(PAIRS)]
        for u in range(PAIRS):
            round_pair(1, 0, u, nc.vector.tensor_copy, rounded[u][:])
        for u in range(PAIRS):
            quantise_w1(1, 0, 2 * u, rounded[u][:], 2)
        tab2_sb.append(load_words(tab2_words[2], "tab2_2", at_tab2_2))
        for t in range(PACK):
            pick(0, t, h0[t], at_raw00 + 4 * t)

        def round_on_gpsimd(rounded, raw):
            nc.gpsimd.tensor_scalar(rounded, raw, 1.0, 0.0, ALU.mult, ALU.add)

        rounded = [placed([P, 2 * PASS], BF16, "w1_bf11%d" % u, at_rounded11[u]) for u in range(PAIRS)]
        for u in range(PAIRS):
            round_pair(1, 1, u, round_on_gpsimd, rounded[u][:])
        w2_sb.append(load_w2(1, at_raw11))
        gain_sb = placed([P, BLOCKS, PACK], F32, "gain_sb", at_raw11 + 6)
        nc.sync.dma_start(out=gain_sb[:], in_=gain.rearrange("(b p t) -> p b t", b=BLOCKS, t=PACK))
        w3_sb = placed([P, BLOCKS * N], I32, "w3_sb", at_raw11 + 7)
        nc.sync.dma_start(
            out=w3_sb[:].rearrange("p (b c) -> p b c", b=BLOCKS),
            in_=w3_words.rearrange("b p c i -> p b (c i)").bitcast(I32),
        )
        for u in range(PAIRS):
            quantise_w1(1, 1, 2 * u, rounded[u][:], 2)
        for t in range(2):
            square(0, t, nc.scalar)
            log_of_a(0, t)
        square(0, 2, nc.scalar)
        h1 = [new_tile([P, S], F32, "h1%d" % t) for t in range(PACK)]
        first_stage(1, h1, itertools.product(range(PACK), range(HALVES)))
        log_of_a(0, 2)
        last_squares = placed([P, M], F32, "last_squares", at_rounded11[0] + 1)
        nc.gpsimd.tensor_tensor(last_squares[:], picked[0, 3][:], picked[0, 3][:], ALU.mult)
        log_half_plus(log_a[0][:, 3, :], last_squares[:])
        w3_planes = v_planes[:, :BLOCKS * N]
        load_planes(w3_planes, w3_scales, BLOCKS, ROWS)
        for a in range(2):
            v2_codes[a] = placed([P, M], U32, "v2_%d" % a, (at_rounded11[0] - 3, at_rounded11[1] + 1)[a])
            gather_v2(a, 0, M)
        pick(1, 0, h1[0], at_tab1 + 16)
        for first in range(0, M, M // 2):
            gather_v2(2, first, M // 2)
        for t in range(1, PACK):
            pick(1, t, h1[t], at_tab2_2 + 4 * t)
        for t in range(PACK):
            square(1, t, nc.gpsimd)

        z_codes, z_planes = {}, {}

        def round_z(blk, i, diff):
            z = new_tile([P, PASS], BF16, "z%d%d" % (blk, i))
            nc.vector.tensor_tensor(
                z[:].rearrange("p (m u e) -> p m u e", u=PAIRS, e=2),
                diff.rearrange("p u m e -> p m u e"),
                gain_sb[:, blk, :].rearrange("p (u e) -> p u e", u=PAIRS).unsqueeze(1).to_broadcast([P, P, PAIRS, 2]),
                ALU.mult,
            )
            return blk, i, z

        def quantise_z(blk, i, z):
            z_codes[blk, i] = new_tile([P, P], U32, "z_codes%d%d" % (blk, i))[:]
            z_planes[blk, i] = new_tile([P, P], U8, "z_planes%d%d" % (blk, i))[:]
            nc.vector.quantize_mx(out=z_codes[blk, i].bitcast(FP8X4), scales=z_planes[blk, i], in_=z[:])

        log_bt = [new_tile([P, CHUNKS, PASS], F32, "log_bt%d" % blk) for blk in range(BLOCKS)]
        chunk_pairs = [(i, i + 1) for i in range(0, CHUNKS, 2)]

        def difference(blk, i, b):
            log_b = bank([P, PACK, P], "log_b", b)
            for t in range(PACK):
                nc.tensor.transpose(log_b[:, t, :], log_bt[blk][:, i, t * P:(t + 1) * P], ident[:])
            diff = new_tile([P, PAIRS, P, 2], F32, "diff%d%d" % (blk, i), "diff%d%d" % (blk, min(i, CHUNKS - 1 - blk)))
            nc.vector.tensor_tensor(
                diff[:],
                log_b[:].rearrange("p (u e) m -> p u m e", u=PAIRS),
                log_a[blk][:, :, i * P:(i + 1) * P].rearrange("p (u e) m -> p u m e", u=PAIRS),
                ALU.subtract,
            )
            return diff[:]

        def finish_z(blk, pair, diffs):
            for z in [round_z(blk, i, diff) for i, diff in zip(pair, diffs)]:
                quantise_z(*z)

        def logs_of_bt(blk, pair, banks):
            for i in pair:
                square_of_bt(log_bt[blk][:, i, :], banks[i])
            for i in pair:
                log_half_plus(log_bt[blk][:, i, :], log_bt[blk][:, i, :])

        bt0 = [bank([P, BANK], "bt", i) for i in range(CHUNKS)]
        for a, i in itertools.product(range(PASSES2), range(CHUNKS)):
            project(0, i, a, bt0[i])
        bt1 = {}
        for g, pair in enumerate(chunk_pairs):
            logs_of_bt(0, pair, bt0)
            diffs = [difference(0, i, (6, 0)[g] + k) for k, i in enumerate(pair)]
            for k, i in enumerate(pair):
                bt1[i] = bank([P, BANK], "bt", (4, 2)[g] + k)
                for a in range(PASSES2):
                    project(1, i, a, bt1[i])
            finish_z(0, pair, diffs)
        logs_of_bt(1, chunk_pairs[0], bt1)
        for t in range(0, PACK, 2):
            log_half_plus(log_a[1][:, t:t + 2, :], log_a[1][:, t:t + 2, :])
        finish_z(1, chunk_pairs[0], [difference(1, i, 6 + i) for i in chunk_pairs[0]])
        logs_of_bt(1, chunk_pairs[1], bt1)
        for k, i in enumerate(chunk_pairs[1]):
            finish_z(1, (i,), [difference(1, i, k)])

        out_view = out.rearrange("(g p) m -> p g m", p=P)
        levels = new_tile([P, CHUNKS, N // P, P], F32, "levels", "half")

        def alarm(i, g0, groups, b):
            y = bank([P, groups, P], "y", b)
            for blk, g in itertools.product(range(BLOCKS), range(groups)):
                cols = slice(blk * N + (g0 + g) * P, blk * N + (g0 + g + 1) * P)
                nc.tensor.matmul_mx(
                    out=y[:, g, :],
                    lhsT=w3_sb[:, cols].bitcast(FP8X4),
                    lhsT_scale=w3_planes[ROWS:, cols],
                    rhs=z_codes[blk, i].bitcast(FP8X4),
                    rhs_scale=z_planes[blk, i],
                    start=(blk == 0 and g == 0), stop=(blk == BLOCKS - 1 and g == groups - 1),
                )
            nc.scalar.activation(out=levels[:, i, g0:g0 + groups], in_=y[:], func=ACT.Sigmoid)
            nc.sync.dma_start(out=out_view[:, g0:g0 + groups, i * P:(i + 1) * P], in_=levels[:, i, g0:g0 + groups])

        for i in range(CHUNKS - 1):
            alarm(i, 0, N // P, (4, 5, 2)[i])
        for piece in range(2):
            alarm(CHUNKS - 1, piece * N // P // 2, N // P // 2, (3, 6)[piece])
